import numpy as np
import ml_dtypes


def mxq(x, axis, fmt="e4m3"):
    dtype, down = {"e4m3": (ml_dtypes.float8_e4m3fn, 7), "e5m2": (ml_dtypes.float8_e5m2, 14)}[fmt]
    v = np.moveaxis(np.asarray(x, np.float32).astype(ml_dtypes.bfloat16).astype(np.float64), axis, -1)
    blocks = v.reshape(v.shape[:-1] + (-1, 32))
    amax = np.abs(blocks).max(-1, keepdims=True)
    byte = np.maximum(np.where(amax > 0, np.frexp(amax)[1] - 1 + 127, 0) - down, 1)
    scale = np.exp2(byte - 127.0)
    codes = (blocks / scale).astype(np.float32).astype(dtype).astype(np.float64)
    return np.moveaxis((codes * scale).reshape(v.shape), -1, axis)


WIDE = False


def mx_kscale(k):
    if not WIDE:
        return np.ones(k)
    levels = np.array([10, -10, 5, -5, 0])
    if k % 512:
        return np.exp2(np.random.permutation(np.resize(levels, k // 32))).repeat(32)
    a = np.empty((k // 512, 16))
    for p in range(k // 512):
        a[p, :8] = np.random.permutation(np.resize(levels, 8))
        for g in range(8):
            far = levels[np.abs(levels - a[p, g]) >= 10]
            a[p, g + 8] = far[np.random.randint(len(far))]
    return np.exp2(a.ravel()).repeat(32)


def f64(x):
    return np.asarray(x).astype(np.float64)


def striped(idx):
    return np.tile(idx.reshape(-1, 16).T, (8, 1)).astype(np.uint16)


def unstriped(offs):
    return offs[:16].T.reshape(-1).astype(np.int64)


E2M1 = np.array([0.0, 0.5, 1.0, 1.5, 2.0, 3.0, 4.0, 6.0, -0.0, -0.5, -1.0, -1.5, -2.0, -3.0, -4.0, -6.0])


def pack_weight(w, fmt):
    k, n = w.shape
    w = f64(np.asarray(w, np.float32).astype(ml_dtypes.bfloat16)).reshape(k // 32, 32, n)
    amax = np.abs(w).max(1)
    if fmt == "e4m3":
        byte = np.frexp(amax)[1] - 1 + 127 - 7
    else:
        mant, ex = np.frexp(amax / 6.0)
        byte = np.where(mant > 0.5, ex, ex - 1) + 127
    byte = np.clip(np.where(amax > 0, byte, 1), 1, 254)
    scaled = (w * np.exp2(127.0 - byte)[:, None, :]).reshape(k, n).astype(np.float32)
    by_word = np.ascontiguousarray(scaled.reshape(k // 512, 128, 4, n).transpose(0, 1, 3, 2))
    if fmt == "e4m3":
        words = by_word.astype(ml_dtypes.float8_e4m3fn).view(np.uint8)
    else:
        c = by_word.astype(ml_dtypes.float4_e2m1fn).view(np.uint8) & 0xF
        words = (c[..., 0::2] | (c[..., 1::2] << 4)).reshape(k // 512, 128, 2 * n)
    return np.ascontiguousarray(words), np.ascontiguousarray(byte.astype(np.uint8).reshape(k // 512, 16, n))


def unpack_weight(words, scales, fmt):
    g, _, n = scales.shape
    words = np.ascontiguousarray(words).reshape(g, 128, n, -1)
    if fmt == "e4m3":
        vals = words.view(ml_dtypes.float8_e4m3fn).astype(np.float64)
    else:
        nib = np.empty((g, 128, n, 4), np.uint8)
        nib[..., 0::2] = words & 0xF
        nib[..., 1::2] = words >> 4
        vals = E2M1[nib]
    vals = vals * np.repeat(np.exp2(scales.astype(np.float64) - 127.0), 8, axis=1)[..., None]
    return vals.transpose(0, 1, 3, 2).reshape(g * 512, n)


K, T, E, C, H, N = 512, 512, 8, 128, 512, 256


def by_expert(wq, xq):
    return np.concatenate([wq[e].T @ xq[:, e * C:(e + 1) * C] for e in range(E)], axis=1)


def setup_inputs():
    n = np.random.standard_normal
    s = mx_kscale(K)
    u = mx_kscale(H)
    first = np.random.permutation(np.repeat(np.arange(E), T // E))
    second = (first + 1 + np.random.permutation(np.repeat(np.arange(E - 1), -(-T // (E - 1)))[:T])) % E
    while np.bincount(second, minlength=E).max() != T // E:
        load = np.bincount(second, minlength=E); hi, lo = int(load.argmax()), int(load.argmin())
        t = np.flatnonzero((second == hi) & (first != lo))[0]; second[t] = lo
    slot_token = np.empty(E * C, np.int64); pos = np.empty((2, T), np.int64); fill = np.zeros(E, np.int64)
    place = np.stack([np.random.permutation(C) for _ in range(E)])
    for r, deal in enumerate((first, second)):
        for t in np.random.permutation(T):
            e = deal[t]; j = e * C + place[e, fill[e]]; fill[e] += 1; slot_token[j] = t; pos[r, t] = j
    g = np.random.uniform(0.2, 0.8, T)
    x = pack_weight(n((K, T)) * s[:, None], "e4m3")
    w = [pack_weight(m, "e2m1") for m in n((E, K, N)) / np.sqrt(K) / s[None, :, None]]
    wb = [pack_weight(m, "e4m3") for m in n((E, H, N)) / np.sqrt(H) / u[None, :, None]]
    return {
        "x_words": x[0],
        "x_scales": x[1],
        "w_words": np.stack([m[0] for m in w]),
        "w_scales": np.stack([m[1] for m in w]),
        "wa": (n((E, K, H)) / np.sqrt(K) / s[None, :, None] * u).astype(np.float32),
        "wb_words": np.stack([m[0] for m in wb]),
        "wb_scales": np.stack([m[1] for m in wb]),
        "gate": np.stack([np.tile(g, (128, 1)), np.tile(1.0 - g, (128, 1))]).astype(np.float32),
        "offs": striped(slot_token),
        "pos1": striped(pos[0]),
        "pos2": striped(pos[1]),
    }


def reference(x_words, x_scales, w_words, w_scales, wa, wb_words, wb_scales, gate, offs, pos1, pos2):
    w = np.stack([unpack_weight(w_words[e], w_scales[e], "e2m1") for e in range(E)])
    waq = mxq(f64(wa), 1, "e4m3")
    wb = np.stack([unpack_weight(wb_words[e], wb_scales[e], "e4m3") for e in range(E)])
    idx = unstriped(offs)
    xq = unpack_weight(x_words, x_scales, "e4m3")[:, idx]
    h = by_expert(waq, xq)
    y = by_expert(w, xq) + by_expert(wb, mxq(h, 0, "e4m3"))
    out = sum(f64(gate[r, :1]) * y[:, unstriped(p)] for r, p in enumerate((pos1, pos2)))
    return out

@@ -1,0 +1,272 @@
+from contextlib import ExitStack
+
+import concourse.mybir as mybir
+
+K, T, E, C, H, N = 512, 512, 8, 128, 512, 256
+S = E * C
+P = 128
+PACK = 4
+FLOPS = 2 * S * (K * H + K * N + H * N)
+
+F32 = mybir.dt.float32
+BF16 = mybir.dt.bfloat16
+I32 = mybir.dt.int32
+U32 = mybir.dt.uint32
+U16 = mybir.dt.uint16
+U8 = mybir.dt.uint8
+FP8X4 = mybir.dt.float8_e4m3fn_x4
+FP4X4 = mybir.dt.float4_e2m1fn_x4
+MULT = mybir.AluOpType.mult
+ADD = mybir.AluOpType.add
+
+GATHER = 256
+LOADS = ((0, 1, 2, 3), (4, 5), (6, 7))
+GROUPS = ((0, 1), (2, 3), (4, 5), (6, 7))
+SCALAR_CASTS = (0, 1, 3, 5)
+LAST = E - 1
+HALF = H // 2
+QUARTER = H // 4
+
+
+def tile_moe_elr_none_kernel(
+    tc, x_words, x_scales, w_words, w_scales, wa, wb_words, wb_scales, gate, offs, pos1, pos2, out
+):
+    nc = tc.nc
+    with ExitStack() as ctx:
+        keep = ctx.enter_context(tc.tile_pool(name="keep", bufs=1))
+        hbanks = ctx.enter_context(tc.psum_pool(name="hbanks", bufs=2))
+        ybanks = ctx.enter_context(tc.psum_pool(name="ybanks", bufs=3))
+
+        def held(shape, dtype, name, tag=None):
+            return keep.tile(shape, dtype, name=name, tag=tag or name, align_bytes=64)
+
+        def load(tile_view, dram_view):
+            nc.sync.dma_start(out=tile_view, in_=dram_view)
+
+        offs_t = held([P, S // 16], U16, "offs_t")
+        pos_t = [held([P, T // 16], U16, "pos_t%d" % r) for r in range(2)]
+        xw = held([P, T], U32, "xw")
+        xs = held([P, T], U8, "xs")
+        ws = held([P, E, N], U8, "ws")
+        wbs = held([P, E, N], U8, "wbs")
+        for plane in (xs, ws, wbs):
+            nc.vector.memset(plane[:].bitcast(I32), 0)
+
+        def load_scales(plane, rows):
+            for r in range(4):
+                load(plane[:].bitcast(I32)[r:P:32], rows[r].bitcast(I32))
+
+        wa_rows = wa.rearrange("e (p j) i -> e p j i", j=PACK)
+        raw = {}
+
+        def load_wa(e, c0, width):
+            raw[e, c0] = held([P, PACK, width], F32, "raw%d_%d" % (e, c0))
+            load(raw[e, c0][:], wa_rows[e][:, :, c0 : c0 + width])
+
+        w_view = w_words.rearrange("e s p c -> p (e s) c")
+        wb_view = wb_words.rearrange("e s p n d -> p (e s) (n d)")
+        w_t, wb_t = {}, {}
+
+        def load_second(g):
+            group = LOADS[g]
+            wt = held([P, len(group), 2 * N], U8, "w%d" % g)
+            wbt = held([P, len(group), 4 * N], U8, "wb%d" % g)
+            load(wbt[:].bitcast(I32), wb_view[:, group[0] : group[-1] + 1, :].bitcast(I32))
+            load(wt[:].bitcast(I32), w_view[:, group[0] : group[-1] + 1, :].bitcast(I32))
+            for n, e in enumerate(group):
+                w_t[e] = wt[:, n, :]
+                wb_t[e] = wbt[:, n, :]
+
+        gate_t = [held([P, T], F32, "gate%d" % r) for r in range(2)]
+
+        load(offs_t[:], offs)
+        load(xw[:].bitcast(I32), x_words[0].rearrange("p t d -> p (t d)").bitcast(I32))
+        load_scales(xs, x_scales[0].rearrange("(q r) t -> r q t", r=4))
+        load_wa(0, 0, H)
+        load_wa(1, 0, H)
+        load(pos_t[0][:], pos1)
+        load(pos_t[1][:], pos2)
+        load_wa(2, 0, H)
+        load_scales(ws, w_scales.rearrange("e s (q r) n -> r q (e s) n", r=4))
+        load_wa(3, 0, H)
+        load_scales(wbs, wb_scales.rearrange("e s (q r) n -> r q (e s) n", r=4))
+        load_second(0)
+        load_wa(4, 0, H)
+        load_wa(5, 0, H)
+        load_second(1)
+        load_wa(6, 0, H)
+        load_wa(LAST, 0, HALF)
+        load_wa(LAST, HALF, QUARTER)
+        load_wa(LAST, HALF + QUARTER, QUARTER)
+        load_second(2)
+        for r in range(2):
+            load(gate_t[r][:], gate[r])
+
+        xg_w, xg_s = {}, {}
+
+        def gather_tokens(chunk):
+            cols = offs_t[:, chunk * GATHER // 16 : (chunk + 1) * GATHER // 16]
+            words = held([P, GATHER], U32, "xgw%d" % chunk)
+            scales = held([P, GATHER], U8, "xgs%d" % chunk)
+            nc.vector.tensor_copy(words[:], xw[:].indirect(cols))
+            nc.vector.tensor_copy(scales[:], xs[:].indirect(cols))
+            for n in range(GATHER // C):
+                e = chunk * GATHER // C + n
+                xg_w[e] = words[:, n * C : (n + 1) * C]
+                xg_s[e] = scales[:, n * C : (n + 1) * C]
+
+        def cast(engine_copy, dst, src):
+            engine_copy(out=dst.rearrange("p t m j -> p m j t"), in_=src.rearrange("p j (m t) -> p m j t", t=PACK))
+
+        wa_codes = [held([P, H], U32, "wac%d" % e) for e in range(LAST)]
+        wa_scales = [held([P, H], U8, "was%d" % e) for e in range(LAST)]
+        grouped = {}
+
+        def cast_expert(e):
+            grouped[e] = held([P, PACK, P, PACK], BF16, "grp%d" % e)
+            cast(nc.scalar.copy if e in SCALAR_CASTS else nc.vector.tensor_copy, grouped[e][:], raw[e, 0][:])
+
+        def quantize_expert(e):
+            nc.vector.quantize_mx(
+                out=wa_codes[e][:].bitcast(FP8X4),
+                scales=wa_scales[e][:],
+                in_=grouped[e][:].rearrange("p t m j -> p (t m j)"),
+            )
+
+        last_codes = [held([P, P], U32, "lc%d" % t) for t in range(PACK)]
+        last_scales = [held([P, P], U8, "ls%d" % t) for t in range(PACK)]
+
+        def quantize_half(tile, half):
+            for t in range(PACK):
+                cols = slice(half * 64, half * 64 + 64)
+                nc.vector.quantize_mx(
+                    out=last_codes[t][:, cols].bitcast(FP8X4),
+                    scales=last_scales[t][:, cols],
+                    in_=tile[:, t].rearrange("p m j -> p (m j)"),
+                )
+
+        h_bank, h_bf, h_codes, h_scales = {}, {}, {}, {}
+
+        def first_product(e):
+            bank = hbanks.tile([P, PACK, C], F32, name="hbank")
+            for t in range(PACK):
+                cols = slice(t * P, (t + 1) * P)
+                nc.tensor.matmul_mx(
+                    out=bank[:, t, :],
+                    lhsT=(wa_codes[e][:, cols] if e < LAST else last_codes[t][:]).bitcast(FP8X4),
+                    lhsT_scale=wa_scales[e][:, cols] if e < LAST else last_scales[t][:],
+                    rhs=xg_w[e].bitcast(FP8X4),
+                    rhs_scale=xg_s[e],
+                    start=True,
+                    stop=True,
+                )
+            h_bank[e] = bank
+
+        def copy_h(e):
+            bank = h_bank[e]
+            reuse = "raw%d_0" % (e + 1) if e + 1 in SCALAR_CASTS or e + 1 == LAST else None
+            h_bf[e] = held([P, C, PACK], BF16, "hbf%d" % e, reuse)
+            nc.scalar.copy(out=h_bf[e][:], in_=bank[:].rearrange("p t s -> p s t"))
+
+        def quantize_h(e):
+            reuse = "raw%d_0" % (e + 1) if e + 1 not in SCALAR_CASTS and e + 1 < LAST else None
+            h_codes[e] = held([P, C], U32, "hc%d" % e, reuse)
+            h_scales[e] = held([P, C], U8, "hs%d" % e)
+            nc.vector.quantize_mx(
+                out=h_codes[e][:].bitcast(FP8X4),
+                scales=h_scales[e][:],
+                in_=h_bf[e][:].rearrange("p s t -> p (s t)"),
+            )
+
+        y = [held([P, S], F32, "y%d" % b) for b in range(2)]
+
+        y_bank = {}
+
+        def frozen_pass(e, b):
+            if e % 2 == 0:
+                y_bank[b] = ybanks.tile([P, 2, C], F32, name="ybank%d" % b)
+            nc.tensor.matmul_mx(
+                out=y_bank[b][:, e % 2, :],
+                lhsT=w_t[e][:, 2 * b * P : 2 * (b + 1) * P].bitcast(FP4X4),
+                lhsT_scale=ws[:, e, b * P : (b + 1) * P],
+                rhs=xg_w[e].bitcast(FP8X4),
+                rhs_scale=xg_s[e],
+                start=True,
+                stop=False,
+            )
+
+        def adapter_pass(e, b):
+            nc.tensor.matmul_mx(
+                out=y_bank[b][:, e % 2, :],
+                lhsT=wb_t[e][:, 4 * b * P : 4 * (b + 1) * P].bitcast(FP8X4),
+                lhsT_scale=wbs[:, e, b * P : (b + 1) * P],
+                rhs=h_codes[e][:].bitcast(FP8X4),
+                rhs_scale=h_scales[e][:],
+                start=False,
+                stop=True,
+            )
+
+        def second_products(e):
+            for b in range(2):
+                frozen_pass(e - 1, b)
+                adapter_pass(e - 1, b)
+                frozen_pass(e, b)
+            for b in range(2):
+                adapter_pass(e, b)
+
+        def copy_y(e):
+            for b in range(2):
+                nc.scalar.copy(
+                    out=y[b][:, (e - 1) * C : (e + 1) * C],
+                    in_=y_bank[b][:].rearrange("p n s -> p (n s)"),
+                )
+
+        for chunk in range(S // GATHER):
+            gather_tokens(chunk)
+        cast_expert(0)
+        for e in range(1, LAST):
+            quantize_expert(e - 1)
+            first_product(e - 1)
+            cast_expert(e)
+            copy_h(e - 1)
+            if e >= 2:
+                quantize_h(e - 2)
+            if e in (4, 5):
+                second_products(2 * e - 7)
+                copy_y(2 * e - 7)
+
+        halves = [held([P, PACK, 64, PACK], BF16, "half%d" % a) for a in range(2)]
+        quantize_expert(LAST - 1)
+        first_product(LAST - 1)
+        quantize_h(LAST - 2)
+        second_products(LAST - 2)
+        cast(nc.scalar.copy, halves[0][:], raw[LAST, 0][:])
+        cast(nc.vector.tensor_copy, halves[1][:, :, 0:32, :], raw[LAST, HALF][:])
+        cast(nc.vector.tensor_copy, halves[1][:, :, 32:64, :], raw[LAST, HALF + QUARTER][:])
+        copy_h(LAST - 1)
+        copy_y(LAST - 2)
+        quantize_half(halves[0], 0)
+        quantize_half(halves[1], 1)
+        quantize_h(LAST - 1)
+        first_product(LAST)
+        copy_h(LAST)
+        quantize_h(LAST)
+        second_products(LAST)
+        copy_y(LAST)
+
+        picked = [[held([P, T], F32, "pick%d_%d" % (b, r)) for r in range(2)] for b in range(2)]
+        res = [held([P, T], F32, "res%d" % b) for b in range(2)]
+
+        def pick(b, r):
+            nc.vector.tensor_tensor(picked[b][r][:], y[b][:].indirect(pos_t[r][:]), gate_t[r][:], MULT)
+
+        def finish(b):
+            nc.vector.tensor_tensor(res[b][:], picked[b][0][:], picked[b][1][:], ADD)
+            nc.sync.dma_start(out=out[b * P : (b + 1) * P, :], in_=res[b][:])
+
+        pick(0, 0)
+        pick(0, 1)
+        pick(1, 0)
+        finish(0)
+        pick(1, 1)
+        finish(1)

@@ -1,6 +1,7 @@
 from contextlib import ExitStack
 
 import concourse.mybir as mybir
+from concourse.masks import make_identity
 
 K, T, E, C, H, N = 512, 512, 8, 128, 512, 256
 S = E * C
@@ -20,8 +21,6 @@ MULT = mybir.AluOpType.mult
 ADD = mybir.AluOpType.add
 
 GATHER = 256
-LOADS = ((0, 1, 2, 3), (4, 5), (6, 7))
-GROUPS = ((0, 1), (2, 3), (4, 5), (6, 7))
 SCALAR_CASTS = (0, 1, 3, 5)
 LAST = E - 1
 HALF = H // 2
@@ -67,21 +66,28 @@ def tile_moe_elr_none_kernel(
         wb_view = wb_words.rearrange("e s p n d -> p (e s) (n d)")
         w_t, wb_t = {}, {}
 
-        def load_second(g):
-            group = LOADS[g]
-            wt = held([P, len(group), 2 * N], U8, "w%d" % g)
-            wbt = held([P, len(group), 4 * N], U8, "wb%d" % g)
-            load(wbt[:].bitcast(I32), wb_view[:, group[0] : group[-1] + 1, :].bitcast(I32))
-            load(wt[:].bitcast(I32), w_view[:, group[0] : group[-1] + 1, :].bitcast(I32))
-            for n, e in enumerate(group):
-                w_t[e] = wt[:, n, :]
-                wb_t[e] = wbt[:, n, :]
+        def load_second(experts, b):
+            first, count = experts[0], len(experts)
+            wbt = held([P, count, 4 * P], U8, "wb%d_%d" % (first, b))
+            rows = slice(first, first + count)
+            load(wbt[:].bitcast(I32), wb_view[:, rows, 4 * b * P : 4 * (b + 1) * P].bitcast(I32))
+            for n, e in enumerate(experts):
+                wb_t[e, b] = wbt[:, n, :]
+            if b == 0:
+                wt = held([P, count, 2 * N], U8, "w%d" % first)
+                load(wt[:].bitcast(I32), w_view[:, rows, :].bitcast(I32))
+                for n, e in enumerate(experts):
+                    w_t[e] = wt[:, n, :]
 
-        gate_t = [held([P, T], F32, "gate%d" % r) for r in range(2)]
+        gate_rows = held([P, T], F32, "gate_rows")
+        nc.gpsimd.memset(gate_rows[:], 0.0)
+        ident = held([P, P], F32, "ident")
+        make_identity(nc, ident[:])
 
         load(offs_t[:], offs)
         load(xw[:].bitcast(I32), x_words[0].rearrange("p t d -> p (t d)").bitcast(I32))
         load_scales(xs, x_scales[0].rearrange("(q r) t -> r q t", r=4))
+        load(gate_rows[0:2, :], gate[:, 0, :])
         load_wa(0, 0, H)
         load_wa(1, 0, H)
         load(pos_t[0][:], pos1)
@@ -90,17 +96,27 @@ def tile_moe_elr_none_kernel(
         load_scales(ws, w_scales.rearrange("e s (q r) n -> r q (e s) n", r=4))
         load_wa(3, 0, H)
         load_scales(wbs, wb_scales.rearrange("e s (q r) n -> r q (e s) n", r=4))
-        load_second(0)
         load_wa(4, 0, H)
         load_wa(5, 0, H)
-        load_second(1)
         load_wa(6, 0, H)
-        load_wa(LAST, 0, HALF)
-        load_wa(LAST, HALF, QUARTER)
-        load_wa(LAST, HALF + QUARTER, QUARTER)
-        load_second(2)
+        load_second((0, 1), 0)
+        load_wa(LAST, 0, H)
+        load_second((2, 3, 4), 0)
+        load_second((5, 6, 7), 0)
+        load_second((0, 1, 2, 3), 1)
+        load_second((4, 5, 6, 7), 1)
+
+        turned = ybanks.tile([P, T // P, P], F32, name="ybank0")
+        for c in range(T // P):
+            nc.tensor.transpose(turned[:, c, :], gate_rows[:, c * P : (c + 1) * P], ident[:])
+        gate_cols = held([P, T // P, 2], F32, "gate_cols")
+        nc.scalar.copy(out=gate_cols[:], in_=turned[:, :, 0:2])
+        gate_t = [held([P, T], F32, "gate%d" % r) for r in range(2)]
         for r in range(2):
-            load(gate_t[r][:], gate[r])
+            spread = ybanks.tile([P, T // P, P], F32, name="ybank1")
+            for c in range(T // P):
+                nc.tensor.transpose(spread[:, c, :], gate_cols[:, c, r : r + 1].to_broadcast([P, P]), ident[:])
+            nc.scalar.copy(out=gate_t[r][:], in_=spread[:].rearrange("p c t -> p (c t)"))
 
         xg_w, xg_s = {}, {}
 
@@ -180,13 +196,9 @@ def tile_moe_elr_none_kernel(
 
         y = [held([P, S], F32, "y%d" % b) for b in range(2)]
 
-        y_bank = {}
-
-        def frozen_pass(e, b):
-            if e % 2 == 0:
-                y_bank[b] = ybanks.tile([P, 2, C], F32, name="ybank%d" % b)
+        def frozen_pass(acc, e, b):
             nc.tensor.matmul_mx(
-                out=y_bank[b][:, e % 2, :],
+                out=acc,
                 lhsT=w_t[e][:, 2 * b * P : 2 * (b + 1) * P].bitcast(FP4X4),
                 lhsT_scale=ws[:, e, b * P : (b + 1) * P],
                 rhs=xg_w[e].bitcast(FP8X4),
@@ -195,10 +207,10 @@ def tile_moe_elr_none_kernel(
                 stop=False,
             )
 
-        def adapter_pass(e, b):
+        def adapter_pass(acc, e, b):
             nc.tensor.matmul_mx(
-                out=y_bank[b][:, e % 2, :],
-                lhsT=wb_t[e][:, 4 * b * P : 4 * (b + 1) * P].bitcast(FP8X4),
+                out=acc,
+                lhsT=wb_t[e, b].bitcast(FP8X4),
                 lhsT_scale=wbs[:, e, b * P : (b + 1) * P],
                 rhs=h_codes[e][:].bitcast(FP8X4),
                 rhs_scale=h_scales[e][:],
@@ -206,20 +218,15 @@ def tile_moe_elr_none_kernel(
                 stop=True,
             )
 
-        def second_products(e):
-            for b in range(2):
-                frozen_pass(e - 1, b)
-                adapter_pass(e - 1, b)
-                frozen_pass(e, b)
-            for b in range(2):
-                adapter_pass(e, b)
-
-        def copy_y(e):
-            for b in range(2):
-                nc.scalar.copy(
-                    out=y[b][:, (e - 1) * C : (e + 1) * C],
-                    in_=y_bank[b][:].rearrange("p n s -> p (n s)"),
-                )
+        def second_products(experts, b, engine_copy):
+            bank = ybanks.tile([P, len(experts), C], F32, name="ybank%d" % b)
+            for n, e in enumerate(experts):
+                frozen_pass(bank[:, n, :], e, b)
+                adapter_pass(bank[:, n, :], e, b)
+            engine_copy(
+                out=y[b][:, experts[0] * C : (experts[-1] + 1) * C],
+                in_=bank[:].rearrange("p n s -> p (n s)"),
+            )
 
         for chunk in range(S // GATHER):
             gather_tokens(chunk)
@@ -231,28 +238,27 @@ def tile_moe_elr_none_kernel(
             copy_h(e - 1)
             if e >= 2:
                 quantize_h(e - 2)
-            if e in (4, 5):
-                second_products(2 * e - 7)
-                copy_y(2 * e - 7)
-
-        halves = [held([P, PACK, 64, PACK], BF16, "half%d" % a) for a in range(2)]
         quantize_expert(LAST - 1)
         first_product(LAST - 1)
         quantize_h(LAST - 2)
-        second_products(LAST - 2)
-        cast(nc.scalar.copy, halves[0][:], raw[LAST, 0][:])
-        cast(nc.vector.tensor_copy, halves[1][:, :, 0:32, :], raw[LAST, HALF][:])
-        cast(nc.vector.tensor_copy, halves[1][:, :, 32:64, :], raw[LAST, HALF + QUARTER][:])
+        second_products((0, 1), 0, nc.scalar.copy)
+
+        halves = [held([P, PACK, 64, PACK], BF16, "half%d" % a) for a in range(2)]
+        cast(nc.vector.tensor_copy, halves[0][:], raw[LAST, 0][:, :, 0:HALF])
+        cast(nc.vector.tensor_copy, halves[1][:, :, 0:16, :], raw[LAST, 0][:, :, HALF : HALF + 64])
+        cast(nc.scalar.copy, halves[1][:, :, 16:64, :], raw[LAST, 0][:, :, HALF + 64 : H])
         copy_h(LAST - 1)
-        copy_y(LAST - 2)
         quantize_half(halves[0], 0)
         quantize_half(halves[1], 1)
         quantize_h(LAST - 1)
         first_product(LAST)
         copy_h(LAST)
+        second_products((2, 3, 4), 0, nc.vector.tensor_copy)
         quantize_h(LAST)
-        second_products(LAST)
-        copy_y(LAST)
+        second_products((5, 6), 0, nc.scalar.copy)
+        second_products((LAST,), 0, nc.scalar.copy)
+        second_products((0, 1, 2, 3), 1, nc.scalar.copy)
+        second_products((4, 5, 6, 7), 1, nc.scalar.copy)
 
         picked = [[held([P, T], F32, "pick%d_%d" % (b, r)) for r in range(2)] for b in range(2)]
         res = [held([P, T], F32, "res%d" % b) for b in range(2)]

@@ -21,10 +21,12 @@ MULT = mybir.AluOpType.mult
 ADD = mybir.AluOpType.add
 
 GATHER = 256
-SCALAR_CASTS = (0, 1, 3, 5)
 LAST = E - 1
-HALF = H // 2
-QUARTER = H // 4
+SCALAR_ROUNDS = (0, 1, 3, 5)
+HALF = P // 2
+VECTOR_EXTRA = 16
+BLOCK0_LOADS = ((0, 1), (2, 3, 4), (5, 6, 7))
+BLOCK1_LOADS = ((0, 1, 2, 3), (4, 5), (6, 7))
 
 
 def tile_moe_elr_none_kernel(
@@ -48,63 +50,64 @@ def tile_moe_elr_none_kernel(
         xs = held([P, T], U8, "xs")
         ws = held([P, E, N], U8, "ws")
         wbs = held([P, E, N], U8, "wbs")
-        for plane in (xs, ws, wbs):
-            nc.vector.memset(plane[:].bitcast(I32), 0)
+        for scale_tile in (xs, ws, wbs):
+            nc.vector.memset(scale_tile[:].bitcast(I32), 0)
 
-        def load_scales(plane, rows):
+        def load_scales(scale_tile, rows):
             for r in range(4):
-                load(plane[:].bitcast(I32)[r:P:32], rows[r].bitcast(I32))
+                load(scale_tile[:].bitcast(I32)[r:P:32], rows[r].bitcast(I32))
 
         wa_rows = wa.rearrange("e (p j) i -> e p j i", j=PACK)
         raw = {}
 
-        def load_wa(e, c0, width):
-            raw[e, c0] = held([P, PACK, width], F32, "raw%d_%d" % (e, c0))
-            load(raw[e, c0][:], wa_rows[e][:, :, c0 : c0 + width])
+        def load_wa(e):
+            raw[e] = held([P, PACK, H], F32, "raw%d" % e)
+            load(raw[e][:], wa_rows[e])
 
         w_view = w_words.rearrange("e s p c -> p (e s) c")
         wb_view = wb_words.rearrange("e s p n d -> p (e s) (n d)")
         w_t, wb_t = {}, {}
 
-        def load_second(experts, b):
-            first, count = experts[0], len(experts)
-            wbt = held([P, count, 4 * P], U8, "wb%d_%d" % (first, b))
-            rows = slice(first, first + count)
-            load(wbt[:].bitcast(I32), wb_view[:, rows, 4 * b * P : 4 * (b + 1) * P].bitcast(I32))
+        def load_wb(experts, b):
+            group = held([P, len(experts), 4 * P], U8, "wb%d_%d" % (experts[0], b))
+            rows = slice(experts[0], experts[-1] + 1)
+            load(group[:].bitcast(I32), wb_view[:, rows, 4 * b * P : 4 * (b + 1) * P].bitcast(I32))
             for n, e in enumerate(experts):
-                wb_t[e, b] = wbt[:, n, :]
-            if b == 0:
-                wt = held([P, count, 2 * N], U8, "w%d" % first)
-                load(wt[:].bitcast(I32), w_view[:, rows, :].bitcast(I32))
-                for n, e in enumerate(experts):
-                    w_t[e] = wt[:, n, :]
+                wb_t[e, b] = group[:, n, :]
+
+        def load_w(experts):
+            group = held([P, len(experts), 2 * N], U8, "w%d" % experts[0])
+            load(group[:].bitcast(I32), w_view[:, experts[0] : experts[-1] + 1, :].bitcast(I32))
+            for n, e in enumerate(experts):
+                w_t[e] = group[:, n, :]
 
         gate_rows = held([P, T], F32, "gate_rows")
-        nc.gpsimd.memset(gate_rows[:], 0.0)
+        nc.vector.memset(gate_rows[:], 0.0)
         ident = held([P, P], F32, "ident")
         make_identity(nc, ident[:])
 
         load(offs_t[:], offs)
         load(xw[:].bitcast(I32), x_words[0].rearrange("p t d -> p (t d)").bitcast(I32))
+        load_wa(0)
         load_scales(xs, x_scales[0].rearrange("(q r) t -> r q t", r=4))
+        load_wa(1)
         load(gate_rows[0:2, :], gate[:, 0, :])
-        load_wa(0, 0, H)
-        load_wa(1, 0, H)
         load(pos_t[0][:], pos1)
         load(pos_t[1][:], pos2)
-        load_wa(2, 0, H)
+        load_wa(2)
         load_scales(ws, w_scales.rearrange("e s (q r) n -> r q (e s) n", r=4))
-        load_wa(3, 0, H)
+        load_wa(3)
         load_scales(wbs, wb_scales.rearrange("e s (q r) n -> r q (e s) n", r=4))
-        load_wa(4, 0, H)
-        load_wa(5, 0, H)
-        load_wa(6, 0, H)
-        load_second((0, 1), 0)
-        load_wa(LAST, 0, H)
-        load_second((2, 3, 4), 0)
-        load_second((5, 6, 7), 0)
-        load_second((0, 1, 2, 3), 1)
-        load_second((4, 5, 6, 7), 1)
+        for e in range(4, LAST):
+            load_wa(e)
+        load_wb(BLOCK0_LOADS[0], 0)
+        load_w(BLOCK0_LOADS[0])
+        load_wa(LAST)
+        for experts in BLOCK0_LOADS[1:]:
+            load_wb(experts, 0)
+            load_w(experts)
+        for experts in BLOCK1_LOADS:
+            load_wb(experts, 1)
 
         turned = ybanks.tile([P, T // P, P], F32, name="ybank0")
         for c in range(T // P):
@@ -121,26 +124,29 @@ def tile_moe_elr_none_kernel(
         xg_w, xg_s = {}, {}
 
         def gather_tokens(chunk):
-            cols = offs_t[:, chunk * GATHER // 16 : (chunk + 1) * GATHER // 16]
+            entries = offs_t[:, chunk * GATHER // 16 : (chunk + 1) * GATHER // 16]
             words = held([P, GATHER], U32, "xgw%d" % chunk)
             scales = held([P, GATHER], U8, "xgs%d" % chunk)
-            nc.vector.tensor_copy(words[:], xw[:].indirect(cols))
-            nc.vector.tensor_copy(scales[:], xs[:].indirect(cols))
+            nc.vector.tensor_copy(words[:], xw[:].indirect(entries))
+            nc.vector.tensor_copy(scales[:], xs[:].indirect(entries))
             for n in range(GATHER // C):
                 e = chunk * GATHER // C + n
                 xg_w[e] = words[:, n * C : (n + 1) * C]
                 xg_s[e] = scales[:, n * C : (n + 1) * C]
 
-        def cast(engine_copy, dst, src):
-            engine_copy(out=dst.rearrange("p t m j -> p m j t"), in_=src.rearrange("p j (m t) -> p m j t", t=PACK))
+        def round_wa(engine_copy, dst, src):
+            engine_copy(
+                out=dst.rearrange("p t (m a) j -> p m j a t", a=2),
+                in_=src.rearrange("p j (m a t) -> p m j a t", a=2, t=PACK),
+            )
 
         wa_codes = [held([P, H], U32, "wac%d" % e) for e in range(LAST)]
         wa_scales = [held([P, H], U8, "was%d" % e) for e in range(LAST)]
         grouped = {}
 
-        def cast_expert(e):
+        def round_expert(e):
             grouped[e] = held([P, PACK, P, PACK], BF16, "grp%d" % e)
-            cast(nc.scalar.copy if e in SCALAR_CASTS else nc.vector.tensor_copy, grouped[e][:], raw[e, 0][:])
+            round_wa(nc.scalar.copy if e in SCALAR_ROUNDS else nc.vector.tensor_copy, grouped[e][:], raw[e][:])
 
         def quantize_expert(e):
             nc.vector.quantize_mx(
@@ -152,40 +158,46 @@ def tile_moe_elr_none_kernel(
         last_codes = [held([P, P], U32, "lc%d" % t) for t in range(PACK)]
         last_scales = [held([P, P], U8, "ls%d" % t) for t in range(PACK)]
 
-        def quantize_half(tile, half):
+        def quantize_last(rounded, half):
+            places = slice(half * HALF, (half + 1) * HALF)
             for t in range(PACK):
-                cols = slice(half * 64, half * 64 + 64)
                 nc.vector.quantize_mx(
-                    out=last_codes[t][:, cols].bitcast(FP8X4),
-                    scales=last_scales[t][:, cols],
-                    in_=tile[:, t].rearrange("p m j -> p (m j)"),
+                    out=last_codes[t][:, places].bitcast(FP8X4),
+                    scales=last_scales[t][:, places],
+                    in_=rounded[:, t].rearrange("p m j -> p (m j)"),
                 )
+
+        def stationary_wa(e, t):
+            if e == LAST:
+                return last_codes[t][:], last_scales[t][:]
+            return wa_codes[e][:, t * P : (t + 1) * P], wa_scales[e][:, t * P : (t + 1) * P]
 
         h_bank, h_bf, h_codes, h_scales = {}, {}, {}, {}
 
         def first_product(e):
-            bank = hbanks.tile([P, PACK, C], F32, name="hbank")
+            h_bank[e] = hbanks.tile([P, PACK, C], F32, name="hbank")
             for t in range(PACK):
-                cols = slice(t * P, (t + 1) * P)
+                codes, scales = stationary_wa(e, t)
                 nc.tensor.matmul_mx(
-                    out=bank[:, t, :],
-                    lhsT=(wa_codes[e][:, cols] if e < LAST else last_codes[t][:]).bitcast(FP8X4),
-                    lhsT_scale=wa_scales[e][:, cols] if e < LAST else last_scales[t][:],
+                    out=h_bank[e][:, t, :],
+                    lhsT=codes.bitcast(FP8X4),
+                    lhsT_scale=scales,
                     rhs=xg_w[e].bitcast(FP8X4),
                     rhs_scale=xg_s[e],
                     start=True,
                     stop=True,
                 )
-            h_bank[e] = bank
 
-        def copy_h(e):
-            bank = h_bank[e]
-            reuse = "raw%d_0" % (e + 1) if e + 1 in SCALAR_CASTS or e + 1 == LAST else None
+        def next_rounded_by_scalar(e):
+            return e + 1 in SCALAR_ROUNDS or e + 1 == LAST
+
+        def round_h(e):
+            reuse = "raw%d" % (e + 1) if next_rounded_by_scalar(e) else None
             h_bf[e] = held([P, C, PACK], BF16, "hbf%d" % e, reuse)
-            nc.scalar.copy(out=h_bf[e][:], in_=bank[:].rearrange("p t s -> p s t"))
+            nc.scalar.copy(out=h_bf[e][:], in_=h_bank[e][:].rearrange("p t s -> p s t"))
 
         def quantize_h(e):
-            reuse = "raw%d_0" % (e + 1) if e + 1 not in SCALAR_CASTS and e + 1 < LAST else None
+            reuse = "raw%d" % (e + 1) if e < LAST and not next_rounded_by_scalar(e) else None
             h_codes[e] = held([P, C], U32, "hc%d" % e, reuse)
             h_scales[e] = held([P, C], U8, "hs%d" % e)
             nc.vector.quantize_mx(
@@ -196,33 +208,28 @@ def tile_moe_elr_none_kernel(
 
         y = [held([P, S], F32, "y%d" % b) for b in range(2)]
 
-        def frozen_pass(acc, e, b):
-            nc.tensor.matmul_mx(
-                out=acc,
-                lhsT=w_t[e][:, 2 * b * P : 2 * (b + 1) * P].bitcast(FP4X4),
-                lhsT_scale=ws[:, e, b * P : (b + 1) * P],
-                rhs=xg_w[e].bitcast(FP8X4),
-                rhs_scale=xg_s[e],
-                start=True,
-                stop=False,
-            )
-
-        def adapter_pass(acc, e, b):
-            nc.tensor.matmul_mx(
-                out=acc,
-                lhsT=wb_t[e, b].bitcast(FP8X4),
-                lhsT_scale=wbs[:, e, b * P : (b + 1) * P],
-                rhs=h_codes[e][:].bitcast(FP8X4),
-                rhs_scale=h_scales[e][:],
-                start=False,
-                stop=True,
-            )
-
         def second_products(experts, b, engine_copy):
             bank = ybanks.tile([P, len(experts), C], F32, name="ybank%d" % b)
+            outputs = slice(b * P, (b + 1) * P)
             for n, e in enumerate(experts):
-                frozen_pass(bank[:, n, :], e, b)
-                adapter_pass(bank[:, n, :], e, b)
+                nc.tensor.matmul_mx(
+                    out=bank[:, n, :],
+                    lhsT=w_t[e][:, 2 * b * P : 2 * (b + 1) * P].bitcast(FP4X4),
+                    lhsT_scale=ws[:, e, outputs],
+                    rhs=xg_w[e].bitcast(FP8X4),
+                    rhs_scale=xg_s[e],
+                    start=True,
+                    stop=False,
+                )
+                nc.tensor.matmul_mx(
+                    out=bank[:, n, :],
+                    lhsT=wb_t[e, b].bitcast(FP8X4),
+                    lhsT_scale=wbs[:, e, outputs],
+                    rhs=h_codes[e][:].bitcast(FP8X4),
+                    rhs_scale=h_scales[e][:],
+                    start=False,
+                    stop=True,
+                )
             engine_copy(
                 out=y[b][:, experts[0] * C : (experts[-1] + 1) * C],
                 in_=bank[:].rearrange("p n s -> p (n s)"),
@@ -230,35 +237,36 @@ def tile_moe_elr_none_kernel(
 
         for chunk in range(S // GATHER):
             gather_tokens(chunk)
-        cast_expert(0)
+        round_expert(0)
         for e in range(1, LAST):
             quantize_expert(e - 1)
             first_product(e - 1)
-            cast_expert(e)
-            copy_h(e - 1)
+            round_expert(e)
+            round_h(e - 1)
             if e >= 2:
                 quantize_h(e - 2)
         quantize_expert(LAST - 1)
         first_product(LAST - 1)
         quantize_h(LAST - 2)
-        second_products((0, 1), 0, nc.scalar.copy)
+        second_products(BLOCK0_LOADS[0], 0, nc.scalar.copy)
 
-        halves = [held([P, PACK, 64, PACK], BF16, "half%d" % a) for a in range(2)]
-        cast(nc.vector.tensor_copy, halves[0][:], raw[LAST, 0][:, :, 0:HALF])
-        cast(nc.vector.tensor_copy, halves[1][:, :, 0:16, :], raw[LAST, 0][:, :, HALF : HALF + 64])
-        cast(nc.scalar.copy, halves[1][:, :, 16:64, :], raw[LAST, 0][:, :, HALF + 64 : H])
-        copy_h(LAST - 1)
-        quantize_half(halves[0], 0)
-        quantize_half(halves[1], 1)
+        halves = [held([P, PACK, HALF, PACK], BF16, "half%d" % half) for half in range(2)]
+        middle, cut = PACK * HALF, PACK * (HALF + VECTOR_EXTRA)
+        round_wa(nc.vector.tensor_copy, halves[0][:], raw[LAST][:, :, 0:middle])
+        round_wa(nc.vector.tensor_copy, halves[1][:, :, 0:VECTOR_EXTRA, :], raw[LAST][:, :, middle:cut])
+        round_wa(nc.scalar.copy, halves[1][:, :, VECTOR_EXTRA:HALF, :], raw[LAST][:, :, cut:H])
+        round_h(LAST - 1)
+        quantize_last(halves[0], 0)
+        quantize_last(halves[1], 1)
         quantize_h(LAST - 1)
         first_product(LAST)
-        copy_h(LAST)
-        second_products((2, 3, 4), 0, nc.vector.tensor_copy)
+        round_h(LAST)
+        second_products(BLOCK0_LOADS[1], 0, nc.vector.tensor_copy)
         quantize_h(LAST)
-        second_products((5, 6), 0, nc.scalar.copy)
+        second_products(BLOCK0_LOADS[2][:-1], 0, nc.scalar.copy)
         second_products((LAST,), 0, nc.scalar.copy)
-        second_products((0, 1, 2, 3), 1, nc.scalar.copy)
-        second_products((4, 5, 6, 7), 1, nc.scalar.copy)
+        for experts in BLOCK1_LOADS:
+            second_products(experts, 1, nc.scalar.copy)
 
         picked = [[held([P, T], F32, "pick%d_%d" % (b, r)) for r in range(2)] for b in range(2)]
         res = [held([P, T], F32, "res%d" % b) for b in range(2)]

@@ -22,11 +22,12 @@ ADD = mybir.AluOpType.add
 
 GATHER = 256
 LAST = E - 1
-SCALAR_ROUNDS = (0, 1, 3, 5)
+VECTOR_PLACES = (0, 72, 72, 72, 72, 72, 80)
 HALF = P // 2
-VECTOR_EXTRA = 16
+WARM_UPS = 4
+VECTOR_PLACES_OF_HALF = 40
 BLOCK0_LOADS = ((0, 1), (2, 3, 4), (5, 6, 7))
-BLOCK1_LOADS = ((0, 1, 2, 3), (4, 5), (6, 7))
+BLOCK1_LOADS = ((4, 5, 6, 7), (0, 1, 2, 3))
 
 
 def tile_moe_elr_none_kernel(
@@ -36,10 +37,16 @@ def tile_moe_elr_none_kernel(
     with ExitStack() as ctx:
         keep = ctx.enter_context(tc.tile_pool(name="keep", bufs=1))
         hbanks = ctx.enter_context(tc.psum_pool(name="hbanks", bufs=2))
-        ybanks = ctx.enter_context(tc.psum_pool(name="ybanks", bufs=3))
+        ybanks = ctx.enter_context(tc.psum_pool(name="ybanks", bufs=1))
 
         def held(shape, dtype, name, tag=None):
             return keep.tile(shape, dtype, name=name, tag=tag or name, align_bytes=64)
+
+        tail = ctx.enter_context(tc.tile_pool(name="tail", bufs=1))
+        last_bytes = 4 * PACK * H // 2
+
+        def placed(shape, dtype, name, offset):
+            return tail.tile(shape, dtype, name=name, tag=name, align_bytes=64, offset=offset)
 
         def load(tile_view, dram_view):
             nc.sync.dma_start(out=tile_view, in_=dram_view)
@@ -81,58 +88,53 @@ def tile_moe_elr_none_kernel(
             for n, e in enumerate(experts):
                 w_t[e] = group[:, n, :]
 
-        gate_rows = held([P, T], F32, "gate_rows")
-        nc.vector.memset(gate_rows[:], 0.0)
         ident = held([P, P], F32, "ident")
         make_identity(nc, ident[:])
+        gate_cols = held([P, 2, T // P], F32, "gate_cols")
 
-        load(offs_t[:], offs)
         load(xw[:].bitcast(I32), x_words[0].rearrange("p t d -> p (t d)").bitcast(I32))
+        load(offs_t[:], offs)
+        load(gate_cols[:], gate[:, 0, :].rearrange("r (p a) -> p r a", p=P))
         load_wa(0)
         load_scales(xs, x_scales[0].rearrange("(q r) t -> r q t", r=4))
-        load_wa(1)
-        load(gate_rows[0:2, :], gate[:, 0, :])
-        load(pos_t[0][:], pos1)
-        load(pos_t[1][:], pos2)
-        load_wa(2)
-        load_scales(ws, w_scales.rearrange("e s (q r) n -> r q (e s) n", r=4))
-        load_wa(3)
-        load_scales(wbs, wb_scales.rearrange("e s (q r) n -> r q (e s) n", r=4))
-        for e in range(4, LAST):
+        for e in (1, 2, 3):
             load_wa(e)
-        load_wb(BLOCK0_LOADS[0], 0)
+        load_scales(ws, w_scales.rearrange("e s (q r) n -> r q (e s) n", r=4))
+        for e in (4, 5):
+            load_wa(e)
+        load_scales(wbs, wb_scales.rearrange("e s (q r) n -> r q (e s) n", r=4))
+        load_wa(6)
+        last_raw = [held([P, PACK, H // 2], F32, "lastraw0"), placed([P, PACK, H // 2], F32, "lastraw1", 0)]
         load_w(BLOCK0_LOADS[0])
-        load_wa(LAST)
-        for experts in BLOCK0_LOADS[1:]:
-            load_wb(experts, 0)
-            load_w(experts)
+        load(last_raw[0][:], wa_rows[LAST][:, :, 0 : H // 2])
+        load_wb(BLOCK0_LOADS[0], 0)
+        load(last_raw[1][:], wa_rows[LAST][:, :, H // 2 : H])
+        load_w(BLOCK0_LOADS[1] + BLOCK0_LOADS[2])
+        for r in range(2):
+            load_wb(BLOCK0_LOADS[1 + r], 0)
+            load(pos_t[r][:], (pos1, pos2)[r])
         for experts in BLOCK1_LOADS:
             load_wb(experts, 1)
 
-        turned = ybanks.tile([P, T // P, P], F32, name="ybank0")
-        for c in range(T // P):
-            nc.tensor.transpose(turned[:, c, :], gate_rows[:, c * P : (c + 1) * P], ident[:])
-        gate_cols = held([P, T // P, 2], F32, "gate_cols")
-        nc.scalar.copy(out=gate_cols[:], in_=turned[:, :, 0:2])
         gate_t = [held([P, T], F32, "gate%d" % r) for r in range(2)]
         for r in range(2):
-            spread = ybanks.tile([P, T // P, P], F32, name="ybank1")
-            for c in range(T // P):
-                nc.tensor.transpose(spread[:, c, :], gate_cols[:, c, r : r + 1].to_broadcast([P, P]), ident[:])
-            nc.scalar.copy(out=gate_t[r][:], in_=spread[:].rearrange("p c t -> p (c t)"))
+            spread = ybanks.tile([P, T // P, P], F32, name="ybank%d" % r)
+            for a in range(T // P):
+                nc.tensor.transpose(spread[:, a, :], gate_cols[:, r, a : a + 1].to_broadcast([P, P]), ident[:])
+            nc.scalar.copy(
+                out=gate_t[r][:].rearrange("q (p a) -> q p a", p=P), in_=spread[:].rearrange("q a p -> q p a")
+            )
 
-        xg_w, xg_s = {}, {}
+        xg_w, xg_s, pieces = {}, {}, {}
 
-        def gather_tokens(chunk):
-            entries = offs_t[:, chunk * GATHER // 16 : (chunk + 1) * GATHER // 16]
-            words = held([P, GATHER], U32, "xgw%d" % chunk)
-            scales = held([P, GATHER], U8, "xgs%d" % chunk)
-            nc.vector.tensor_copy(words[:], xw[:].indirect(entries))
-            nc.vector.tensor_copy(scales[:], xs[:].indirect(entries))
-            for n in range(GATHER // C):
-                e = chunk * GATHER // C + n
-                xg_w[e] = words[:, n * C : (n + 1) * C]
-                xg_s[e] = scales[:, n * C : (n + 1) * C]
+        def gather_tokens(table, dtype, name, gathered):
+            for chunk in range(S // GATHER):
+                entries = offs_t[:, chunk * GATHER // 16 : (chunk + 1) * GATHER // 16]
+                piece = held([P, GATHER], dtype, "%s%d" % (name, chunk))
+                pieces[name] = piece
+                nc.vector.tensor_copy(piece[:], table[:].indirect(entries))
+                for n in range(GATHER // C):
+                    gathered[chunk * GATHER // C + n] = piece[:, n * C : (n + 1) * C]
 
         def round_wa(engine_copy, dst, src):
             engine_copy(
@@ -146,7 +148,10 @@ def tile_moe_elr_none_kernel(
 
         def round_expert(e):
             grouped[e] = held([P, PACK, P, PACK], BF16, "grp%d" % e)
-            round_wa(nc.scalar.copy if e in SCALAR_ROUNDS else nc.vector.tensor_copy, grouped[e][:], raw[e][:])
+            cut = VECTOR_PLACES[e]
+            if cut:
+                round_wa(nc.vector.tensor_copy, grouped[e][:, :, 0:cut, :], raw[e][:, :, 0 : PACK * cut])
+            round_wa(nc.scalar.copy, grouped[e][:, :, cut:P, :], raw[e][:, :, PACK * cut : H])
 
         def quantize_expert(e):
             nc.vector.quantize_mx(
@@ -157,14 +162,21 @@ def tile_moe_elr_none_kernel(
 
         last_codes = [held([P, P], U32, "lc%d" % t) for t in range(PACK)]
         last_scales = [held([P, P], U8, "ls%d" % t) for t in range(PACK)]
+        last_rounded = [held([P, PACK, HALF, PACK], BF16, "half%d" % half) for half in range(2)]
 
-        def quantize_last(rounded, half):
+        def round_last(half):
+            cut = VECTOR_PLACES_OF_HALF
+            rounded, source = last_rounded[half], last_raw[half]
+            round_wa(nc.vector.tensor_copy, rounded[:, :, 0:cut, :], source[:, :, 0 : PACK * cut])
+            round_wa(nc.scalar.copy, rounded[:, :, cut:HALF, :], source[:, :, PACK * cut : PACK * HALF])
+
+        def quantize_last(half):
             places = slice(half * HALF, (half + 1) * HALF)
             for t in range(PACK):
                 nc.vector.quantize_mx(
                     out=last_codes[t][:, places].bitcast(FP8X4),
                     scales=last_scales[t][:, places],
-                    in_=rounded[:, t].rearrange("p m j -> p (m j)"),
+                    in_=last_rounded[half][:, t].rearrange("p m j -> p (m j)"),
                 )
 
         def stationary_wa(e, t):
@@ -188,17 +200,19 @@ def tile_moe_elr_none_kernel(
                     stop=True,
                 )
 
-        def next_rounded_by_scalar(e):
-            return e + 1 in SCALAR_ROUNDS or e + 1 == LAST
-
         def round_h(e):
-            reuse = "raw%d" % (e + 1) if next_rounded_by_scalar(e) else None
-            h_bf[e] = held([P, C, PACK], BF16, "hbf%d" % e, reuse)
+            if e == LAST - 1:
+                h_bf[e] = placed([P, C, PACK], BF16, "hbf%d" % e, 0)
+            else:
+                reuse = None if e == LAST else "lastraw0" if e == LAST - 2 else "raw%d" % (e + 1)
+                h_bf[e] = held([P, C, PACK], BF16, "hbf%d" % e, reuse)
             nc.scalar.copy(out=h_bf[e][:], in_=h_bank[e][:].rearrange("p t s -> p s t"))
 
         def quantize_h(e):
-            reuse = "raw%d" % (e + 1) if e < LAST and not next_rounded_by_scalar(e) else None
-            h_codes[e] = held([P, C], U32, "hc%d" % e, reuse)
+            if e == LAST - 2:
+                h_codes[e] = placed([P, C], U32, "hc%d" % e, 2 * C * PACK)
+            else:
+                h_codes[e] = held([P, C], U32, "hc%d" % e, "half1" if e == LAST - 1 else None)
             h_scales[e] = held([P, C], U8, "hs%d" % e)
             nc.vector.quantize_mx(
                 out=h_codes[e][:].bitcast(FP8X4),
@@ -206,12 +220,13 @@ def tile_moe_elr_none_kernel(
                 in_=h_bf[e][:].rearrange("p s t -> p (s t)"),
             )
 
-        y = [held([P, S], F32, "y%d" % b) for b in range(2)]
+        y = [placed([P, S], F32, "y0", last_bytes - 64), held([P, S], F32, "y1")]
 
-        def second_products(experts, b, engine_copy):
-            bank = ybanks.tile([P, len(experts), C], F32, name="ybank%d" % b)
+        def second_products(experts, b, engine_copy, bank_name):
+            bank = ybanks.tile([P, len(experts), C], F32, name=bank_name)
             outputs = slice(b * P, (b + 1) * P)
-            for n, e in enumerate(experts):
+            for e in sorted(experts, key=lambda expert: expert != LAST):
+                n = e - experts[0]
                 nc.tensor.matmul_mx(
                     out=bank[:, n, :],
                     lhsT=w_t[e][:, 2 * b * P : 2 * (b + 1) * P].bitcast(FP4X4),
@@ -235,52 +250,67 @@ def tile_moe_elr_none_kernel(
                 in_=bank[:].rearrange("p n s -> p (n s)"),
             )
 
-        for chunk in range(S // GATHER):
-            gather_tokens(chunk)
+        gather_tokens(xw, U32, "xgw", xg_w)
+        gather_tokens(xs, U8, "xgs", xg_s)
         round_expert(0)
-        for e in range(1, LAST):
-            quantize_expert(e - 1)
-            first_product(e - 1)
+        quantize_expert(0)
+        first_product(0)
+        for e in range(1, LAST - 1):
             round_expert(e)
             round_h(e - 1)
-            if e >= 2:
-                quantize_h(e - 2)
+            quantize_expert(e)
+            quantize_h(e - 1)
+            first_product(e)
+        round_expert(LAST - 1)
         quantize_expert(LAST - 1)
         first_product(LAST - 1)
-        quantize_h(LAST - 2)
-        second_products(BLOCK0_LOADS[0], 0, nc.scalar.copy)
-
-        halves = [held([P, PACK, HALF, PACK], BF16, "half%d" % half) for half in range(2)]
-        middle, cut = PACK * HALF, PACK * (HALF + VECTOR_EXTRA)
-        round_wa(nc.vector.tensor_copy, halves[0][:], raw[LAST][:, :, 0:middle])
-        round_wa(nc.vector.tensor_copy, halves[1][:, :, 0:VECTOR_EXTRA, :], raw[LAST][:, :, middle:cut])
-        round_wa(nc.scalar.copy, halves[1][:, :, VECTOR_EXTRA:HALF, :], raw[LAST][:, :, cut:H])
-        round_h(LAST - 1)
-        quantize_last(halves[0], 0)
-        quantize_last(halves[1], 1)
-        quantize_h(LAST - 1)
+        warm = ybanks.tile([P, 2, GATHER], F32, name="warm")
+        for n in range(WARM_UPS):
+            nc.tensor.matmul_mx(
+                out=warm[:, n % 2, :],
+                lhsT=wa_codes[LAST - 1][:, 0:P].bitcast(FP8X4),
+                lhsT_scale=wa_scales[LAST - 1][:, 0:P],
+                rhs=pieces["xgw"][:].bitcast(FP8X4),
+                rhs_scale=pieces["xgs"][:],
+                start=True,
+                stop=True,
+            )
+        round_last(0)
+        round_h(LAST - 2)
+        quantize_last(0)
+        round_last(1)
+        quantize_last(1)
         first_product(LAST)
+        round_h(LAST - 1)
+        quantize_h(LAST - 2)
+        quantize_h(LAST - 1)
         round_h(LAST)
-        second_products(BLOCK0_LOADS[1], 0, nc.vector.tensor_copy)
         quantize_h(LAST)
-        second_products(BLOCK0_LOADS[2][:-1], 0, nc.scalar.copy)
-        second_products((LAST,), 0, nc.scalar.copy)
-        for experts in BLOCK1_LOADS:
-            second_products(experts, 1, nc.scalar.copy)
+        second_products(BLOCK0_LOADS[0], 0, nc.scalar.copy, "ybank0")
+        second_products(BLOCK0_LOADS[1], 0, nc.vector.tensor_copy, "ybank1")
+        second_products(BLOCK0_LOADS[2][:-1], 0, nc.scalar.copy, "ybank2")
+        second_products((LAST,), 0, nc.scalar.copy, "ybank3")
+        second_products(BLOCK1_LOADS[0], 1, nc.scalar.copy, "ybank4")
+        second_products(BLOCK1_LOADS[1], 1, nc.scalar.copy, "ybank3")
 
         picked = [[held([P, T], F32, "pick%d_%d" % (b, r)) for r in range(2)] for b in range(2)]
         res = [held([P, T], F32, "res%d" % b) for b in range(2)]
 
-        def pick(b, r):
-            nc.vector.tensor_tensor(picked[b][r][:], y[b][:].indirect(pos_t[r][:]), gate_t[r][:], MULT)
+        def pick(b, r, first, count):
+            tokens = slice(first, first + count)
+            entries = pos_t[r][:, first // 16 : (first + count) // 16]
+            nc.vector.tensor_tensor(picked[b][r][:, tokens], y[b][:].indirect(entries), gate_t[r][:, tokens], MULT)
 
-        def finish(b):
-            nc.vector.tensor_tensor(res[b][:], picked[b][0][:], picked[b][1][:], ADD)
-            nc.sync.dma_start(out=out[b * P : (b + 1) * P, :], in_=res[b][:])
+        def finish(b, first, count):
+            tokens = slice(first, first + count)
+            nc.vector.tensor_tensor(res[b][:, tokens], picked[b][0][:, tokens], picked[b][1][:, tokens], ADD)
+            nc.sync.dma_start(out=out[b * P : (b + 1) * P, tokens], in_=res[b][:, tokens])
 
-        pick(0, 0)
-        pick(0, 1)
-        pick(1, 0)
-        finish(0)
-        pick(1, 1)
-        finish(1)
+        pick(0, 0, 0, T)
+        pick(0, 1, 0, T)
+        pick(1, 0, 0, T)
+        finish(0, 0, T)
+        for first in (0, T // 2):
+            pick(1, 1, first, T // 2)
+        for first in (0, T // 2):
+            finish(1, first, T // 2)

@@ -23,10 +23,9 @@ ADD = mybir.AluOpType.add
 GATHER = 256
 LAST = E - 1
 VECTOR_PLACES = (0, 72, 72, 72, 72, 72, 80)
-HALF = P // 2
 WARM_UPS = 4
-VECTOR_PLACES_OF_HALF = 40
-BLOCK0_LOADS = ((0, 1), (2, 3, 4), (5, 6, 7))
+VECTOR_PLACES_OF_LAST = 84
+BLOCK0_LOADS = ((0, 1, 2), (3, 4, 5), (6, 7))
 BLOCK1_LOADS = ((4, 5, 6, 7), (0, 1, 2, 3))
 
 
@@ -82,11 +81,9 @@ def tile_moe_elr_none_kernel(
             for n, e in enumerate(experts):
                 wb_t[e, b] = group[:, n, :]
 
-        def load_w(experts):
-            group = held([P, len(experts), 2 * N], U8, "w%d" % experts[0])
-            load(group[:].bitcast(I32), w_view[:, experts[0] : experts[-1] + 1, :].bitcast(I32))
-            for n, e in enumerate(experts):
-                w_t[e] = group[:, n, :]
+        def load_w(b):
+            w_t[b] = held([P, E, 2 * P], U8, "w%d" % b)
+            load(w_t[b][:].bitcast(I32), w_view[:, :, 2 * b * P : 2 * (b + 1) * P].bitcast(I32))
 
         ident = held([P, P], F32, "ident")
         make_identity(nc, ident[:])
@@ -99,20 +96,20 @@ def tile_moe_elr_none_kernel(
         load_scales(xs, x_scales[0].rearrange("(q r) t -> r q t", r=4))
         for e in (1, 2, 3):
             load_wa(e)
-        load_scales(ws, w_scales.rearrange("e s (q r) n -> r q (e s) n", r=4))
+        load(pos_t[0][:], pos1)
+        load(pos_t[1][:], pos2)
         for e in (4, 5):
             load_wa(e)
-        load_scales(wbs, wb_scales.rearrange("e s (q r) n -> r q (e s) n", r=4))
+        load_scales(ws, w_scales.rearrange("e s (q r) n -> r q (e s) n", r=4))
         load_wa(6)
-        last_raw = [held([P, PACK, H // 2], F32, "lastraw0"), placed([P, PACK, H // 2], F32, "lastraw1", 0)]
-        load_w(BLOCK0_LOADS[0])
-        load(last_raw[0][:], wa_rows[LAST][:, :, 0 : H // 2])
-        load_wb(BLOCK0_LOADS[0], 0)
-        load(last_raw[1][:], wa_rows[LAST][:, :, H // 2 : H])
-        load_w(BLOCK0_LOADS[1] + BLOCK0_LOADS[2])
-        for r in range(2):
-            load_wb(BLOCK0_LOADS[1 + r], 0)
-            load(pos_t[r][:], (pos1, pos2)[r])
+        last_raw = [held([P, 2, H], F32, "lastraw0"), placed([P, 2, H], F32, "lastraw1", 0)]
+        for half in range(2):
+            load(last_raw[half][:], wa_rows[LAST][:, 2 * half : 2 * half + 2, :])
+        load_scales(wbs, wb_scales.rearrange("e s (q r) n -> r q (e s) n", r=4))
+        load_w(0)
+        for experts in BLOCK0_LOADS:
+            load_wb(experts, 0)
+        load_w(1)
         for experts in BLOCK1_LOADS:
             load_wb(experts, 1)
 
@@ -142,8 +139,8 @@ def tile_moe_elr_none_kernel(
                 in_=src.rearrange("p j (m a t) -> p m j a t", a=2, t=PACK),
             )
 
-        wa_codes = [held([P, H], U32, "wac%d" % e) for e in range(LAST)]
-        wa_scales = [held([P, H], U8, "was%d" % e) for e in range(LAST)]
+        wa_codes = [held([P, H], U32, "wac%d" % e) for e in range(E)]
+        wa_scales = [held([P, H], U8, "was%d" % e) for e in range(E)]
         grouped = {}
 
         def round_expert(e):
@@ -160,28 +157,15 @@ def tile_moe_elr_none_kernel(
                 in_=grouped[e][:].rearrange("p t m j -> p (t m j)"),
             )
 
-        last_codes = [held([P, P], U32, "lc%d" % t) for t in range(PACK)]
-        last_scales = [held([P, P], U8, "ls%d" % t) for t in range(PACK)]
-        last_rounded = [held([P, PACK, HALF, PACK], BF16, "half%d" % half) for half in range(2)]
+        grouped[LAST] = held([P, PACK, P, PACK], BF16, "grp%d" % LAST)
 
         def round_last(half):
-            cut = VECTOR_PLACES_OF_HALF
-            rounded, source = last_rounded[half], last_raw[half]
+            cut = VECTOR_PLACES_OF_LAST
+            rounded, source = grouped[LAST][:, :, :, 2 * half : 2 * half + 2], last_raw[half]
             round_wa(nc.vector.tensor_copy, rounded[:, :, 0:cut, :], source[:, :, 0 : PACK * cut])
-            round_wa(nc.scalar.copy, rounded[:, :, cut:HALF, :], source[:, :, PACK * cut : PACK * HALF])
-
-        def quantize_last(half):
-            places = slice(half * HALF, (half + 1) * HALF)
-            for t in range(PACK):
-                nc.vector.quantize_mx(
-                    out=last_codes[t][:, places].bitcast(FP8X4),
-                    scales=last_scales[t][:, places],
-                    in_=last_rounded[half][:, t].rearrange("p m j -> p (m j)"),
-                )
+            round_wa(nc.scalar.copy, rounded[:, :, cut:P, :], source[:, :, PACK * cut : H])
 
         def stationary_wa(e, t):
-            if e == LAST:
-                return last_codes[t][:], last_scales[t][:]
             return wa_codes[e][:, t * P : (t + 1) * P], wa_scales[e][:, t * P : (t + 1) * P]
 
         h_bank, h_bf, h_codes, h_scales = {}, {}, {}, {}
@@ -204,7 +188,7 @@ def tile_moe_elr_none_kernel(
             if e == LAST - 1:
                 h_bf[e] = placed([P, C, PACK], BF16, "hbf%d" % e, 0)
             else:
-                reuse = None if e == LAST else "lastraw0" if e == LAST - 2 else "raw%d" % (e + 1)
+                reuse = None if e == LAST else "raw%d" % (e + 1)
                 h_bf[e] = held([P, C, PACK], BF16, "hbf%d" % e, reuse)
             nc.scalar.copy(out=h_bf[e][:], in_=h_bank[e][:].rearrange("p t s -> p s t"))
 
@@ -212,7 +196,7 @@ def tile_moe_elr_none_kernel(
             if e == LAST - 2:
                 h_codes[e] = placed([P, C], U32, "hc%d" % e, 2 * C * PACK)
             else:
-                h_codes[e] = held([P, C], U32, "hc%d" % e, "half1" if e == LAST - 1 else None)
+                h_codes[e] = held([P, C], U32, "hc%d" % e, "grp%d" % LAST if e == LAST - 1 else None)
             h_scales[e] = held([P, C], U8, "hs%d" % e)
             nc.vector.quantize_mx(
                 out=h_codes[e][:].bitcast(FP8X4),
@@ -229,7 +213,7 @@ def tile_moe_elr_none_kernel(
                 n = e - experts[0]
                 nc.tensor.matmul_mx(
                     out=bank[:, n, :],
-                    lhsT=w_t[e][:, 2 * b * P : 2 * (b + 1) * P].bitcast(FP4X4),
+                    lhsT=w_t[b][:, e, :].bitcast(FP4X4),
                     lhsT_scale=ws[:, e, outputs],
                     rhs=xg_w[e].bitcast(FP8X4),
                     rhs_scale=xg_s[e],
@@ -262,6 +246,7 @@ def tile_moe_elr_none_kernel(
             quantize_h(e - 1)
             first_product(e)
         round_expert(LAST - 1)
+        round_h(LAST - 2)
         quantize_expert(LAST - 1)
         first_product(LAST - 1)
         warm = ybanks.tile([P, 2, GATHER], F32, name="warm")
@@ -276,18 +261,16 @@ def tile_moe_elr_none_kernel(
                 stop=True,
             )
         round_last(0)
-        round_h(LAST - 2)
-        quantize_last(0)
         round_last(1)
-        quantize_last(1)
+        quantize_expert(LAST)
         first_product(LAST)
         round_h(LAST - 1)
         quantize_h(LAST - 2)
         quantize_h(LAST - 1)
         round_h(LAST)
         quantize_h(LAST)
-        second_products(BLOCK0_LOADS[0], 0, nc.scalar.copy, "ybank0")
-        second_products(BLOCK0_LOADS[1], 0, nc.vector.tensor_copy, "ybank1")
+        second_products(BLOCK0_LOADS[0], 0, nc.vector.tensor_copy, "ybank0")
+        second_products(BLOCK0_LOADS[1], 0, nc.scalar.copy, "ybank1")
         second_products(BLOCK0_LOADS[2][:-1], 0, nc.scalar.copy, "ybank2")
         second_products((LAST,), 0, nc.scalar.copy, "ybank3")
         second_products(BLOCK1_LOADS[0], 1, nc.scalar.copy, "ybank4")

@@ -24,9 +24,10 @@ GATHER = 256
 LAST = E - 1
 VECTOR_PLACES = (0, 72, 72, 72, 72, 72, 80)
 WARM_UPS = 4
+WB_PLANE = 4
 VECTOR_PLACES_OF_LAST = 84
 BLOCK0_LOADS = ((0, 1, 2), (3, 4, 5), (6, 7))
-BLOCK1_LOADS = ((4, 5, 6, 7), (0, 1, 2, 3))
+BLOCK1_LOADS = ((4, 5, 6, 7), (0, 1, 2), (3,))
 
 
 def tile_moe_elr_none_kernel(
@@ -59,9 +60,9 @@ def tile_moe_elr_none_kernel(
         for scale_tile in (xs, ws, wbs):
             nc.vector.memset(scale_tile[:].bitcast(I32), 0)
 
-        def load_scales(scale_tile, rows):
+        def load_scales(queue, scale_tile, first, rows):
             for r in range(4):
-                load(scale_tile[:].bitcast(I32)[r:P:32], rows[r].bitcast(I32))
+                queue.dma_start(out=scale_tile[:].bitcast(I32)[first + r : P : 32], in_=rows[r].bitcast(I32))
 
         wa_rows = wa.rearrange("e (p j) i -> e p j i", j=PACK)
         raw = {}
@@ -87,25 +88,25 @@ def tile_moe_elr_none_kernel(
 
         ident = held([P, P], F32, "ident")
         make_identity(nc, ident[:])
+        load_scales(nc.gpsimd, ws, 0, w_scales.rearrange("e s (q r) n -> r q (e s) n", r=4))
+        load_scales(nc.gpsimd, wbs, WB_PLANE, wb_scales.rearrange("e s (q r) n -> r q (e s) n", r=4))
         gate_cols = held([P, 2, T // P], F32, "gate_cols")
 
         load(xw[:].bitcast(I32), x_words[0].rearrange("p t d -> p (t d)").bitcast(I32))
         load(offs_t[:], offs)
         load(gate_cols[:], gate[:, 0, :].rearrange("r (p a) -> p r a", p=P))
         load_wa(0)
-        load_scales(xs, x_scales[0].rearrange("(q r) t -> r q t", r=4))
+        load_scales(nc.sync, xs, 0, x_scales[0].rearrange("(q r) t -> r q t", r=4))
         for e in (1, 2, 3):
             load_wa(e)
         load(pos_t[0][:], pos1)
         load(pos_t[1][:], pos2)
         for e in (4, 5):
             load_wa(e)
-        load_scales(ws, w_scales.rearrange("e s (q r) n -> r q (e s) n", r=4))
         load_wa(6)
         last_raw = [held([P, 2, H], F32, "lastraw0"), placed([P, 2, H], F32, "lastraw1", 0)]
         for half in range(2):
             load(last_raw[half][:], wa_rows[LAST][:, 2 * half : 2 * half + 2, :])
-        load_scales(wbs, wb_scales.rearrange("e s (q r) n -> r q (e s) n", r=4))
         load_w(0)
         for experts in BLOCK0_LOADS:
             load_wb(experts, 0)
@@ -223,7 +224,7 @@ def tile_moe_elr_none_kernel(
                 nc.tensor.matmul_mx(
                     out=bank[:, n, :],
                     lhsT=wb_t[e, b].bitcast(FP8X4),
-                    lhsT_scale=wbs[:, e, outputs],
+                    lhsT_scale=wbs[WB_PLANE:P, e, outputs],
                     rhs=h_codes[e][:].bitcast(FP8X4),
                     rhs_scale=h_scales[e][:],
                     start=False,
@@ -275,6 +276,7 @@ def tile_moe_elr_none_kernel(
         second_products((LAST,), 0, nc.scalar.copy, "ybank3")
         second_products(BLOCK1_LOADS[0], 1, nc.scalar.copy, "ybank4")
         second_products(BLOCK1_LOADS[1], 1, nc.scalar.copy, "ybank3")
+        second_products(BLOCK1_LOADS[2], 1, nc.scalar.copy, "ybank0")
 
         picked = [[held([P, T], F32, "pick%d_%d" % (b, r)) for r in range(2)] for b in range(2)]
         res = [held([P, T], F32, "res%d" % b) for b in range(2)]
@@ -289,10 +291,37 @@ def tile_moe_elr_none_kernel(
             nc.vector.tensor_tensor(res[b][:, tokens], picked[b][0][:, tokens], picked[b][1][:, tokens], ADD)
             nc.sync.dma_start(out=out[b * P : (b + 1) * P, tokens], in_=res[b][:, tokens])
 
+        def add_by_transposes():
+            summed = ybanks.tile([P, T // P, P], F32, name="ybank0")
+            for c in range(T // P):
+                for r in range(2):
+                    nc.tensor.matmul(
+                        summed[:, c, :],
+                        picked[0][r][:, c * P : (c + 1) * P],
+                        ident[:],
+                        start=r == 0,
+                        stop=r == 1,
+                        is_transpose=True,
+                    )
+            return summed
+
+        def turn_back(summed, half):
+            first = half * T // 2
+            turned = held([P, 2, P], F32, "turned%d" % half)
+            nc.scalar.copy(out=turned[:], in_=summed[:, 2 * half : 2 * half + 2, :])
+            back = ybanks.tile([P, 2, P], F32, name="ybank%d" % (1 + half))
+            for c in range(2):
+                nc.tensor.transpose(back[:, c, :], turned[:, c, :], ident[:])
+            tokens = slice(first, first + T // 2)
+            nc.scalar.copy(out=res[0][:, tokens], in_=back[:].rearrange("p c t -> p (c t)"))
+            nc.sync.dma_start(out=out[0:P, tokens], in_=res[0][:, tokens])
+
         pick(0, 0, 0, T)
         pick(0, 1, 0, T)
         pick(1, 0, 0, T)
-        finish(0, 0, T)
+        summed = add_by_transposes()
+        for half in range(2):
+            turn_back(summed, half)
         for first in (0, T // 2):
             pick(1, 1, first, T // 2)
         for first in (0, T // 2):

@@ -23,10 +23,9 @@ ADD = mybir.AluOpType.add
 GATHER = 256
 LAST = E - 1
 VECTOR_PLACES = (0, 72, 72, 72, 72, 72, 80)
-WARM_UPS = 4
 WB_PLANE = 4
 VECTOR_PLACES_OF_LAST = 84
-BLOCK0_LOADS = ((0, 1, 2), (3, 4, 5), (6, 7))
+BLOCK0_LOADS = ((0, 1, 2), (3, 4), (5, 6), (7,))
 BLOCK1_LOADS = ((4, 5, 6, 7), (0, 1, 2), (3,))
 
 
@@ -60,9 +59,9 @@ def tile_moe_elr_none_kernel(
         for scale_tile in (xs, ws, wbs):
             nc.vector.memset(scale_tile[:].bitcast(I32), 0)
 
-        def load_scales(queue, scale_tile, first, rows):
+        def load_scales(scale_tile, first, rows):
             for r in range(4):
-                queue.dma_start(out=scale_tile[:].bitcast(I32)[first + r : P : 32], in_=rows[r].bitcast(I32))
+                load(scale_tile[:].bitcast(I32)[first + r : P : 32], rows[r].bitcast(I32))
 
         wa_rows = wa.rearrange("e (p j) i -> e p j i", j=PACK)
         raw = {}
@@ -88,28 +87,28 @@ def tile_moe_elr_none_kernel(
 
         ident = held([P, P], F32, "ident")
         make_identity(nc, ident[:])
-        load_scales(nc.gpsimd, ws, 0, w_scales.rearrange("e s (q r) n -> r q (e s) n", r=4))
-        load_scales(nc.gpsimd, wbs, WB_PLANE, wb_scales.rearrange("e s (q r) n -> r q (e s) n", r=4))
         gate_cols = held([P, 2, T // P], F32, "gate_cols")
 
         load(xw[:].bitcast(I32), x_words[0].rearrange("p t d -> p (t d)").bitcast(I32))
         load(offs_t[:], offs)
         load(gate_cols[:], gate[:, 0, :].rearrange("r (p a) -> p r a", p=P))
         load_wa(0)
-        load_scales(nc.sync, xs, 0, x_scales[0].rearrange("(q r) t -> r q t", r=4))
+        load_scales(xs, 0, x_scales[0].rearrange("(q r) t -> r q t", r=4))
         for e in (1, 2, 3):
             load_wa(e)
-        load(pos_t[0][:], pos1)
-        load(pos_t[1][:], pos2)
         for e in (4, 5):
             load_wa(e)
+        load_scales(ws, 0, w_scales.rearrange("e s (q r) n -> r q (e s) n", r=4))
         load_wa(6)
         last_raw = [held([P, 2, H], F32, "lastraw0"), placed([P, 2, H], F32, "lastraw1", 0)]
         for half in range(2):
             load(last_raw[half][:], wa_rows[LAST][:, 2 * half : 2 * half + 2, :])
         load_w(0)
+        load_scales(wbs, WB_PLANE, wb_scales.rearrange("e s (q r) n -> r q (e s) n", r=4))
         for experts in BLOCK0_LOADS:
             load_wb(experts, 0)
+        load(pos_t[0][:], pos1)
+        load(pos_t[1][:], pos2)
         load_w(1)
         for experts in BLOCK1_LOADS:
             load_wb(experts, 1)
@@ -123,13 +122,12 @@ def tile_moe_elr_none_kernel(
                 out=gate_t[r][:].rearrange("q (p a) -> q p a", p=P), in_=spread[:].rearrange("q a p -> q p a")
             )
 
-        xg_w, xg_s, pieces = {}, {}, {}
+        xg_w, xg_s = {}, {}
 
         def gather_tokens(table, dtype, name, gathered):
             for chunk in range(S // GATHER):
                 entries = offs_t[:, chunk * GATHER // 16 : (chunk + 1) * GATHER // 16]
                 piece = held([P, GATHER], dtype, "%s%d" % (name, chunk))
-                pieces[name] = piece
                 nc.vector.tensor_copy(piece[:], table[:].indirect(entries))
                 for n in range(GATHER // C):
                     gathered[chunk * GATHER // C + n] = piece[:, n * C : (n + 1) * C]
@@ -140,8 +138,8 @@ def tile_moe_elr_none_kernel(
                 in_=src.rearrange("p j (m a t) -> p m j a t", a=2, t=PACK),
             )
 
-        wa_codes = [held([P, H], U32, "wac%d" % e) for e in range(E)]
-        wa_scales = [held([P, H], U8, "was%d" % e) for e in range(E)]
+        wa_codes = [held([P, H], U32, "wac%d" % e) for e in range(LAST)]
+        wa_scales = [held([P, H], U8, "was%d" % e) for e in range(LAST)]
         grouped = {}
 
         def round_expert(e):
@@ -166,7 +164,20 @@ def tile_moe_elr_none_kernel(
             round_wa(nc.vector.tensor_copy, rounded[:, :, 0:cut, :], source[:, :, 0 : PACK * cut])
             round_wa(nc.scalar.copy, rounded[:, :, cut:P, :], source[:, :, PACK * cut : H])
 
+        last_codes = [held([P, P], U32, "lc%d" % t) for t in range(PACK)]
+        last_scales = [held([P, P], U8, "ls%d" % t) for t in range(PACK)]
+
+        def quantize_last():
+            for t in range(PACK):
+                nc.vector.quantize_mx(
+                    out=last_codes[t][:].bitcast(FP8X4),
+                    scales=last_scales[t][:],
+                    in_=grouped[LAST][:, t].rearrange("p m j -> p (m j)"),
+                )
+
         def stationary_wa(e, t):
+            if e == LAST:
+                return last_codes[t][:], last_scales[t][:]
             return wa_codes[e][:, t * P : (t + 1) * P], wa_scales[e][:, t * P : (t + 1) * P]
 
         h_bank, h_bf, h_codes, h_scales = {}, {}, {}, {}
@@ -250,30 +261,19 @@ def tile_moe_elr_none_kernel(
         round_h(LAST - 2)
         quantize_expert(LAST - 1)
         first_product(LAST - 1)
-        warm = ybanks.tile([P, 2, GATHER], F32, name="warm")
-        for n in range(WARM_UPS):
-            nc.tensor.matmul_mx(
-                out=warm[:, n % 2, :],
-                lhsT=wa_codes[LAST - 1][:, 0:P].bitcast(FP8X4),
-                lhsT_scale=wa_scales[LAST - 1][:, 0:P],
-                rhs=pieces["xgw"][:].bitcast(FP8X4),
-                rhs_scale=pieces["xgs"][:],
-                start=True,
-                stop=True,
-            )
         round_last(0)
         round_last(1)
-        quantize_expert(LAST)
+        quantize_last()
         first_product(LAST)
         round_h(LAST - 1)
         quantize_h(LAST - 2)
         quantize_h(LAST - 1)
         round_h(LAST)
         quantize_h(LAST)
-        second_products(BLOCK0_LOADS[0], 0, nc.vector.tensor_copy, "ybank0")
-        second_products(BLOCK0_LOADS[1], 0, nc.scalar.copy, "ybank1")
-        second_products(BLOCK0_LOADS[2][:-1], 0, nc.scalar.copy, "ybank2")
-        second_products((LAST,), 0, nc.scalar.copy, "ybank3")
+        second_products(BLOCK0_LOADS[0], 0, nc.scalar.copy, "ybank0")
+        second_products(BLOCK0_LOADS[1], 0, nc.vector.tensor_copy, "ybank1")
+        second_products(BLOCK0_LOADS[2], 0, nc.scalar.copy, "ybank2")
+        second_products(BLOCK0_LOADS[3], 0, nc.vector.tensor_copy, "ybank3")
         second_products(BLOCK1_LOADS[0], 1, nc.scalar.copy, "ybank4")
         second_products(BLOCK1_LOADS[1], 1, nc.scalar.copy, "ybank3")
         second_products(BLOCK1_LOADS[2], 1, nc.scalar.copy, "ybank0")
@@ -291,37 +291,10 @@ def tile_moe_elr_none_kernel(
             nc.vector.tensor_tensor(res[b][:, tokens], picked[b][0][:, tokens], picked[b][1][:, tokens], ADD)
             nc.sync.dma_start(out=out[b * P : (b + 1) * P, tokens], in_=res[b][:, tokens])
 
-        def add_by_transposes():
-            summed = ybanks.tile([P, T // P, P], F32, name="ybank0")
-            for c in range(T // P):
-                for r in range(2):
-                    nc.tensor.matmul(
-                        summed[:, c, :],
-                        picked[0][r][:, c * P : (c + 1) * P],
-                        ident[:],
-                        start=r == 0,
-                        stop=r == 1,
-                        is_transpose=True,
-                    )
-            return summed
-
-        def turn_back(summed, half):
-            first = half * T // 2
-            turned = held([P, 2, P], F32, "turned%d" % half)
-            nc.scalar.copy(out=turned[:], in_=summed[:, 2 * half : 2 * half + 2, :])
-            back = ybanks.tile([P, 2, P], F32, name="ybank%d" % (1 + half))
-            for c in range(2):
-                nc.tensor.transpose(back[:, c, :], turned[:, c, :], ident[:])
-            tokens = slice(first, first + T // 2)
-            nc.scalar.copy(out=res[0][:, tokens], in_=back[:].rearrange("p c t -> p (c t)"))
-            nc.sync.dma_start(out=out[0:P, tokens], in_=res[0][:, tokens])
-
         pick(0, 0, 0, T)
         pick(0, 1, 0, T)
         pick(1, 0, 0, T)
-        summed = add_by_transposes()
-        for half in range(2):
-            turn_back(summed, half)
+        finish(0, 0, T)
         for first in (0, T // 2):
             pick(1, 1, first, T // 2)
         for first in (0, T // 2):

@@ -23,6 +23,7 @@ ADD = mybir.AluOpType.add
 GATHER = 256
 LAST = E - 1
 VECTOR_PLACES = (0, 72, 72, 72, 72, 72, 80)
+WARM_UPS = 4
 WB_PLANE = 4
 VECTOR_PLACES_OF_LAST = 84
 BLOCK0_LOADS = ((0, 1, 2), (3, 4), (5, 6), (7,))
@@ -122,12 +123,13 @@ def tile_moe_elr_none_kernel(
                 out=gate_t[r][:].rearrange("q (p a) -> q p a", p=P), in_=spread[:].rearrange("q a p -> q p a")
             )
 
-        xg_w, xg_s = {}, {}
+        xg_w, xg_s, pieces = {}, {}, {}
 
         def gather_tokens(table, dtype, name, gathered):
             for chunk in range(S // GATHER):
                 entries = offs_t[:, chunk * GATHER // 16 : (chunk + 1) * GATHER // 16]
                 piece = held([P, GATHER], dtype, "%s%d" % (name, chunk))
+                pieces[name] = piece
                 nc.vector.tensor_copy(piece[:], table[:].indirect(entries))
                 for n in range(GATHER // C):
                     gathered[chunk * GATHER // C + n] = piece[:, n * C : (n + 1) * C]
@@ -261,6 +263,17 @@ def tile_moe_elr_none_kernel(
         round_h(LAST - 2)
         quantize_expert(LAST - 1)
         first_product(LAST - 1)
+        warm = ybanks.tile([P, 2, GATHER], F32, name="warm")
+        for n in range(WARM_UPS):
+            nc.tensor.matmul_mx(
+                out=warm[:, n % 2, :],
+                lhsT=wa_codes[LAST - 1][:, 0:P].bitcast(FP8X4),
+                lhsT_scale=wa_scales[LAST - 1][:, 0:P],
+                rhs=pieces["xgw"][:].bitcast(FP8X4),
+                rhs_scale=pieces["xgs"][:],
+                start=True,
+                stop=True,
+            )
         round_last(0)
         round_last(1)
         quantize_last()

@@ -22,12 +22,12 @@ ADD = mybir.AluOpType.add
 
 GATHER = 256
 LAST = E - 1
-VECTOR_PLACES = (0, 72, 72, 72, 72, 72, 80)
-WARM_UPS = 4
+VECTOR_PLACES = 84
+WARM_UPS = 3
 WB_PLANE = 4
-VECTOR_PLACES_OF_LAST = 84
-BLOCK0_LOADS = ((0, 1, 2), (3, 4), (5, 6), (7,))
-BLOCK1_LOADS = ((4, 5, 6, 7), (0, 1, 2), (3,))
+BLOCK0_GROUPS = ((0, 1, 2), (3, 4), (5, 6), (7,))
+BLOCK1_GROUPS = ((6, 7), (4, 5), (2, 3), (1,), (0,))
+BLOCK1_BANKS = (4, 3, 0, 1, 2)
 
 
 def tile_moe_elr_none_kernel(
@@ -43,7 +43,8 @@ def tile_moe_elr_none_kernel(
             return keep.tile(shape, dtype, name=name, tag=tag or name, align_bytes=64)
 
         tail = ctx.enter_context(tc.tile_pool(name="tail", bufs=1))
-        last_bytes = 4 * PACK * H // 2
+        last_load_bytes = 4 * 2 * H
+        rounded_h_bytes = 2 * C * PACK
 
         def placed(shape, dtype, name, offset):
             return tail.tile(shape, dtype, name=name, tag=name, align_bytes=64, offset=offset)
@@ -95,23 +96,21 @@ def tile_moe_elr_none_kernel(
         load(gate_cols[:], gate[:, 0, :].rearrange("r (p a) -> p r a", p=P))
         load_wa(0)
         load_scales(xs, 0, x_scales[0].rearrange("(q r) t -> r q t", r=4))
-        for e in (1, 2, 3):
-            load_wa(e)
-        for e in (4, 5):
+        for e in range(1, LAST - 1):
             load_wa(e)
         load_scales(ws, 0, w_scales.rearrange("e s (q r) n -> r q (e s) n", r=4))
-        load_wa(6)
+        load_wa(LAST - 1)
         last_raw = [held([P, 2, H], F32, "lastraw0"), placed([P, 2, H], F32, "lastraw1", 0)]
         for half in range(2):
             load(last_raw[half][:], wa_rows[LAST][:, 2 * half : 2 * half + 2, :])
         load_w(0)
         load_scales(wbs, WB_PLANE, wb_scales.rearrange("e s (q r) n -> r q (e s) n", r=4))
-        for experts in BLOCK0_LOADS:
+        for experts in BLOCK0_GROUPS:
             load_wb(experts, 0)
         load(pos_t[0][:], pos1)
         load(pos_t[1][:], pos2)
         load_w(1)
-        for experts in BLOCK1_LOADS:
+        for experts in BLOCK1_GROUPS:
             load_wb(experts, 1)
 
         gate_t = [held([P, T], F32, "gate%d" % r) for r in range(2)]
@@ -123,13 +122,13 @@ def tile_moe_elr_none_kernel(
                 out=gate_t[r][:].rearrange("q (p a) -> q p a", p=P), in_=spread[:].rearrange("q a p -> q p a")
             )
 
-        xg_w, xg_s, pieces = {}, {}, {}
+        xg_w, xg_s, last_gathered = {}, {}, {}
 
         def gather_tokens(table, dtype, name, gathered):
             for chunk in range(S // GATHER):
                 entries = offs_t[:, chunk * GATHER // 16 : (chunk + 1) * GATHER // 16]
                 piece = held([P, GATHER], dtype, "%s%d" % (name, chunk))
-                pieces[name] = piece
+                last_gathered[name] = piece
                 nc.vector.tensor_copy(piece[:], table[:].indirect(entries))
                 for n in range(GATHER // C):
                     gathered[chunk * GATHER // C + n] = piece[:, n * C : (n + 1) * C]
@@ -146,7 +145,7 @@ def tile_moe_elr_none_kernel(
 
         def round_expert(e):
             grouped[e] = held([P, PACK, P, PACK], BF16, "grp%d" % e)
-            cut = VECTOR_PLACES[e]
+            cut = VECTOR_PLACES if e else 0
             if cut:
                 round_wa(nc.vector.tensor_copy, grouped[e][:, :, 0:cut, :], raw[e][:, :, 0 : PACK * cut])
             round_wa(nc.scalar.copy, grouped[e][:, :, cut:P, :], raw[e][:, :, PACK * cut : H])
@@ -161,7 +160,7 @@ def tile_moe_elr_none_kernel(
         grouped[LAST] = held([P, PACK, P, PACK], BF16, "grp%d" % LAST)
 
         def round_last(half):
-            cut = VECTOR_PLACES_OF_LAST
+            cut = VECTOR_PLACES
             rounded, source = grouped[LAST][:, :, :, 2 * half : 2 * half + 2], last_raw[half]
             round_wa(nc.vector.tensor_copy, rounded[:, :, 0:cut, :], source[:, :, 0 : PACK * cut])
             round_wa(nc.scalar.copy, rounded[:, :, cut:P, :], source[:, :, PACK * cut : H])
@@ -208,7 +207,7 @@ def tile_moe_elr_none_kernel(
 
         def quantize_h(e):
             if e == LAST - 2:
-                h_codes[e] = placed([P, C], U32, "hc%d" % e, 2 * C * PACK)
+                h_codes[e] = placed([P, C], U32, "hc%d" % e, rounded_h_bytes)
             else:
                 h_codes[e] = held([P, C], U32, "hc%d" % e, "grp%d" % LAST if e == LAST - 1 else None)
             h_scales[e] = held([P, C], U8, "hs%d" % e)
@@ -218,10 +217,10 @@ def tile_moe_elr_none_kernel(
                 in_=h_bf[e][:].rearrange("p s t -> p (s t)"),
             )
 
-        y = [placed([P, S], F32, "y0", last_bytes - 64), held([P, S], F32, "y1")]
+        y = [placed([P, S], F32, "y0", last_load_bytes - 64), held([P, S], F32, "y1")]
 
-        def second_products(experts, b, engine_copy, bank_name):
-            bank = ybanks.tile([P, len(experts), C], F32, name=bank_name)
+        def second_products(experts, b, engine_copy, bank_number):
+            bank = ybanks.tile([P, len(experts), C], F32, name="ybank%d" % bank_number)
             outputs = slice(b * P, (b + 1) * P)
             for e in sorted(experts, key=lambda expert: expert != LAST):
                 n = e - experts[0]
@@ -248,6 +247,19 @@ def tile_moe_elr_none_kernel(
                 in_=bank[:].rearrange("p n s -> p (n s)"),
             )
 
+        def warm_up(e):
+            warm = ybanks.tile([P, 2, GATHER], F32, name="warm")
+            for n in range(WARM_UPS):
+                nc.tensor.matmul_mx(
+                    out=warm[:, n % 2, :],
+                    lhsT=wa_codes[e][:, 0:P].bitcast(FP8X4),
+                    lhsT_scale=wa_scales[e][:, 0:P],
+                    rhs=last_gathered["xgw"][:].bitcast(FP8X4),
+                    rhs_scale=last_gathered["xgs"][:],
+                    start=True,
+                    stop=True,
+                )
+
         gather_tokens(xw, U32, "xgw", xg_w)
         gather_tokens(xs, U8, "xgs", xg_s)
         round_expert(0)
@@ -259,21 +271,12 @@ def tile_moe_elr_none_kernel(
             quantize_expert(e)
             quantize_h(e - 1)
             first_product(e)
+        warm_up(LAST - 2)
         round_expert(LAST - 1)
         round_h(LAST - 2)
         quantize_expert(LAST - 1)
         first_product(LAST - 1)
-        warm = ybanks.tile([P, 2, GATHER], F32, name="warm")
-        for n in range(WARM_UPS):
-            nc.tensor.matmul_mx(
-                out=warm[:, n % 2, :],
-                lhsT=wa_codes[LAST - 1][:, 0:P].bitcast(FP8X4),
-                lhsT_scale=wa_scales[LAST - 1][:, 0:P],
-                rhs=pieces["xgw"][:].bitcast(FP8X4),
-                rhs_scale=pieces["xgs"][:],
-                start=True,
-                stop=True,
-            )
+        warm_up(LAST - 1)
         round_last(0)
         round_last(1)
         quantize_last()
@@ -283,13 +286,10 @@ def tile_moe_elr_none_kernel(
         quantize_h(LAST - 1)
         round_h(LAST)
         quantize_h(LAST)
-        second_products(BLOCK0_LOADS[0], 0, nc.scalar.copy, "ybank0")
-        second_products(BLOCK0_LOADS[1], 0, nc.vector.tensor_copy, "ybank1")
-        second_products(BLOCK0_LOADS[2], 0, nc.scalar.copy, "ybank2")
-        second_products(BLOCK0_LOADS[3], 0, nc.vector.tensor_copy, "ybank3")
-        second_products(BLOCK1_LOADS[0], 1, nc.scalar.copy, "ybank4")
-        second_products(BLOCK1_LOADS[1], 1, nc.scalar.copy, "ybank3")
-        second_products(BLOCK1_LOADS[2], 1, nc.scalar.copy, "ybank0")
+        for n, experts in enumerate(BLOCK0_GROUPS):
+            second_products(experts, 0, (nc.scalar.copy, nc.vector.tensor_copy)[n % 2], n)
+        for experts, bank_number in zip(BLOCK1_GROUPS, BLOCK1_BANKS):
+            second_products(experts, 1, nc.scalar.copy, bank_number)
 
         picked = [[held([P, T], F32, "pick%d_%d" % (b, r)) for r in range(2)] for b in range(2)]
         res = [held([P, T], F32, "res%d" % b) for b in range(2)]

@@ -28,6 +28,7 @@ WB_PLANE = 4
 BLOCK0_GROUPS = ((0, 1, 2), (3, 4), (5, 6), (7,))
 BLOCK1_GROUPS = ((6, 7), (4, 5), (2, 3), (1,), (0,))
 BLOCK1_BANKS = (4, 3, 0, 1, 2)
+LATE_H = (0, 3, 5, 6)
 
 
 def tile_moe_elr_none_kernel(
@@ -98,11 +99,11 @@ def tile_moe_elr_none_kernel(
         load_scales(xs, 0, x_scales[0].rearrange("(q r) t -> r q t", r=4))
         for e in range(1, LAST - 1):
             load_wa(e)
-        load_scales(ws, 0, w_scales.rearrange("e s (q r) n -> r q (e s) n", r=4))
         load_wa(LAST - 1)
         last_raw = [held([P, 2, H], F32, "lastraw0"), placed([P, 2, H], F32, "lastraw1", 0)]
         for half in range(2):
             load(last_raw[half][:], wa_rows[LAST][:, 2 * half : 2 * half + 2, :])
+        load_scales(ws, 0, w_scales.rearrange("e s (q r) n -> r q (e s) n", r=4))
         load_w(0)
         load_scales(wbs, WB_PLANE, wb_scales.rearrange("e s (q r) n -> r q (e s) n", r=4))
         for experts in BLOCK0_GROUPS:
@@ -157,7 +158,8 @@ def tile_moe_elr_none_kernel(
                 in_=grouped[e][:].rearrange("p t m j -> p (t m j)"),
             )
 
-        grouped[LAST] = held([P, PACK, P, PACK], BF16, "grp%d" % LAST)
+        last_grouped_at = 2 * last_load_bytes + rounded_h_bytes
+        grouped[LAST] = placed([P, PACK, P, PACK], BF16, "grp%d" % LAST, last_grouped_at)
 
         def round_last(half):
             cut = VECTOR_PLACES
@@ -200,16 +202,17 @@ def tile_moe_elr_none_kernel(
         def round_h(e):
             if e == LAST - 1:
                 h_bf[e] = placed([P, C, PACK], BF16, "hbf%d" % e, 0)
+            elif e == LAST:
+                h_bf[e] = placed([P, C, PACK], BF16, "hbf%d" % e, last_load_bytes)
             else:
-                reuse = None if e == LAST else "raw%d" % (e + 1)
-                h_bf[e] = held([P, C, PACK], BF16, "hbf%d" % e, reuse)
+                h_bf[e] = held([P, C, PACK], BF16, "hbf%d" % e, "raw%d" % (e + 1))
             nc.scalar.copy(out=h_bf[e][:], in_=h_bank[e][:].rearrange("p t s -> p s t"))
 
         def quantize_h(e):
-            if e == LAST - 2:
-                h_codes[e] = placed([P, C], U32, "hc%d" % e, rounded_h_bytes)
+            if e in LATE_H:
+                h_codes[e] = placed([P, C], U32, "hc%d" % e, last_grouped_at + 4 * C * LATE_H.index(e))
             else:
-                h_codes[e] = held([P, C], U32, "hc%d" % e, "grp%d" % LAST if e == LAST - 1 else None)
+                h_codes[e] = held([P, C], U32, "hc%d" % e)
             h_scales[e] = held([P, C], U8, "hs%d" % e)
             nc.vector.quantize_mx(
                 out=h_codes[e][:].bitcast(FP8X4),
@@ -217,7 +220,7 @@ def tile_moe_elr_none_kernel(
                 in_=h_bf[e][:].rearrange("p s t -> p (s t)"),
             )
 
-        y = [placed([P, S], F32, "y0", last_load_bytes - 64), held([P, S], F32, "y1")]
+        y = [placed([P, S], F32, "y0", last_load_bytes + rounded_h_bytes - 64), held([P, S], F32, "y1")]
 
         def second_products(experts, b, engine_copy, bank_number):
             bank = ybanks.tile([P, len(experts), C], F32, name="ybank%d" % bank_number)
@@ -226,19 +229,19 @@ def tile_moe_elr_none_kernel(
                 n = e - experts[0]
                 nc.tensor.matmul_mx(
                     out=bank[:, n, :],
-                    lhsT=w_t[b][:, e, :].bitcast(FP4X4),
-                    lhsT_scale=ws[:, e, outputs],
-                    rhs=xg_w[e].bitcast(FP8X4),
-                    rhs_scale=xg_s[e],
+                    lhsT=wb_t[e, b].bitcast(FP8X4),
+                    lhsT_scale=wbs[WB_PLANE:P, e, outputs],
+                    rhs=h_codes[e][:].bitcast(FP8X4),
+                    rhs_scale=h_scales[e][:],
                     start=True,
                     stop=False,
                 )
                 nc.tensor.matmul_mx(
                     out=bank[:, n, :],
-                    lhsT=wb_t[e, b].bitcast(FP8X4),
-                    lhsT_scale=wbs[WB_PLANE:P, e, outputs],
-                    rhs=h_codes[e][:].bitcast(FP8X4),
-                    rhs_scale=h_scales[e][:],
+                    lhsT=w_t[b][:, e, :].bitcast(FP4X4),
+                    lhsT_scale=ws[:, e, outputs],
+                    rhs=xg_w[e].bitcast(FP8X4),
+                    rhs_scale=xg_s[e],
                     start=False,
                     stop=True,
                 )
@@ -249,11 +252,12 @@ def tile_moe_elr_none_kernel(
 
         def warm_up(e):
             warm = ybanks.tile([P, 2, GATHER], F32, name="warm")
+            codes, scales = stationary_wa(e, PACK - 1)
             for n in range(WARM_UPS):
                 nc.tensor.matmul_mx(
                     out=warm[:, n % 2, :],
-                    lhsT=wa_codes[e][:, 0:P].bitcast(FP8X4),
-                    lhsT_scale=wa_scales[e][:, 0:P],
+                    lhsT=codes.bitcast(FP8X4),
+                    lhsT_scale=scales,
                     rhs=last_gathered["xgw"][:].bitcast(FP8X4),
                     rhs_scale=last_gathered["xgs"][:],
                     start=True,
@@ -269,9 +273,9 @@ def tile_moe_elr_none_kernel(
             round_expert(e)
             round_h(e - 1)
             quantize_expert(e)
-            quantize_h(e - 1)
+            if e - 1 not in LATE_H:
+                quantize_h(e - 1)
             first_product(e)
-        warm_up(LAST - 2)
         round_expert(LAST - 1)
         round_h(LAST - 2)
         quantize_expert(LAST - 1)
@@ -281,9 +285,10 @@ def tile_moe_elr_none_kernel(
         round_last(1)
         quantize_last()
         first_product(LAST)
+        warm_up(LAST)
         round_h(LAST - 1)
-        quantize_h(LAST - 2)
-        quantize_h(LAST - 1)
+        for e in LATE_H:
+            quantize_h(e)
         round_h(LAST)
         quantize_h(LAST)
         for n, experts in enumerate(BLOCK0_GROUPS):
@@ -291,7 +296,7 @@ def tile_moe_elr_none_kernel(
         for experts, bank_number in zip(BLOCK1_GROUPS, BLOCK1_BANKS):
             second_products(experts, 1, nc.scalar.copy, bank_number)
 
-        picked = [[held([P, T], F32, "pick%d_%d" % (b, r)) for r in range(2)] for b in range(2)]
+        picked = {}
         res = [held([P, T], F32, "res%d" % b) for b in range(2)]
 
         def pick(b, r, first, count):
@@ -302,13 +307,16 @@ def tile_moe_elr_none_kernel(
         def finish(b, first, count):
             tokens = slice(first, first + count)
             nc.vector.tensor_tensor(res[b][:, tokens], picked[b][0][:, tokens], picked[b][1][:, tokens], ADD)
-            nc.sync.dma_start(out=out[b * P : (b + 1) * P, tokens], in_=res[b][:, tokens])
+            if b == 1:
+                nc.sync.dma_start(out=out[b * P : (b + 1) * P, tokens], in_=res[b][:, tokens])
+            elif first:
+                nc.sync.dma_start(out=out[b * P : (b + 1) * P, :], in_=res[b][:])
 
-        pick(0, 0, 0, T)
-        pick(0, 1, 0, T)
-        pick(1, 0, 0, T)
-        finish(0, 0, T)
-        for first in (0, T // 2):
-            pick(1, 1, first, T // 2)
-        for first in (0, T // 2):
-            finish(1, first, T // 2)
+        halves = (0, T // 2)
+        for b in range(2):
+            picked[b] = [held([P, T], F32, "pick%d_%d" % (b, r), "pick%d" % r) for r in range(2)]
+            pick(b, 0, 0, T)
+            for first in halves:
+                pick(b, 1, first, T // 2)
+            for first in halves:
+                finish(b, first, T // 2)

@@ -25,10 +25,11 @@ LAST = E - 1
 VECTOR_PLACES = 84
 WARM_UPS = 3
 WB_PLANE = 4
-BLOCK0_GROUPS = ((0, 1, 2), (3, 4), (5, 6), (7,))
+BLOCK0_GROUPS = ((0, 1, 2), (3, 4, 5), (6,), (7,))
 BLOCK1_GROUPS = ((6, 7), (4, 5), (2, 3), (1,), (0,))
 BLOCK1_BANKS = (4, 3, 0, 1, 2)
 LATE_H = (0, 3, 5, 6)
+GATE_RUN = 2 * T // P
 
 
 def tile_moe_elr_none_kernel(
@@ -69,9 +70,15 @@ def tile_moe_elr_none_kernel(
         wa_rows = wa.rearrange("e (p j) i -> e p j i", j=PACK)
         raw = {}
 
-        def load_wa(e):
-            raw[e] = held([P, PACK, H], F32, "raw%d" % e)
-            load(raw[e][:], wa_rows[e])
+        raw_tag = {}
+
+        def load_wa(first, count=1):
+            name = "raw%d" % first
+            rows = held([P, count, PACK * H], F32, name)
+            load(rows[:], wa[first : first + count].rearrange("e (p j) i -> p e (j i)", j=PACK))
+            for n in range(count):
+                raw[first + n] = rows[:, n, :].rearrange("p (j i) -> p j i", j=PACK)
+            raw_tag[first + count - 1] = name
 
         w_view = w_words.rearrange("e s p c -> p (e s) c")
         wb_view = wb_words.rearrange("e s p n d -> p (e s) (n d)")
@@ -90,11 +97,12 @@ def tile_moe_elr_none_kernel(
 
         ident = held([P, P], F32, "ident")
         make_identity(nc, ident[:])
-        gate_cols = held([P, 2, T // P], F32, "gate_cols")
+        gate_cols = held([P, GATE_RUN], F32, "gate_cols")
 
         load(xw[:].bitcast(I32), x_words[0].rearrange("p t d -> p (t d)").bitcast(I32))
         load(offs_t[:], offs)
-        load(gate_cols[:], gate[:, 0, :].rearrange("r (p a) -> p r a", p=P))
+        gate_runs = gate.rearrange("r p (x a) -> (r p x) a", a=GATE_RUN)
+        load(gate_cols[:], gate_runs[0 : P * P : P + 1, :])
         load_wa(0)
         load_scales(xs, 0, x_scales[0].rearrange("(q r) t -> r q t", r=4))
         for e in range(1, LAST - 1):
@@ -114,13 +122,15 @@ def tile_moe_elr_none_kernel(
         for experts in BLOCK1_GROUPS:
             load_wb(experts, 1)
 
-        gate_t = [held([P, T], F32, "gate%d" % r) for r in range(2)]
-        for r in range(2):
-            spread = ybanks.tile([P, T // P, P], F32, name="ybank%d" % r)
-            for a in range(T // P):
-                nc.tensor.transpose(spread[:, a, :], gate_cols[:, r, a : a + 1].to_broadcast([P, P]), ident[:])
+        gate_t = held([P, 2 * T], F32, "gate_t")
+        for half in range(2):
+            spread = ybanks.tile([P, 4, P], F32, name="ybank%d" % half)
+            for a in range(4):
+                column = 4 * half + a
+                nc.tensor.transpose(spread[:, a, :], gate_cols[:, column : column + 1].to_broadcast([P, P]), ident[:])
             nc.scalar.copy(
-                out=gate_t[r][:].rearrange("q (p a) -> q p a", p=P), in_=spread[:].rearrange("q a p -> q p a")
+                out=gate_t[:].rearrange("q (p a) -> q p a", p=P)[:, :, 4 * half : 4 * half + 4],
+                in_=spread[:].rearrange("q a p -> q p a"),
             )
 
         xg_w, xg_s, last_gathered = {}, {}, {}
@@ -205,7 +215,7 @@ def tile_moe_elr_none_kernel(
             elif e == LAST:
                 h_bf[e] = placed([P, C, PACK], BF16, "hbf%d" % e, last_load_bytes)
             else:
-                h_bf[e] = held([P, C, PACK], BF16, "hbf%d" % e, "raw%d" % (e + 1))
+                h_bf[e] = held([P, C, PACK], BF16, "hbf%d" % e, raw_tag.get(e + 1))
             nc.scalar.copy(out=h_bf[e][:], in_=h_bank[e][:].rearrange("p t s -> p s t"))
 
         def quantize_h(e):
@@ -302,21 +312,41 @@ def tile_moe_elr_none_kernel(
         def pick(b, r, first, count):
             tokens = slice(first, first + count)
             entries = pos_t[r][:, first // 16 : (first + count) // 16]
-            nc.vector.tensor_tensor(picked[b][r][:, tokens], y[b][:].indirect(entries), gate_t[r][:, tokens], MULT)
+            nc.vector.tensor_tensor(picked[b][r][:, tokens], y[b][:].indirect(entries), gate_t[:, r * T + first : r * T + first + count], MULT)
 
         def finish(b, first, count):
             tokens = slice(first, first + count)
             nc.vector.tensor_tensor(res[b][:, tokens], picked[b][0][:, tokens], picked[b][1][:, tokens], ADD)
-            if b == 1:
-                nc.sync.dma_start(out=out[b * P : (b + 1) * P, tokens], in_=res[b][:, tokens])
-            elif first:
-                nc.sync.dma_start(out=out[b * P : (b + 1) * P, :], in_=res[b][:])
+            nc.sync.dma_start(out=out[b * P : (b + 1) * P, tokens], in_=res[b][:, tokens])
 
         halves = (0, T // 2)
         for b in range(2):
-            picked[b] = [held([P, T], F32, "pick%d_%d" % (b, r), "pick%d" % r) for r in range(2)]
-            pick(b, 0, 0, T)
-            for first in halves:
-                pick(b, 1, first, T // 2)
-            for first in halves:
-                finish(b, first, T // 2)
+            picked[b] = [held([P, T], F32, "pick%d_%d" % (b, r)) for r in range(2)]
+        def finish_by_transposes(first, banks):
+            chunks = T // 2 // P
+            turned = ybanks.tile([P, chunks, P], F32, name="ybank%d" % banks[0])
+            for a in range(chunks):
+                tokens = slice(first + a * P, first + (a + 1) * P)
+                for r in range(2):
+                    nc.tensor.matmul(
+                        turned[:, a, :], picked[0][r][:, tokens], ident[:], is_transpose=True, start=r == 0, stop=r == 1
+                    )
+            summed = held([P, chunks, P], F32, "summed%d" % first)
+            nc.scalar.copy(out=summed[:], in_=turned[:])
+            back = ybanks.tile([P, chunks, P], F32, name="ybank%d" % banks[1])
+            for a in range(chunks):
+                nc.tensor.transpose(back[:, a, :], summed[:, a, :], ident[:])
+            tokens = slice(first, first + T // 2)
+            nc.scalar.copy(out=res[0][:, tokens], in_=back[:].rearrange("p a t -> p (a t)"))
+            nc.scalar.dma_start(out=out[0:P, tokens], in_=res[0][:, tokens])
+
+        pick(0, 0, 0, T)
+        for first in halves:
+            pick(0, 1, first, T // 2)
+        finish_by_transposes(0, (2, 0))
+        finish_by_transposes(T // 2, (1, 3))
+        pick(1, 0, 0, T)
+        for first in halves:
+            pick(1, 1, first, T // 2)
+        for first in halves:
+            finish(1, first, T // 2)

@@ -21,14 +21,20 @@ MULT = mybir.AluOpType.mult
 ADD = mybir.AluOpType.add
 
 GATHER = 256
+GATHERS = ((0, 1, 2), (3, 4, 5), (6, 7))
 LAST = E - 1
 VECTOR_PLACES = 84
-WARM_UPS = 3
-WB_PLANE = 4
+WARM_UPS = 2
+WB_PLANE = 0
 BLOCK0_GROUPS = ((0, 1, 2), (3, 4, 5), (6,), (7,))
-BLOCK1_GROUPS = ((6, 7), (4, 5), (2, 3), (1,), (0,))
-BLOCK1_BANKS = (4, 3, 0, 1, 2)
+BLOCK0_LOADS = ((0, 1, 2, 3), (4, 5, 6, 7))
+W_LOADS = ((0, 1, 2), (3, 4, 5), (6, 7))
+BLOCK1_LOADS = ((4, 5, 6, 7), (2, 3), (0, 1))
+BLOCK1_GROUPS = ((4, 5, 6, 7), (0, 1, 2, 3))
+BLOCK0_BANKS = (0, 1, 2, 3)
+BLOCK1_BANKS = (4, 3)
 LATE_H = (0, 3, 5, 6)
+H_PLANES = ((0, 1, 2, 5), (3, 4, 6), (7,))
 GATE_RUN = 2 * T // P
 
 
@@ -38,7 +44,6 @@ def tile_moe_elr_none_kernel(
     nc = tc.nc
     with ExitStack() as ctx:
         keep = ctx.enter_context(tc.tile_pool(name="keep", bufs=1))
-        hbanks = ctx.enter_context(tc.psum_pool(name="hbanks", bufs=2))
         ybanks = ctx.enter_context(tc.psum_pool(name="ybanks", bufs=1))
 
         def held(shape, dtype, name, tag=None):
@@ -84,6 +89,13 @@ def tile_moe_elr_none_kernel(
         wb_view = wb_words.rearrange("e s p n d -> p (e s) (n d)")
         w_t, wb_t = {}, {}
 
+        def load_w(experts):
+            group = held([P, len(experts), 2 * N], U8, "w%d" % experts[0])
+            load(group[:].bitcast(I32), w_view[:, experts[0] : experts[-1] + 1, :].bitcast(I32))
+            for n, e in enumerate(experts):
+                w_t[e] = group[:, n, :]
+
+
         def load_wb(experts, b):
             group = held([P, len(experts), 4 * P], U8, "wb%d_%d" % (experts[0], b))
             rows = slice(experts[0], experts[-1] + 1)
@@ -91,9 +103,6 @@ def tile_moe_elr_none_kernel(
             for n, e in enumerate(experts):
                 wb_t[e, b] = group[:, n, :]
 
-        def load_w(b):
-            w_t[b] = held([P, E, 2 * P], U8, "w%d" % b)
-            load(w_t[b][:].bitcast(I32), w_view[:, :, 2 * b * P : 2 * (b + 1) * P].bitcast(I32))
 
         ident = held([P, P], F32, "ident")
         make_identity(nc, ident[:])
@@ -111,15 +120,15 @@ def tile_moe_elr_none_kernel(
         last_raw = [held([P, 2, H], F32, "lastraw0"), placed([P, 2, H], F32, "lastraw1", 0)]
         for half in range(2):
             load(last_raw[half][:], wa_rows[LAST][:, 2 * half : 2 * half + 2, :])
-        load_scales(ws, 0, w_scales.rearrange("e s (q r) n -> r q (e s) n", r=4))
-        load_w(0)
         load_scales(wbs, WB_PLANE, wb_scales.rearrange("e s (q r) n -> r q (e s) n", r=4))
-        for experts in BLOCK0_GROUPS:
+        for experts in BLOCK0_LOADS:
             load_wb(experts, 0)
+        load_scales(ws, 0, w_scales.rearrange("e s (q r) n -> r q (e s) n", r=4))
+        for experts in W_LOADS:
+            load_w(experts)
         load(pos_t[0][:], pos1)
         load(pos_t[1][:], pos2)
-        load_w(1)
-        for experts in BLOCK1_GROUPS:
+        for experts in BLOCK1_LOADS:
             load_wb(experts, 1)
 
         gate_t = held([P, 2 * T], F32, "gate_t")
@@ -136,13 +145,13 @@ def tile_moe_elr_none_kernel(
         xg_w, xg_s, last_gathered = {}, {}, {}
 
         def gather_tokens(table, dtype, name, gathered):
-            for chunk in range(S // GATHER):
-                entries = offs_t[:, chunk * GATHER // 16 : (chunk + 1) * GATHER // 16]
-                piece = held([P, GATHER], dtype, "%s%d" % (name, chunk))
+            for experts in GATHERS:
+                entries = offs_t[:, experts[0] * C // 16 : (experts[-1] + 1) * C // 16]
+                piece = held([P, len(experts) * C], dtype, "%s%d" % (name, experts[0]))
                 last_gathered[name] = piece
                 nc.vector.tensor_copy(piece[:], table[:].indirect(entries))
-                for n in range(GATHER // C):
-                    gathered[chunk * GATHER // C + n] = piece[:, n * C : (n + 1) * C]
+                for n, e in enumerate(experts):
+                    gathered[e] = piece[:, n * C : (n + 1) * C]
 
         def round_wa(engine_copy, dst, src):
             engine_copy(
@@ -194,9 +203,13 @@ def tile_moe_elr_none_kernel(
             return wa_codes[e][:, t * P : (t + 1) * P], wa_scales[e][:, t * P : (t + 1) * P]
 
         h_bank, h_bf, h_codes, h_scales = {}, {}, {}, {}
+        for experts in H_PLANES:
+            planes = held([P, C], U8, "hs%d" % experts[0])
+            for n, e in enumerate(experts):
+                h_scales[e] = planes[4 * n : P, :]
 
         def first_product(e):
-            h_bank[e] = hbanks.tile([P, PACK, C], F32, name="hbank")
+            h_bank[e] = ybanks.tile([P, PACK, C], F32, name="ybank%d" % (5 + e % 2))
             for t in range(PACK):
                 codes, scales = stationary_wa(e, t)
                 nc.tensor.matmul_mx(
@@ -223,38 +236,36 @@ def tile_moe_elr_none_kernel(
                 h_codes[e] = placed([P, C], U32, "hc%d" % e, last_grouped_at + 4 * C * LATE_H.index(e))
             else:
                 h_codes[e] = held([P, C], U32, "hc%d" % e)
-            h_scales[e] = held([P, C], U8, "hs%d" % e)
             nc.vector.quantize_mx(
                 out=h_codes[e][:].bitcast(FP8X4),
-                scales=h_scales[e][:],
+                scales=h_scales[e],
                 in_=h_bf[e][:].rearrange("p s t -> p (s t)"),
             )
 
         y = [placed([P, S], F32, "y0", last_load_bytes + rounded_h_bytes - 64), held([P, S], F32, "y1")]
 
-        def second_products(experts, b, engine_copy, bank_number):
-            bank = ybanks.tile([P, len(experts), C], F32, name="ybank%d" % bank_number)
+        def second_pass(bank, place, e, b, frozen, start=False, stop=False):
             outputs = slice(b * P, (b + 1) * P)
-            for e in sorted(experts, key=lambda expert: expert != LAST):
-                n = e - experts[0]
-                nc.tensor.matmul_mx(
-                    out=bank[:, n, :],
-                    lhsT=wb_t[e, b].bitcast(FP8X4),
-                    lhsT_scale=wbs[WB_PLANE:P, e, outputs],
-                    rhs=h_codes[e][:].bitcast(FP8X4),
-                    rhs_scale=h_scales[e][:],
-                    start=True,
-                    stop=False,
-                )
-                nc.tensor.matmul_mx(
-                    out=bank[:, n, :],
-                    lhsT=w_t[b][:, e, :].bitcast(FP4X4),
-                    lhsT_scale=ws[:, e, outputs],
-                    rhs=xg_w[e].bitcast(FP8X4),
-                    rhs_scale=xg_s[e],
-                    start=False,
-                    stop=True,
-                )
+            if frozen:
+                words, scales = w_t[e][:, 2 * b * P : 2 * (b + 1) * P].bitcast(FP4X4), ws[:, e, outputs]
+                moving, moving_scales = xg_w[e], xg_s[e]
+            else:
+                words, scales = wb_t[e, b].bitcast(FP8X4), wbs[WB_PLANE:P, e, outputs]
+                moving, moving_scales = h_codes[e][:], h_scales[e]
+            nc.tensor.matmul_mx(
+                out=bank[:, place, :],
+                lhsT=words,
+                lhsT_scale=scales,
+                rhs=moving.bitcast(FP8X4),
+                rhs_scale=moving_scales,
+                start=start,
+                stop=stop,
+            )
+
+        def y_bank(experts, bank_number):
+            return ybanks.tile([P, len(experts), C], F32, name="ybank%d" % bank_number)
+
+        def empty_bank(bank, experts, b, engine_copy):
             engine_copy(
                 out=y[b][:, experts[0] * C : (experts[-1] + 1) * C],
                 in_=bank[:].rearrange("p n s -> p (n s)"),
@@ -286,6 +297,7 @@ def tile_moe_elr_none_kernel(
             if e - 1 not in LATE_H:
                 quantize_h(e - 1)
             first_product(e)
+        warm_up(LAST - 2)
         round_expert(LAST - 1)
         round_h(LAST - 2)
         quantize_expert(LAST - 1)
@@ -301,10 +313,23 @@ def tile_moe_elr_none_kernel(
             quantize_h(e)
         round_h(LAST)
         quantize_h(LAST)
-        for n, experts in enumerate(BLOCK0_GROUPS):
-            second_products(experts, 0, (nc.scalar.copy, nc.vector.tensor_copy)[n % 2], n)
-        for experts, bank_number in zip(BLOCK1_GROUPS, BLOCK1_BANKS):
-            second_products(experts, 1, nc.scalar.copy, bank_number)
+        banks = [y_bank(experts, number) for experts, number in zip(BLOCK0_GROUPS, BLOCK0_BANKS)]
+        for bank, experts in zip(banks, BLOCK0_GROUPS):
+            for place, e in enumerate(experts):
+                second_pass(bank, place, e, 0, frozen=False, start=place == 0)
+        for n, (bank, experts) in enumerate(zip(banks, BLOCK0_GROUPS)):
+            for place, e in enumerate(experts):
+                second_pass(bank, place, e, 0, frozen=True, stop=e == experts[-1])
+            empty_bank(bank, experts, 0, (nc.scalar.copy, nc.vector.tensor_copy)[n % 2])
+        for experts, number in zip(BLOCK1_GROUPS, BLOCK1_BANKS):
+            bank = y_bank(experts, number)
+            order = [(e, True) for e in experts] + [(e, False) for e in reversed(experts)]
+            if LAST in experts:
+                order.remove((LAST, False))
+                order = [(LAST, False)] + order
+            for k, (e, frozen) in enumerate(order):
+                second_pass(bank, e - experts[0], e, 1, frozen, start=k == 0, stop=k == len(order) - 1)
+            empty_bank(bank, experts, 1, nc.scalar.copy)
 
         picked = {}
         res = [held([P, T], F32, "res%d" % b) for b in range(2)]
@@ -317,36 +342,16 @@ def tile_moe_elr_none_kernel(
         def finish(b, first, count):
             tokens = slice(first, first + count)
             nc.vector.tensor_tensor(res[b][:, tokens], picked[b][0][:, tokens], picked[b][1][:, tokens], ADD)
-            nc.sync.dma_start(out=out[b * P : (b + 1) * P, tokens], in_=res[b][:, tokens])
+            if b == 1:
+                nc.sync.dma_start(out=out[b * P : (b + 1) * P, tokens], in_=res[b][:, tokens])
+            elif first:
+                nc.sync.dma_start(out=out[b * P : (b + 1) * P, :], in_=res[b][:])
 
         halves = (0, T // 2)
         for b in range(2):
-            picked[b] = [held([P, T], F32, "pick%d_%d" % (b, r)) for r in range(2)]
-        def finish_by_transposes(first, banks):
-            chunks = T // 2 // P
-            turned = ybanks.tile([P, chunks, P], F32, name="ybank%d" % banks[0])
-            for a in range(chunks):
-                tokens = slice(first + a * P, first + (a + 1) * P)
-                for r in range(2):
-                    nc.tensor.matmul(
-                        turned[:, a, :], picked[0][r][:, tokens], ident[:], is_transpose=True, start=r == 0, stop=r == 1
-                    )
-            summed = held([P, chunks, P], F32, "summed%d" % first)
-            nc.scalar.copy(out=summed[:], in_=turned[:])
-            back = ybanks.tile([P, chunks, P], F32, name="ybank%d" % banks[1])
-            for a in range(chunks):
-                nc.tensor.transpose(back[:, a, :], summed[:, a, :], ident[:])
-            tokens = slice(first, first + T // 2)
-            nc.scalar.copy(out=res[0][:, tokens], in_=back[:].rearrange("p a t -> p (a t)"))
-            nc.scalar.dma_start(out=out[0:P, tokens], in_=res[0][:, tokens])
-
-        pick(0, 0, 0, T)
-        for first in halves:
-            pick(0, 1, first, T // 2)
-        finish_by_transposes(0, (2, 0))
-        finish_by_transposes(T // 2, (1, 3))
-        pick(1, 0, 0, T)
-        for first in halves:
-            pick(1, 1, first, T // 2)
-        for first in halves:
-            finish(1, first, T // 2)
+            picked[b] = [held([P, T], F32, "pick%d_%d" % (b, r), "pick%d" % r) for r in range(2)]
+            pick(b, 0, 0, T)
+            for first in halves:
+                pick(b, 1, first, T // 2)
+            for first in halves:
+                finish(b, first, T // 2)

@@ -30,12 +30,11 @@ BLOCK0_GROUPS = ((0, 1, 2), (3, 4, 5), (6,), (7,))
 BLOCK0_LOADS = ((0, 1, 2, 3), (4, 5, 6, 7))
 W_LOADS = ((0, 1, 2), (3, 4, 5), (6, 7))
 BLOCK1_LOADS = ((4, 5, 6, 7), (2, 3), (0, 1))
-BLOCK1_GROUPS = ((4, 5, 6, 7), (0, 1, 2, 3))
+BLOCK1_GROUPS = ((4, 5, 6, 7), (2, 3), (0, 1))
 BLOCK0_BANKS = (0, 1, 2, 3)
-BLOCK1_BANKS = (4, 3)
+BLOCK1_BANKS = (4, 3, 2)
 LATE_H = (0, 3, 5, 6)
 H_PLANES = ((0, 1, 2, 5), (3, 4, 6), (7,))
-GATE_RUN = 2 * T // P
 
 
 def tile_moe_elr_none_kernel(
@@ -75,15 +74,9 @@ def tile_moe_elr_none_kernel(
         wa_rows = wa.rearrange("e (p j) i -> e p j i", j=PACK)
         raw = {}
 
-        raw_tag = {}
-
-        def load_wa(first, count=1):
-            name = "raw%d" % first
-            rows = held([P, count, PACK * H], F32, name)
-            load(rows[:], wa[first : first + count].rearrange("e (p j) i -> p e (j i)", j=PACK))
-            for n in range(count):
-                raw[first + n] = rows[:, n, :].rearrange("p (j i) -> p j i", j=PACK)
-            raw_tag[first + count - 1] = name
+        def load_wa(e):
+            raw[e] = held([P, PACK, H], F32, "raw%d" % e)
+            load(raw[e][:], wa_rows[e])
 
         w_view = w_words.rearrange("e s p c -> p (e s) c")
         wb_view = wb_words.rearrange("e s p n d -> p (e s) (n d)")
@@ -106,12 +99,11 @@ def tile_moe_elr_none_kernel(
 
         ident = held([P, P], F32, "ident")
         make_identity(nc, ident[:])
-        gate_cols = held([P, GATE_RUN], F32, "gate_cols")
+        gate_cols = held([P, 2, T // P], F32, "gate_cols")
 
         load(xw[:].bitcast(I32), x_words[0].rearrange("p t d -> p (t d)").bitcast(I32))
         load(offs_t[:], offs)
-        gate_runs = gate.rearrange("r p (x a) -> (r p x) a", a=GATE_RUN)
-        load(gate_cols[:], gate_runs[0 : P * P : P + 1, :])
+        load(gate_cols[:], gate[:, 0, :].rearrange("r (p a) -> p r a", p=P))
         load_wa(0)
         load_scales(xs, 0, x_scales[0].rearrange("(q r) t -> r q t", r=4))
         for e in range(1, LAST - 1):
@@ -131,15 +123,13 @@ def tile_moe_elr_none_kernel(
         for experts in BLOCK1_LOADS:
             load_wb(experts, 1)
 
-        gate_t = held([P, 2 * T], F32, "gate_t")
-        for half in range(2):
-            spread = ybanks.tile([P, 4, P], F32, name="ybank%d" % half)
-            for a in range(4):
-                column = 4 * half + a
-                nc.tensor.transpose(spread[:, a, :], gate_cols[:, column : column + 1].to_broadcast([P, P]), ident[:])
+        gate_t = [held([P, T], F32, "gate%d" % r) for r in range(2)]
+        for r in range(2):
+            spread = ybanks.tile([P, T // P, P], F32, name="ybank%d" % r)
+            for a in range(T // P):
+                nc.tensor.transpose(spread[:, a, :], gate_cols[:, r, a : a + 1].to_broadcast([P, P]), ident[:])
             nc.scalar.copy(
-                out=gate_t[:].rearrange("q (p a) -> q p a", p=P)[:, :, 4 * half : 4 * half + 4],
-                in_=spread[:].rearrange("q a p -> q p a"),
+                out=gate_t[r][:].rearrange("q (p a) -> q p a", p=P), in_=spread[:].rearrange("q a p -> q p a")
             )
 
         xg_w, xg_s, last_gathered = {}, {}, {}
@@ -228,7 +218,7 @@ def tile_moe_elr_none_kernel(
             elif e == LAST:
                 h_bf[e] = placed([P, C, PACK], BF16, "hbf%d" % e, last_load_bytes)
             else:
-                h_bf[e] = held([P, C, PACK], BF16, "hbf%d" % e, raw_tag.get(e + 1))
+                h_bf[e] = held([P, C, PACK], BF16, "hbf%d" % e, "raw%d" % (e + 1))
             nc.scalar.copy(out=h_bf[e][:], in_=h_bank[e][:].rearrange("p t s -> p s t"))
 
         def quantize_h(e):
@@ -337,21 +327,45 @@ def tile_moe_elr_none_kernel(
         def pick(b, r, first, count):
             tokens = slice(first, first + count)
             entries = pos_t[r][:, first // 16 : (first + count) // 16]
-            nc.vector.tensor_tensor(picked[b][r][:, tokens], y[b][:].indirect(entries), gate_t[:, r * T + first : r * T + first + count], MULT)
+            nc.vector.tensor_tensor(picked[b][r][:, tokens], y[b][:].indirect(entries), gate_t[r][:, tokens], MULT)
 
         def finish(b, first, count):
             tokens = slice(first, first + count)
             nc.vector.tensor_tensor(res[b][:, tokens], picked[b][0][:, tokens], picked[b][1][:, tokens], ADD)
-            if b == 1:
-                nc.sync.dma_start(out=out[b * P : (b + 1) * P, tokens], in_=res[b][:, tokens])
-            elif first:
-                nc.sync.dma_start(out=out[b * P : (b + 1) * P, :], in_=res[b][:])
+            nc.sync.dma_start(out=out[b * P : (b + 1) * P, tokens], in_=res[b][:, tokens])
 
         halves = (0, T // 2)
         for b in range(2):
-            picked[b] = [held([P, T], F32, "pick%d_%d" % (b, r), "pick%d" % r) for r in range(2)]
-            pick(b, 0, 0, T)
-            for first in halves:
-                pick(b, 1, first, T // 2)
-            for first in halves:
-                finish(b, first, T // 2)
+            picked[b] = [held([P, T], F32, "pick%d_%d" % (b, r)) for r in range(2)]
+        def finish_by_transposes(first, banks):
+            chunks = T // 2 // P
+            turned = ybanks.tile([P, chunks, P], F32, name="ybank%d" % banks[0])
+            for r in range(2):
+                for a in range(chunks):
+                    nc.tensor.matmul(
+                        turned[:, a, :],
+                        picked[0][r][:, first + a * P : first + (a + 1) * P],
+                        ident[:],
+                        is_transpose=True,
+                        start=(r, a) == (0, 0),
+                        stop=(r, a) == (1, chunks - 1),
+                    )
+            summed = held([P, chunks, P], F32, "summed%d" % first)
+            nc.scalar.copy(out=summed[:], in_=turned[:])
+            back = ybanks.tile([P, chunks, P], F32, name="ybank%d" % banks[1])
+            for a in range(chunks):
+                nc.tensor.transpose(back[:, a, :], summed[:, a, :], ident[:])
+            tokens = slice(first, first + T // 2)
+            nc.scalar.copy(out=res[0][:, tokens], in_=back[:].rearrange("p a t -> p (a t)"))
+            nc.scalar.dma_start(out=out[0:P, tokens], in_=res[0][:, tokens])
+
+        pick(0, 0, 0, T)
+        for first in halves:
+            pick(0, 1, first, T // 2)
+        finish_by_transposes(0, (2, 0))
+        finish_by_transposes(T // 2, (3, 1))
+        pick(1, 0, 0, T)
+        for first in halves:
+            pick(1, 1, first, T // 2)
+        for first in halves:
+            finish(1, first, T // 2)

@@ -20,21 +20,23 @@ FP4X4 = mybir.dt.float4_e2m1fn_x4
 MULT = mybir.AluOpType.mult
 ADD = mybir.AluOpType.add
 
-GATHER = 256
-GATHERS = ((0, 1, 2), (3, 4, 5), (6, 7))
 LAST = E - 1
+ALL_EXPERTS = tuple(range(E))
+GATHERS = ((0, 1, 2), (3, 4, 5), (6, 7))
 VECTOR_PLACES = 84
-WARM_UPS = 2
-WB_PLANE = 0
-BLOCK0_GROUPS = ((0, 1, 2), (3, 4, 5), (6,), (7,))
-BLOCK0_LOADS = ((0, 1, 2, 3), (4, 5, 6, 7))
+WARM_UPS = 3
+WB_PLANE = 4
+
 W_LOADS = ((0, 1, 2), (3, 4, 5), (6, 7))
-BLOCK1_LOADS = ((4, 5, 6, 7), (2, 3), (0, 1))
-BLOCK1_GROUPS = ((4, 5, 6, 7), (2, 3), (0, 1))
-BLOCK0_BANKS = (0, 1, 2, 3)
-BLOCK1_BANKS = (4, 3, 2)
+BLOCK1_LOADS = ((5, 6, 7), (2, 3, 4), (0, 1))
+BLOCK0_GROUPS = ((0, 1, 2), (3, 4, 5), (6,), (7,))
+BLOCK1_GROUPS = ((5, 6, 7), (2, 3, 4), (1,), (0,))
 LATE_H = (0, 3, 5, 6)
-H_PLANES = ((0, 1, 2, 5), (3, 4, 6), (7,))
+
+H_BANKS = (5, 6)
+BLOCK0_BANKS = (0, 1, H_BANKS[LAST % 2], 3)
+BLOCK1_BANKS = (4, BLOCK0_BANKS[2], BLOCK0_BANKS[3], 2)
+SUM_BANKS = ((BLOCK1_BANKS[2], BLOCK0_BANKS[0]), (BLOCK1_BANKS[3], BLOCK0_BANKS[1]))
 
 
 def tile_moe_elr_none_kernel(
@@ -43,14 +45,17 @@ def tile_moe_elr_none_kernel(
     nc = tc.nc
     with ExitStack() as ctx:
         keep = ctx.enter_context(tc.tile_pool(name="keep", bufs=1))
-        ybanks = ctx.enter_context(tc.psum_pool(name="ybanks", bufs=1))
+        psum = ctx.enter_context(tc.psum_pool(name="psum", bufs=1))
 
         def held(shape, dtype, name, tag=None):
             return keep.tile(shape, dtype, name=name, tag=tag or name, align_bytes=64)
 
+        def numbered_bank(number, parts):
+            return psum.tile([P, parts, P], F32, name="bank%d" % number)
+
         tail = ctx.enter_context(tc.tile_pool(name="tail", bufs=1))
         last_load_bytes = 4 * 2 * H
-        rounded_h_bytes = 2 * C * PACK
+        last_grouped_at = last_load_bytes + 4 * S
 
         def placed(shape, dtype, name, offset):
             return tail.tile(shape, dtype, name=name, tag=name, align_bytes=64, offset=offset)
@@ -83,19 +88,17 @@ def tile_moe_elr_none_kernel(
         w_t, wb_t = {}, {}
 
         def load_w(experts):
-            group = held([P, len(experts), 2 * N], U8, "w%d" % experts[0])
-            load(group[:].bitcast(I32), w_view[:, experts[0] : experts[-1] + 1, :].bitcast(I32))
+            piece = held([P, len(experts), 2 * N], U8, "w%d" % experts[0])
+            load(piece[:].bitcast(I32), w_view[:, experts[0] : experts[-1] + 1, :].bitcast(I32))
             for n, e in enumerate(experts):
-                w_t[e] = group[:, n, :]
-
+                w_t[e] = piece[:, n, :]
 
         def load_wb(experts, b):
-            group = held([P, len(experts), 4 * P], U8, "wb%d_%d" % (experts[0], b))
+            piece = held([P, len(experts), 4 * P], U8, "wb%d_%d" % (experts[0], b))
             rows = slice(experts[0], experts[-1] + 1)
-            load(group[:].bitcast(I32), wb_view[:, rows, 4 * b * P : 4 * (b + 1) * P].bitcast(I32))
+            load(piece[:].bitcast(I32), wb_view[:, rows, 4 * b * P : 4 * (b + 1) * P].bitcast(I32))
             for n, e in enumerate(experts):
-                wb_t[e, b] = group[:, n, :]
-
+                wb_t[e, b] = piece[:, n, :]
 
         ident = held([P, P], F32, "ident")
         make_identity(nc, ident[:])
@@ -106,15 +109,13 @@ def tile_moe_elr_none_kernel(
         load(gate_cols[:], gate[:, 0, :].rearrange("r (p a) -> p r a", p=P))
         load_wa(0)
         load_scales(xs, 0, x_scales[0].rearrange("(q r) t -> r q t", r=4))
-        for e in range(1, LAST - 1):
+        for e in range(1, LAST):
             load_wa(e)
-        load_wa(LAST - 1)
         last_raw = [held([P, 2, H], F32, "lastraw0"), placed([P, 2, H], F32, "lastraw1", 0)]
         for half in range(2):
             load(last_raw[half][:], wa_rows[LAST][:, 2 * half : 2 * half + 2, :])
         load_scales(wbs, WB_PLANE, wb_scales.rearrange("e s (q r) n -> r q (e s) n", r=4))
-        for experts in BLOCK0_LOADS:
-            load_wb(experts, 0)
+        load_wb(ALL_EXPERTS, 0)
         load_scales(ws, 0, w_scales.rearrange("e s (q r) n -> r q (e s) n", r=4))
         for experts in W_LOADS:
             load_w(experts)
@@ -125,7 +126,7 @@ def tile_moe_elr_none_kernel(
 
         gate_t = [held([P, T], F32, "gate%d" % r) for r in range(2)]
         for r in range(2):
-            spread = ybanks.tile([P, T // P, P], F32, name="ybank%d" % r)
+            spread = numbered_bank(r, T // P)
             for a in range(T // P):
                 nc.tensor.transpose(spread[:, a, :], gate_cols[:, r, a : a + 1].to_broadcast([P, P]), ident[:])
             nc.scalar.copy(
@@ -167,7 +168,6 @@ def tile_moe_elr_none_kernel(
                 in_=grouped[e][:].rearrange("p t m j -> p (t m j)"),
             )
 
-        last_grouped_at = 2 * last_load_bytes + rounded_h_bytes
         grouped[LAST] = placed([P, PACK, P, PACK], BF16, "grp%d" % LAST, last_grouped_at)
 
         def round_last(half):
@@ -193,13 +193,9 @@ def tile_moe_elr_none_kernel(
             return wa_codes[e][:, t * P : (t + 1) * P], wa_scales[e][:, t * P : (t + 1) * P]
 
         h_bank, h_bf, h_codes, h_scales = {}, {}, {}, {}
-        for experts in H_PLANES:
-            planes = held([P, C], U8, "hs%d" % experts[0])
-            for n, e in enumerate(experts):
-                h_scales[e] = planes[4 * n : P, :]
 
         def first_product(e):
-            h_bank[e] = ybanks.tile([P, PACK, C], F32, name="ybank%d" % (5 + e % 2))
+            h_bank[e] = numbered_bank(H_BANKS[e % 2], PACK)
             for t in range(PACK):
                 codes, scales = stationary_wa(e, t)
                 nc.tensor.matmul_mx(
@@ -215,10 +211,9 @@ def tile_moe_elr_none_kernel(
         def round_h(e):
             if e == LAST - 1:
                 h_bf[e] = placed([P, C, PACK], BF16, "hbf%d" % e, 0)
-            elif e == LAST:
-                h_bf[e] = placed([P, C, PACK], BF16, "hbf%d" % e, last_load_bytes)
             else:
-                h_bf[e] = held([P, C, PACK], BF16, "hbf%d" % e, "raw%d" % (e + 1))
+                reuse = None if e == LAST else "raw%d" % (e + 1)
+                h_bf[e] = held([P, C, PACK], BF16, "hbf%d" % e, reuse)
             nc.scalar.copy(out=h_bf[e][:], in_=h_bank[e][:].rearrange("p t s -> p s t"))
 
         def quantize_h(e):
@@ -226,43 +221,15 @@ def tile_moe_elr_none_kernel(
                 h_codes[e] = placed([P, C], U32, "hc%d" % e, last_grouped_at + 4 * C * LATE_H.index(e))
             else:
                 h_codes[e] = held([P, C], U32, "hc%d" % e)
+            h_scales[e] = held([P, C], U8, "hs%d" % e)
             nc.vector.quantize_mx(
                 out=h_codes[e][:].bitcast(FP8X4),
-                scales=h_scales[e],
+                scales=h_scales[e][:],
                 in_=h_bf[e][:].rearrange("p s t -> p (s t)"),
             )
 
-        y = [placed([P, S], F32, "y0", last_load_bytes + rounded_h_bytes - 64), held([P, S], F32, "y1")]
-
-        def second_pass(bank, place, e, b, frozen, start=False, stop=False):
-            outputs = slice(b * P, (b + 1) * P)
-            if frozen:
-                words, scales = w_t[e][:, 2 * b * P : 2 * (b + 1) * P].bitcast(FP4X4), ws[:, e, outputs]
-                moving, moving_scales = xg_w[e], xg_s[e]
-            else:
-                words, scales = wb_t[e, b].bitcast(FP8X4), wbs[WB_PLANE:P, e, outputs]
-                moving, moving_scales = h_codes[e][:], h_scales[e]
-            nc.tensor.matmul_mx(
-                out=bank[:, place, :],
-                lhsT=words,
-                lhsT_scale=scales,
-                rhs=moving.bitcast(FP8X4),
-                rhs_scale=moving_scales,
-                start=start,
-                stop=stop,
-            )
-
-        def y_bank(experts, bank_number):
-            return ybanks.tile([P, len(experts), C], F32, name="ybank%d" % bank_number)
-
-        def empty_bank(bank, experts, b, engine_copy):
-            engine_copy(
-                out=y[b][:, experts[0] * C : (experts[-1] + 1) * C],
-                in_=bank[:].rearrange("p n s -> p (n s)"),
-            )
-
         def warm_up(e):
-            warm = ybanks.tile([P, 2, GATHER], F32, name="warm")
+            warm = psum.tile([P, 2, len(GATHERS[-1]) * C], F32, name="warm")
             codes, scales = stationary_wa(e, PACK - 1)
             for n in range(WARM_UPS):
                 nc.tensor.matmul_mx(
@@ -280,66 +247,80 @@ def tile_moe_elr_none_kernel(
         round_expert(0)
         quantize_expert(0)
         first_product(0)
-        for e in range(1, LAST - 1):
+        for e in range(1, LAST):
             round_expert(e)
             round_h(e - 1)
             quantize_expert(e)
             if e - 1 not in LATE_H:
                 quantize_h(e - 1)
             first_product(e)
-        warm_up(LAST - 2)
-        round_expert(LAST - 1)
-        round_h(LAST - 2)
-        quantize_expert(LAST - 1)
-        first_product(LAST - 1)
-        warm_up(LAST - 1)
+            if e >= LAST - 2:
+                warm_up(e)
         round_last(0)
         round_last(1)
         quantize_last()
         first_product(LAST)
-        warm_up(LAST)
         round_h(LAST - 1)
         for e in LATE_H:
             quantize_h(e)
         round_h(LAST)
         quantize_h(LAST)
-        banks = [y_bank(experts, number) for experts, number in zip(BLOCK0_GROUPS, BLOCK0_BANKS)]
-        for bank, experts in zip(banks, BLOCK0_GROUPS):
-            for place, e in enumerate(experts):
-                second_pass(bank, place, e, 0, frozen=False, start=place == 0)
-        for n, (bank, experts) in enumerate(zip(banks, BLOCK0_GROUPS)):
-            for place, e in enumerate(experts):
-                second_pass(bank, place, e, 0, frozen=True, stop=e == experts[-1])
-            empty_bank(bank, experts, 0, (nc.scalar.copy, nc.vector.tensor_copy)[n % 2])
-        for experts, number in zip(BLOCK1_GROUPS, BLOCK1_BANKS):
-            bank = y_bank(experts, number)
-            order = [(e, True) for e in experts] + [(e, False) for e in reversed(experts)]
-            if LAST in experts:
-                order.remove((LAST, False))
-                order = [(LAST, False)] + order
-            for k, (e, frozen) in enumerate(order):
-                second_pass(bank, e - experts[0], e, 1, frozen, start=k == 0, stop=k == len(order) - 1)
-            empty_bank(bank, experts, 1, nc.scalar.copy)
 
-        picked = {}
+        y = [placed([P, S], F32, "y0", last_load_bytes - 64), held([P, S], F32, "y1")]
+
+        def frozen_operands(e, b):
+            words = w_t[e][:, 2 * b * P : 2 * (b + 1) * P].bitcast(FP4X4)
+            return words, ws[:, e, b * P : (b + 1) * P], xg_w[e], xg_s[e]
+
+        def adapter_operands(e, b):
+            return wb_t[e, b].bitcast(FP8X4), wbs[WB_PLANE:P, e, b * P : (b + 1) * P], h_codes[e][:], h_scales[e][:]
+
+        def y_passes(bank, experts, b, operands, opening):
+            for place, e in enumerate(experts):
+                words, scales, moving, moving_scales = operands(e, b)
+                nc.tensor.matmul_mx(
+                    out=bank[:, place, :],
+                    lhsT=words,
+                    lhsT_scale=scales,
+                    rhs=moving.bitcast(FP8X4),
+                    rhs_scale=moving_scales,
+                    start=opening and e == experts[0],
+                    stop=not opening and e == experts[-1],
+                )
+
+        def row_block(b, groups, bank_numbers, opening_operands, closing_operands, single_bank_copy):
+            banks = [numbered_bank(number, len(experts)) for experts, number in zip(groups, bank_numbers)]
+            for bank, experts in zip(banks, groups):
+                y_passes(bank, experts, b, opening_operands, True)
+            for bank, experts in zip(banks, groups):
+                y_passes(bank, experts, b, closing_operands, False)
+                engine_copy = nc.scalar.copy if len(experts) > 1 else single_bank_copy
+                engine_copy(
+                    out=y[b][:, experts[0] * C : (experts[-1] + 1) * C],
+                    in_=bank[:].rearrange("p n s -> p (n s)"),
+                )
+
+        row_block(0, BLOCK0_GROUPS, BLOCK0_BANKS, adapter_operands, frozen_operands, nc.vector.tensor_copy)
+        row_block(1, BLOCK1_GROUPS, BLOCK1_BANKS, frozen_operands, adapter_operands, nc.scalar.copy)
+
         res = [held([P, T], F32, "res%d" % b) for b in range(2)]
+        picked = [[held([P, T], F32, "pick%d_%d" % (b, r)) for r in range(2)] for b in range(2)]
+        half_tokens = T // 2
+        halves = (0, half_tokens)
 
         def pick(b, r, first, count):
             tokens = slice(first, first + count)
             entries = pos_t[r][:, first // 16 : (first + count) // 16]
             nc.vector.tensor_tensor(picked[b][r][:, tokens], y[b][:].indirect(entries), gate_t[r][:, tokens], MULT)
 
-        def finish(b, first, count):
-            tokens = slice(first, first + count)
-            nc.vector.tensor_tensor(res[b][:, tokens], picked[b][0][:, tokens], picked[b][1][:, tokens], ADD)
-            nc.sync.dma_start(out=out[b * P : (b + 1) * P, tokens], in_=res[b][:, tokens])
+        def pick_row_block(b):
+            pick(b, 0, 0, T)
+            for first in halves:
+                pick(b, 1, first, half_tokens)
 
-        halves = (0, T // 2)
-        for b in range(2):
-            picked[b] = [held([P, T], F32, "pick%d_%d" % (b, r)) for r in range(2)]
-        def finish_by_transposes(first, banks):
-            chunks = T // 2 // P
-            turned = ybanks.tile([P, chunks, P], F32, name="ybank%d" % banks[0])
+        def sum_by_transposes(first, sum_bank, back_bank):
+            chunks = half_tokens // P
+            turned = numbered_bank(sum_bank, chunks)
             for r in range(2):
                 for a in range(chunks):
                     nc.tensor.matmul(
@@ -352,20 +333,18 @@ def tile_moe_elr_none_kernel(
                     )
             summed = held([P, chunks, P], F32, "summed%d" % first)
             nc.scalar.copy(out=summed[:], in_=turned[:])
-            back = ybanks.tile([P, chunks, P], F32, name="ybank%d" % banks[1])
+            back = numbered_bank(back_bank, chunks)
             for a in range(chunks):
                 nc.tensor.transpose(back[:, a, :], summed[:, a, :], ident[:])
-            tokens = slice(first, first + T // 2)
+            tokens = slice(first, first + half_tokens)
             nc.scalar.copy(out=res[0][:, tokens], in_=back[:].rearrange("p a t -> p (a t)"))
             nc.scalar.dma_start(out=out[0:P, tokens], in_=res[0][:, tokens])
 
-        pick(0, 0, 0, T)
+        pick_row_block(0)
+        for first, (sum_bank, back_bank) in zip(halves, SUM_BANKS):
+            sum_by_transposes(first, sum_bank, back_bank)
+        pick_row_block(1)
         for first in halves:
-            pick(0, 1, first, T // 2)
-        finish_by_transposes(0, (2, 0))
-        finish_by_transposes(T // 2, (3, 1))
-        pick(1, 0, 0, T)
-        for first in halves:
-            pick(1, 1, first, T // 2)
-        for first in halves:
-            finish(1, first, T // 2)
+            tokens = slice(first, first + half_tokens)
+            nc.vector.tensor_tensor(res[1][:, tokens], picked[1][0][:, tokens], picked[1][1][:, tokens], ADD)
+            nc.sync.dma_start(out=out[P:N, tokens], in_=res[1][:, tokens])

@@ -23,20 +23,23 @@ ADD = mybir.AluOpType.add
 LAST = E - 1
 ALL_EXPERTS = tuple(range(E))
 GATHERS = ((0, 1, 2), (3, 4, 5), (6, 7))
-VECTOR_PLACES = 84
+LAST_PLACES = (60, 84)
+GATE_BEHIND = 2
+STREAM_PLACES = (0, 44, 80, 80, 80, 80, 84)
 WARM_UPS = 3
 WB_PLANE = 4
 
-W_LOADS = ((0, 1, 2), (3, 4, 5), (6, 7))
+BLOCK0_LOADS = ((0, 1, 2, 3), (4, 5, 6, 7))
+
 BLOCK1_LOADS = ((5, 6, 7), (2, 3, 4), (0, 1))
 BLOCK0_GROUPS = ((0, 1, 2), (3, 4, 5), (6,), (7,))
 BLOCK1_GROUPS = ((5, 6, 7), (2, 3, 4), (1,), (0,))
-LATE_H = (0, 3, 5, 6)
+LATE_H = (3, 5, 6)
 
 H_BANKS = (5, 6)
-BLOCK0_BANKS = (0, 1, H_BANKS[LAST % 2], 3)
-BLOCK1_BANKS = (4, BLOCK0_BANKS[2], BLOCK0_BANKS[3], 2)
-SUM_BANKS = ((BLOCK1_BANKS[2], BLOCK0_BANKS[0]), (BLOCK1_BANKS[3], BLOCK0_BANKS[1]))
+BLOCK0_BANKS = (0, 1, 4, 3)
+BLOCK1_BANKS = (BLOCK0_BANKS[0], BLOCK0_BANKS[1], BLOCK0_BANKS[2], BLOCK0_BANKS[3])
+SUM_BANKS = ((BLOCK1_BANKS[2], 2), (BLOCK1_BANKS[3], H_BANKS[LAST % 2]))
 
 
 def tile_moe_elr_none_kernel(
@@ -57,41 +60,49 @@ def tile_moe_elr_none_kernel(
         last_load_bytes = 4 * 2 * H
         last_grouped_at = last_load_bytes + 4 * S
 
+        stream = ctx.enter_context(tc.tile_pool(name="stream", bufs=1))
+
+        def on_raw(shape, dtype, name, e, offset):
+            return stream.tile(shape, dtype, name=name, align_bytes=64, offset=4 * PACK * H * e + offset)
+
         def placed(shape, dtype, name, offset):
             return tail.tile(shape, dtype, name=name, tag=name, align_bytes=64, offset=offset)
 
         def load(tile_view, dram_view):
             nc.sync.dma_start(out=tile_view, in_=dram_view)
 
+        gate_cols = held([P, 2, T // P], F32, "gate_cols")
         offs_t = held([P, S // 16], U16, "offs_t")
         pos_t = [held([P, T // 16], U16, "pos_t%d" % r) for r in range(2)]
         xw = held([P, T], U32, "xw")
         xs = held([P, T], U8, "xs")
-        ws = held([P, E, N], U8, "ws")
-        wbs = held([P, E, N], U8, "wbs")
-        for scale_tile in (xs, ws, wbs):
+        ws = held([P, E * N], U8, "ws")
+        wbs = held([P, E // PACK, N], U8, "wbs")
+        nc.gpsimd.memset(xs[:].bitcast(I32), 0)
+        for scale_tile in (wbs, ws):
             nc.vector.memset(scale_tile[:].bitcast(I32), 0)
 
-        def load_scales(scale_tile, first, rows):
+        def load_scales(scale_tile, first, rows, load=load):
             for r in range(4):
-                load(scale_tile[:].bitcast(I32)[first + r : P : 32], rows[r].bitcast(I32))
+                load(scale_tile.bitcast(I32)[first + r : P : 32], rows[r].bitcast(I32))
 
         wa_rows = wa.rearrange("e (p j) i -> e p j i", j=PACK)
         raw = {}
 
         def load_wa(e):
-            raw[e] = held([P, PACK, H], F32, "raw%d" % e)
+            raw[e] = stream.tile([P, PACK, H], F32, name="raw%d" % e, align_bytes=64, offset=4 * PACK * H * e)
             load(raw[e][:], wa_rows[e])
 
         w_view = w_words.rearrange("e s p c -> p (e s) c")
         wb_view = wb_words.rearrange("e s p n d -> p (e s) (n d)")
         w_t, wb_t = {}, {}
 
-        def load_w(experts):
-            piece = held([P, len(experts), 2 * N], U8, "w%d" % experts[0])
-            load(piece[:].bitcast(I32), w_view[:, experts[0] : experts[-1] + 1, :].bitcast(I32))
+        def load_w(experts, b):
+            piece = held([P, len(experts), 2 * P], U8, "w%d_%d" % (experts[0], b))
+            rows = slice(experts[0], experts[-1] + 1)
+            load(piece[:].bitcast(I32), w_view[:, rows, 2 * b * P : 2 * (b + 1) * P].bitcast(I32))
             for n, e in enumerate(experts):
-                w_t[e] = piece[:, n, :]
+                w_t[e, b] = piece[:, n, :]
 
         def load_wb(experts, b):
             piece = held([P, len(experts), 4 * P], U8, "wb%d_%d" % (experts[0], b))
@@ -100,38 +111,49 @@ def tile_moe_elr_none_kernel(
             for n, e in enumerate(experts):
                 wb_t[e, b] = piece[:, n, :]
 
+        load_scales(xs[:], 0, x_scales[0].rearrange("(q r) t -> r q t", r=4), nc.gpsimd.dma_start)
         ident = held([P, P], F32, "ident")
         make_identity(nc, ident[:])
-        gate_cols = held([P, 2, T // P], F32, "gate_cols")
+        for g in range(E // PACK):
+            for q in range(4):
+                nc.gpsimd.dma_start(
+                    out=wbs[:].bitcast(I32)[32 * q : 32 * q + 16, g, :],
+                    in_=wb_scales[PACK * g : PACK * (g + 1), 0, 4 * q : 4 * q + 4, :].bitcast(I32),
+                )
 
         load(xw[:].bitcast(I32), x_words[0].rearrange("p t d -> p (t d)").bitcast(I32))
         load(offs_t[:], offs)
         load(gate_cols[:], gate[:, 0, :].rearrange("r (p a) -> p r a", p=P))
         load_wa(0)
-        load_scales(xs, 0, x_scales[0].rearrange("(q r) t -> r q t", r=4))
         for e in range(1, LAST):
             load_wa(e)
         last_raw = [held([P, 2, H], F32, "lastraw0"), placed([P, 2, H], F32, "lastraw1", 0)]
         for half in range(2):
             load(last_raw[half][:], wa_rows[LAST][:, 2 * half : 2 * half + 2, :])
-        load_scales(wbs, WB_PLANE, wb_scales.rearrange("e s (q r) n -> r q (e s) n", r=4))
-        load_wb(ALL_EXPERTS, 0)
-        load_scales(ws, 0, w_scales.rearrange("e s (q r) n -> r q (e s) n", r=4))
-        for experts in W_LOADS:
-            load_w(experts)
+        load_scales(ws[:].rearrange("p (e n) -> p e n", e=E), 0, w_scales.rearrange("e s (q r) n -> r q (e s) n", r=4))
+        load_w(ALL_EXPERTS, 0)
+        for experts in BLOCK0_LOADS:
+            load_wb(experts, 0)
         load(pos_t[0][:], pos1)
-        load(pos_t[1][:], pos2)
-        for experts in BLOCK1_LOADS:
+        load_w(ALL_EXPERTS, 1)
+        for experts in BLOCK1_LOADS[:-1]:
             load_wb(experts, 1)
+        load(pos_t[1][:], pos2)
+        load_wb(BLOCK1_LOADS[-1], 1)
 
-        gate_t = [held([P, T], F32, "gate%d" % r) for r in range(2)]
+        gate_t, spread = {}, {}
         for r in range(2):
-            spread = numbered_bank(r, T // P)
+            spread[r] = numbered_bank(r, T // P)
             for a in range(T // P):
-                nc.tensor.transpose(spread[:, a, :], gate_cols[:, r, a : a + 1].to_broadcast([P, P]), ident[:])
+                nc.tensor.transpose(spread[r][:, a, :], gate_cols[:, r, a : a + 1].to_broadcast([P, P]), ident[:])
+
+        def keep_gate(r):
+            gate_t[r] = on_raw([P, T], F32, "gate1", GATE_BEHIND, 2 * PACK * C) if r else held([P, T], F32, "gate0")
             nc.scalar.copy(
-                out=gate_t[r][:].rearrange("q (p a) -> q p a", p=P), in_=spread[:].rearrange("q a p -> q p a")
+                out=gate_t[r][:].rearrange("q (p a) -> q p a", p=P), in_=spread[r][:].rearrange("q a p -> q p a")
             )
+
+        keep_gate(0)
 
         xg_w, xg_s, last_gathered = {}, {}, {}
 
@@ -155,8 +177,11 @@ def tile_moe_elr_none_kernel(
         grouped = {}
 
         def round_expert(e):
-            grouped[e] = held([P, PACK, P, PACK], BF16, "grp%d" % e)
-            cut = VECTOR_PLACES if e else 0
+            if e:
+                grouped[e] = on_raw([P, PACK, P, PACK], BF16, "grp%d" % e, e - 1, 8 * PACK * C)
+            else:
+                grouped[e] = held([P, PACK, P, PACK], BF16, "grp0", "gate_cols")
+            cut = STREAM_PLACES[e]
             if cut:
                 round_wa(nc.vector.tensor_copy, grouped[e][:, :, 0:cut, :], raw[e][:, :, 0 : PACK * cut])
             round_wa(nc.scalar.copy, grouped[e][:, :, cut:P, :], raw[e][:, :, PACK * cut : H])
@@ -171,31 +196,32 @@ def tile_moe_elr_none_kernel(
         grouped[LAST] = placed([P, PACK, P, PACK], BF16, "grp%d" % LAST, last_grouped_at)
 
         def round_last(half):
-            cut = VECTOR_PLACES
+            cut = LAST_PLACES[half]
             rounded, source = grouped[LAST][:, :, :, 2 * half : 2 * half + 2], last_raw[half]
             round_wa(nc.vector.tensor_copy, rounded[:, :, 0:cut, :], source[:, :, 0 : PACK * cut])
             round_wa(nc.scalar.copy, rounded[:, :, cut:P, :], source[:, :, PACK * cut : H])
 
-        last_codes = [held([P, P], U32, "lc%d" % t) for t in range(PACK)]
-        last_scales = [held([P, P], U8, "ls%d" % t) for t in range(PACK)]
+        last_codes = [held([P, P], U32, "lc%d" % t) for t in range(PACK - 1)]
+        last_codes.append(placed([P, P], U32, "lc3", last_grouped_at + 2 * PACK * H))
+        last_scales = [held([P, P], U8, "ls%d" % t)[:] for t in range(PACK - 1)] + [ws[4:P, 0:P]]
 
         def quantize_last():
             for t in range(PACK):
                 nc.vector.quantize_mx(
                     out=last_codes[t][:].bitcast(FP8X4),
-                    scales=last_scales[t][:],
+                    scales=last_scales[t],
                     in_=grouped[LAST][:, t].rearrange("p m j -> p (m j)"),
                 )
 
         def stationary_wa(e, t):
             if e == LAST:
-                return last_codes[t][:], last_scales[t][:]
+                return last_codes[t][:], last_scales[t]
             return wa_codes[e][:, t * P : (t + 1) * P], wa_scales[e][:, t * P : (t + 1) * P]
 
         h_bank, h_bf, h_codes, h_scales = {}, {}, {}, {}
 
         def first_product(e):
-            h_bank[e] = numbered_bank(H_BANKS[e % 2], PACK)
+            h_bank[e] = numbered_bank(H_BANKS[e % 2] if e < LAST else 4, PACK)
             for t in range(PACK):
                 codes, scales = stationary_wa(e, t)
                 nc.tensor.matmul_mx(
@@ -209,18 +235,19 @@ def tile_moe_elr_none_kernel(
                 )
 
         def round_h(e):
-            if e == LAST - 1:
-                h_bf[e] = placed([P, C, PACK], BF16, "hbf%d" % e, 0)
+            if e in (LAST - 2, LAST - 1):
+                h_bf[e] = placed([P, C, PACK], BF16, "hbf%d" % e, 2 * PACK * C * (LAST - 1 - e))
+            elif e == LAST:
+                h_bf[e] = held([P, C, PACK], BF16, "hbf%d" % e)
             else:
-                reuse = None if e == LAST else "raw%d" % (e + 1)
-                h_bf[e] = held([P, C, PACK], BF16, "hbf%d" % e, reuse)
+                h_bf[e] = on_raw([P, C, PACK], BF16, "hbf%d" % e, e + 1, 0)
             nc.scalar.copy(out=h_bf[e][:], in_=h_bank[e][:].rearrange("p t s -> p s t"))
 
         def quantize_h(e):
             if e in LATE_H:
                 h_codes[e] = placed([P, C], U32, "hc%d" % e, last_grouped_at + 4 * C * LATE_H.index(e))
             else:
-                h_codes[e] = held([P, C], U32, "hc%d" % e)
+                h_codes[e] = on_raw([P, C], U32, "hc%d" % e, e + 2, 6 * PACK * C) if e < 3 else held([P, C], U32, "hc%d" % e)
             h_scales[e] = held([P, C], U8, "hs%d" % e)
             nc.vector.quantize_mx(
                 out=h_codes[e][:].bitcast(FP8X4),
@@ -228,19 +255,18 @@ def tile_moe_elr_none_kernel(
                 in_=h_bf[e][:].rearrange("p s t -> p (s t)"),
             )
 
-        def warm_up(e):
-            warm = psum.tile([P, 2, len(GATHERS[-1]) * C], F32, name="warm")
-            codes, scales = stationary_wa(e, PACK - 1)
-            for n in range(WARM_UPS):
-                nc.tensor.matmul_mx(
-                    out=warm[:, n % 2, :],
-                    lhsT=codes.bitcast(FP8X4),
-                    lhsT_scale=scales,
-                    rhs=last_gathered["xgw"][:].bitcast(FP8X4),
-                    rhs_scale=last_gathered["xgs"][:],
-                    start=True,
-                    stop=True,
-                )
+        warm = psum.tile([P, H], F32, name="warm")
+
+        def warm_up(e, plane):
+            nc.tensor.matmul_mx(
+                out=warm[:],
+                lhsT=xg_w[e].bitcast(FP8X4),
+                lhsT_scale=plane,
+                rhs=wa_codes[e][:].bitcast(FP8X4),
+                rhs_scale=wa_scales[e][:],
+                start=True,
+                stop=True,
+            )
 
         gather_tokens(xw, U32, "xgw", xg_w)
         gather_tokens(xs, U8, "xgs", xg_s)
@@ -249,59 +275,83 @@ def tile_moe_elr_none_kernel(
         first_product(0)
         for e in range(1, LAST):
             round_expert(e)
-            round_h(e - 1)
+            if e >= 2 and e - 2 not in LATE_H:
+                quantize_h(e - 2)
+            if e < LAST - 1:
+                round_h(e - 1)
+            if e == GATE_BEHIND:
+                keep_gate(1)
             quantize_expert(e)
-            if e - 1 not in LATE_H:
-                quantize_h(e - 1)
             first_product(e)
             if e >= LAST - 2:
-                warm_up(e)
+                for n in range(2):
+                    warm_up(e, xg_s[e])
         round_last(0)
         round_last(1)
         quantize_last()
         first_product(LAST)
+        round_h(LAST - 2)
         round_h(LAST - 1)
         for e in LATE_H:
             quantize_h(e)
         round_h(LAST)
         quantize_h(LAST)
 
-        y = [placed([P, S], F32, "y0", last_load_bytes - 64), held([P, S], F32, "y1")]
+        y = [placed([P, S], F32, "y0", last_grouped_at + 2 * PACK * H + 4 * P - 64), held([P, S], F32, "y1")]
 
         def frozen_operands(e, b):
-            words = w_t[e][:, 2 * b * P : 2 * (b + 1) * P].bitcast(FP4X4)
-            return words, ws[:, e, b * P : (b + 1) * P], xg_w[e], xg_s[e]
+            return w_t[e, b].bitcast(FP4X4), ws[:, e * N + b * P : e * N + (b + 1) * P], xg_w[e], xg_s[e]
 
         def adapter_operands(e, b):
-            return wb_t[e, b].bitcast(FP8X4), wbs[WB_PLANE:P, e, b * P : (b + 1) * P], h_codes[e][:], h_scales[e][:]
+            return wb_t[e, b].bitcast(FP8X4), wbs[4 * (e % PACK) : P, e // PACK, b * P : (b + 1) * P], h_codes[e][:], h_scales[e][:]
 
-        def y_passes(bank, experts, b, operands, opening):
-            for place, e in enumerate(experts):
+        def y_passes(bank, experts, b, passes, opens=False, closes=False):
+            for n, (operands, e) in enumerate(passes):
                 words, scales, moving, moving_scales = operands(e, b)
                 nc.tensor.matmul_mx(
-                    out=bank[:, place, :],
+                    out=bank[:, e - experts[0], :],
                     lhsT=words,
                     lhsT_scale=scales,
                     rhs=moving.bitcast(FP8X4),
                     rhs_scale=moving_scales,
-                    start=opening and e == experts[0],
-                    stop=not opening and e == experts[-1],
+                    start=opens and n == 0,
+                    stop=closes and n == len(passes) - 1,
                 )
 
-        def row_block(b, groups, bank_numbers, opening_operands, closing_operands, single_bank_copy):
-            banks = [numbered_bank(number, len(experts)) for experts, number in zip(groups, bank_numbers)]
-            for bank, experts in zip(banks, groups):
-                y_passes(bank, experts, b, opening_operands, True)
-            for bank, experts in zip(banks, groups):
-                y_passes(bank, experts, b, closing_operands, False)
-                engine_copy = nc.scalar.copy if len(experts) > 1 else single_bank_copy
-                engine_copy(
-                    out=y[b][:, experts[0] * C : (experts[-1] + 1) * C],
-                    in_=bank[:].rearrange("p n s -> p (n s)"),
-                )
+        def frozen(experts):
+            return [(frozen_operands, e) for e in experts]
 
-        row_block(0, BLOCK0_GROUPS, BLOCK0_BANKS, adapter_operands, frozen_operands, nc.vector.tensor_copy)
-        row_block(1, BLOCK1_GROUPS, BLOCK1_BANKS, frozen_operands, adapter_operands, nc.scalar.copy)
+        def adapter(experts):
+            return [(adapter_operands, e) for e in experts]
+
+        def empty(engine_copy, bank, experts, b):
+            engine_copy(
+                out=y[b][:, experts[0] * C : (experts[-1] + 1) * C],
+                in_=bank[:].rearrange("p n s -> p (n s)"),
+            )
+
+        def banks_of(groups, bank_numbers):
+            return [numbered_bank(number, len(experts)) for experts, number in zip(groups, bank_numbers)]
+
+        banks = banks_of(BLOCK0_GROUPS, BLOCK0_BANKS)
+        wide0, wide1, single0, single1 = BLOCK0_GROUPS
+        y_passes(banks[0], wide0, 0, frozen(wide0) + adapter(wide0), True, True)
+        empty(nc.scalar.copy, banks[0], wide0, 0)
+        y_passes(banks[1], wide1, 0, adapter(wide1[:1]) + frozen(wide1) + adapter(wide1[1:]), True, True)
+        empty(nc.scalar.copy, banks[1], wide1, 0)
+        y_passes(banks[2], single0, 0, adapter(single0) + frozen(single0), True, True)
+        empty(nc.vector.tensor_copy, banks[2], single0, 0)
+        y_passes(banks[3], single1, 0, adapter(single1) + frozen(single1), True, True)
+        empty(nc.vector.tensor_copy, banks[3], single1, 0)
+        banks = banks_of(BLOCK1_GROUPS, BLOCK1_BANKS)
+        for bank, experts in zip(banks[1:], BLOCK1_GROUPS[1:]):
+            y_passes(bank, experts, 1, frozen(experts), opens=True)
+        for bank, experts in zip(banks, BLOCK1_GROUPS):
+            if LAST in experts:
+                y_passes(bank, experts, 1, adapter(experts[::-1]) + frozen(experts), True, True)
+            else:
+                y_passes(bank, experts, 1, adapter(experts), closes=True)
+            empty(nc.scalar.copy, bank, experts, 1)
 
         res = [held([P, T], F32, "res%d" % b) for b in range(2)]
         picked = [[held([P, T], F32, "pick%d_%d" % (b, r)) for r in range(2)] for b in range(2)]

@@ -24,8 +24,8 @@ LAST = E - 1
 ALL_EXPERTS = tuple(range(E))
 GATHERS = ((0, 1, 2), (3, 4, 5), (6, 7))
 LAST_PLACES = (60, 84)
-GATE_BEHIND = 2
-STREAM_PLACES = (0, 44, 80, 80, 80, 80, 84)
+GATE_BEHIND = (2, 4)
+STREAM_PLACES = (0, 56, 84, 84, 84, 84, 84)
 WARM_UPS = 3
 WB_PLANE = 4
 
@@ -57,7 +57,7 @@ def tile_moe_elr_none_kernel(
             return psum.tile([P, parts, P], F32, name="bank%d" % number)
 
         tail = ctx.enter_context(tc.tile_pool(name="tail", bufs=1))
-        last_load_bytes = 4 * 2 * H
+        last_load_bytes = 4 * PACK * H
         last_grouped_at = last_load_bytes + 4 * S
 
         stream = ctx.enter_context(tc.tile_pool(name="stream", bufs=1))
@@ -78,11 +78,11 @@ def tile_moe_elr_none_kernel(
         xs = held([P, T], U8, "xs")
         ws = held([P, E * N], U8, "ws")
         wbs = held([P, E // PACK, N], U8, "wbs")
-        nc.gpsimd.memset(xs[:].bitcast(I32), 0)
-        for scale_tile in (wbs, ws):
+        nc.gpsimd.dma_start(gate_cols[:], gate[:, 0, :].rearrange("r (p a) -> p r a", p=P))
+        for scale_tile in (xs, wbs, ws):
             nc.vector.memset(scale_tile[:].bitcast(I32), 0)
 
-        def load_scales(scale_tile, first, rows, load=load):
+        def load_scales(scale_tile, first, rows):
             for r in range(4):
                 load(scale_tile.bitcast(I32)[first + r : P : 32], rows[r].bitcast(I32))
 
@@ -111,7 +111,6 @@ def tile_moe_elr_none_kernel(
             for n, e in enumerate(experts):
                 wb_t[e, b] = piece[:, n, :]
 
-        load_scales(xs[:], 0, x_scales[0].rearrange("(q r) t -> r q t", r=4), nc.gpsimd.dma_start)
         ident = held([P, P], F32, "ident")
         make_identity(nc, ident[:])
         for g in range(E // PACK):
@@ -123,13 +122,12 @@ def tile_moe_elr_none_kernel(
 
         load(xw[:].bitcast(I32), x_words[0].rearrange("p t d -> p (t d)").bitcast(I32))
         load(offs_t[:], offs)
-        load(gate_cols[:], gate[:, 0, :].rearrange("r (p a) -> p r a", p=P))
         load_wa(0)
+        load_scales(xs[:], 0, x_scales[0].rearrange("(q r) t -> r q t", r=4))
         for e in range(1, LAST):
             load_wa(e)
-        last_raw = [held([P, 2, H], F32, "lastraw0"), placed([P, 2, H], F32, "lastraw1", 0)]
-        for half in range(2):
-            load(last_raw[half][:], wa_rows[LAST][:, 2 * half : 2 * half + 2, :])
+        last_raw = placed([P, PACK, H], F32, "lastraw", 0)
+        load(last_raw[:], wa_rows[LAST])
         load_scales(ws[:].rearrange("p (e n) -> p e n", e=E), 0, w_scales.rearrange("e s (q r) n -> r q (e s) n", r=4))
         load_w(ALL_EXPERTS, 0)
         for experts in BLOCK0_LOADS:
@@ -148,12 +146,10 @@ def tile_moe_elr_none_kernel(
                 nc.tensor.transpose(spread[r][:, a, :], gate_cols[:, r, a : a + 1].to_broadcast([P, P]), ident[:])
 
         def keep_gate(r):
-            gate_t[r] = on_raw([P, T], F32, "gate1", GATE_BEHIND, 2 * PACK * C) if r else held([P, T], F32, "gate0")
+            gate_t[r] = on_raw([P, T], F32, "gate%d" % r, GATE_BEHIND[r], 2 * PACK * C)
             nc.scalar.copy(
                 out=gate_t[r][:].rearrange("q (p a) -> q p a", p=P), in_=spread[r][:].rearrange("q a p -> q p a")
             )
-
-        keep_gate(0)
 
         xg_w, xg_s, last_gathered = {}, {}, {}
 
@@ -180,7 +176,7 @@ def tile_moe_elr_none_kernel(
             if e:
                 grouped[e] = on_raw([P, PACK, P, PACK], BF16, "grp%d" % e, e - 1, 8 * PACK * C)
             else:
-                grouped[e] = held([P, PACK, P, PACK], BF16, "grp0", "gate_cols")
+                grouped[e] = held([P, PACK, P, PACK], BF16, "grp0")
             cut = STREAM_PLACES[e]
             if cut:
                 round_wa(nc.vector.tensor_copy, grouped[e][:, :, 0:cut, :], raw[e][:, :, 0 : PACK * cut])
@@ -195,9 +191,9 @@ def tile_moe_elr_none_kernel(
 
         grouped[LAST] = placed([P, PACK, P, PACK], BF16, "grp%d" % LAST, last_grouped_at)
 
-        def round_last(half):
-            cut = LAST_PLACES[half]
-            rounded, source = grouped[LAST][:, :, :, 2 * half : 2 * half + 2], last_raw[half]
+        def round_last():
+            cut = STREAM_PLACES[-1]
+            rounded, source = grouped[LAST], last_raw
             round_wa(nc.vector.tensor_copy, rounded[:, :, 0:cut, :], source[:, :, 0 : PACK * cut])
             round_wa(nc.scalar.copy, rounded[:, :, cut:P, :], source[:, :, PACK * cut : H])
 
@@ -235,7 +231,7 @@ def tile_moe_elr_none_kernel(
                 )
 
         def round_h(e):
-            if e in (LAST - 2, LAST - 1):
+            if e == LAST - 1:
                 h_bf[e] = placed([P, C, PACK], BF16, "hbf%d" % e, 2 * PACK * C * (LAST - 1 - e))
             elif e == LAST:
                 h_bf[e] = held([P, C, PACK], BF16, "hbf%d" % e)
@@ -277,20 +273,17 @@ def tile_moe_elr_none_kernel(
             round_expert(e)
             if e >= 2 and e - 2 not in LATE_H:
                 quantize_h(e - 2)
-            if e < LAST - 1:
-                round_h(e - 1)
-            if e == GATE_BEHIND:
-                keep_gate(1)
+            round_h(e - 1)
+            if e in GATE_BEHIND:
+                keep_gate(GATE_BEHIND.index(e))
             quantize_expert(e)
             first_product(e)
             if e >= LAST - 2:
                 for n in range(2):
                     warm_up(e, xg_s[e])
-        round_last(0)
-        round_last(1)
+        round_last()
         quantize_last()
         first_product(LAST)
-        round_h(LAST - 2)
         round_h(LAST - 1)
         for e in LATE_H:
             quantize_h(e)

@@ -19,27 +19,28 @@ FP8X4 = mybir.dt.float8_e4m3fn_x4
 FP4X4 = mybir.dt.float4_e2m1fn_x4
 MULT = mybir.AluOpType.mult
 ADD = mybir.AluOpType.add
+COPY = mybir.ActivationFunctionType.Copy
 
 LAST = E - 1
 ALL_EXPERTS = tuple(range(E))
 GATHERS = ((0, 1, 2), (3, 4, 5), (6, 7))
-LAST_PLACES = (60, 84)
+LAST_PLACES = (32, 44)
 GATE_BEHIND = (2, 4)
 STREAM_PLACES = (0, 56, 84, 84, 84, 84, 84)
 WARM_UPS = 3
 WB_PLANE = 4
 
 BLOCK0_LOADS = ((0, 1, 2, 3), (4, 5, 6, 7))
-
 BLOCK1_LOADS = ((5, 6, 7), (2, 3, 4), (0, 1))
-BLOCK0_GROUPS = ((0, 1, 2), (3, 4, 5), (6,), (7,))
-BLOCK1_GROUPS = ((5, 6, 7), (2, 3, 4), (1,), (0,))
-LATE_H = (3, 5, 6)
+BLOCK0_GROUPS = ((0, 1, 2, 3), (4, 5, 6), (7,))
+BLOCK1_GROUPS = BLOCK1_LOADS
+LATE_H = (5, 6)
+ORDER = (1, 2, 3, 4, 5, 0, 6, 7)
+WARM_UP_COLUMNS = (512, 256)
 
 H_BANKS = (5, 6)
-BLOCK0_BANKS = (0, 1, 4, 3)
-BLOCK1_BANKS = (BLOCK0_BANKS[0], BLOCK0_BANKS[1], BLOCK0_BANKS[2], BLOCK0_BANKS[3])
-SUM_BANKS = ((BLOCK1_BANKS[2], 2), (BLOCK1_BANKS[3], H_BANKS[LAST % 2]))
+BLOCK0_BANKS = (0, 1, 2)
+BLOCK1_BANKS = (1, 0, 4)
 
 
 def tile_moe_elr_none_kernel(
@@ -91,7 +92,7 @@ def tile_moe_elr_none_kernel(
 
         def load_wa(e):
             raw[e] = stream.tile([P, PACK, H], F32, name="raw%d" % e, align_bytes=64, offset=4 * PACK * H * e)
-            load(raw[e][:], wa_rows[e])
+            load(raw[e][:], wa_rows[ORDER[e]])
 
         w_view = w_words.rearrange("e s p c -> p (e s) c")
         wb_view = wb_words.rearrange("e s p n d -> p (e s) (n d)")
@@ -126,18 +127,18 @@ def tile_moe_elr_none_kernel(
         load_scales(xs[:], 0, x_scales[0].rearrange("(q r) t -> r q t", r=4))
         for e in range(1, LAST):
             load_wa(e)
-        last_raw = placed([P, PACK, H], F32, "lastraw", 0)
-        load(last_raw[:], wa_rows[LAST])
+        last_raw = [placed([P, PACK, H // 2], F32, "lastraw%d" % u, u * last_load_bytes // 2) for u in range(2)]
+        for u in range(2):
+            load(last_raw[u][:], wa_rows[LAST][:, :, u * H // 2 : (u + 1) * H // 2])
+        load_wb(ALL_EXPERTS, 0)
         load_scales(ws[:].rearrange("p (e n) -> p e n", e=E), 0, w_scales.rearrange("e s (q r) n -> r q (e s) n", r=4))
-        load_w(ALL_EXPERTS, 0)
         for experts in BLOCK0_LOADS:
-            load_wb(experts, 0)
-        load(pos_t[0][:], pos1)
+            load_w(experts, 0)
         load_w(ALL_EXPERTS, 1)
-        for experts in BLOCK1_LOADS[:-1]:
-            load_wb(experts, 1)
         load(pos_t[1][:], pos2)
-        load_wb(BLOCK1_LOADS[-1], 1)
+        load(pos_t[0][:], pos1)
+        for experts in BLOCK1_LOADS:
+            load_wb(experts, 1)
 
         gate_t, spread = {}, {}
         for r in range(2):
@@ -191,15 +192,14 @@ def tile_moe_elr_none_kernel(
 
         grouped[LAST] = placed([P, PACK, P, PACK], BF16, "grp%d" % LAST, last_grouped_at)
 
-        def round_last():
-            cut = STREAM_PLACES[-1]
-            rounded, source = grouped[LAST], last_raw
-            round_wa(nc.vector.tensor_copy, rounded[:, :, 0:cut, :], source[:, :, 0 : PACK * cut])
-            round_wa(nc.scalar.copy, rounded[:, :, cut:P, :], source[:, :, PACK * cut : H])
+        def round_last(u):
+            first, cut, end = u * P // 2, LAST_PLACES[u], P // 2
+            rounded, source = grouped[LAST], last_raw[u]
+            round_wa(nc.vector.tensor_copy, rounded[:, :, first : first + cut, :], source[:, :, 0 : PACK * cut])
+            round_wa(nc.scalar.copy, rounded[:, :, first + cut : first + end, :], source[:, :, PACK * cut : H // 2])
 
-        last_codes = [held([P, P], U32, "lc%d" % t) for t in range(PACK - 1)]
-        last_codes.append(placed([P, P], U32, "lc3", last_grouped_at + 2 * PACK * H))
-        last_scales = [held([P, P], U8, "ls%d" % t)[:] for t in range(PACK - 1)] + [ws[4:P, 0:P]]
+        last_codes = [placed([P, P], U32, "lc%d" % t, last_load_bytes - 4 * P * (PACK - t)) for t in range(PACK)]
+        last_scales = [held([P, P], U8, "ls%d" % t)[:] for t in range(PACK)]
 
         def quantize_last():
             for t in range(PACK):
@@ -224,15 +224,15 @@ def tile_moe_elr_none_kernel(
                     out=h_bank[e][:, t, :],
                     lhsT=codes.bitcast(FP8X4),
                     lhsT_scale=scales,
-                    rhs=xg_w[e].bitcast(FP8X4),
-                    rhs_scale=xg_s[e],
+                    rhs=xg_w[ORDER[e]].bitcast(FP8X4),
+                    rhs_scale=xg_s[ORDER[e]],
                     start=True,
                     stop=True,
                 )
 
         def round_h(e):
             if e == LAST - 1:
-                h_bf[e] = placed([P, C, PACK], BF16, "hbf%d" % e, 2 * PACK * C * (LAST - 1 - e))
+                h_bf[e] = placed([P, C, PACK], BF16, "hbf%d" % e, last_load_bytes // 2)
             elif e == LAST:
                 h_bf[e] = held([P, C, PACK], BF16, "hbf%d" % e)
             else:
@@ -243,7 +243,7 @@ def tile_moe_elr_none_kernel(
             if e in LATE_H:
                 h_codes[e] = placed([P, C], U32, "hc%d" % e, last_grouped_at + 4 * C * LATE_H.index(e))
             else:
-                h_codes[e] = on_raw([P, C], U32, "hc%d" % e, e + 2, 6 * PACK * C) if e < 3 else held([P, C], U32, "hc%d" % e)
+                h_codes[e] = on_raw([P, C], U32, "hc%d" % e, e + 2, 6 * PACK * C) if e < 5 else held([P, C], U32, "hc%d" % e)
             h_scales[e] = held([P, C], U8, "hs%d" % e)
             nc.vector.quantize_mx(
                 out=h_codes[e][:].bitcast(FP8X4),
@@ -253,13 +253,13 @@ def tile_moe_elr_none_kernel(
 
         warm = psum.tile([P, H], F32, name="warm")
 
-        def warm_up(e, plane):
+        def warm_up(e, columns):
             nc.tensor.matmul_mx(
-                out=warm[:],
-                lhsT=xg_w[e].bitcast(FP8X4),
-                lhsT_scale=plane,
-                rhs=wa_codes[e][:].bitcast(FP8X4),
-                rhs_scale=wa_scales[e][:],
+                out=warm[:, 0:columns],
+                lhsT=h_codes[e][:].bitcast(FP8X4),
+                lhsT_scale=h_scales[e][:],
+                rhs=wa_codes[e][:, 0:columns].bitcast(FP8X4),
+                rhs_scale=wa_scales[e][:, 0:columns],
                 start=True,
                 stop=True,
             )
@@ -273,15 +273,16 @@ def tile_moe_elr_none_kernel(
             round_expert(e)
             if e >= 2 and e - 2 not in LATE_H:
                 quantize_h(e - 2)
+            if e == LAST - 1:
+                for columns in WARM_UP_COLUMNS:
+                    warm_up(e - 2, columns)
             round_h(e - 1)
             if e in GATE_BEHIND:
                 keep_gate(GATE_BEHIND.index(e))
             quantize_expert(e)
             first_product(e)
-            if e >= LAST - 2:
-                for n in range(2):
-                    warm_up(e, xg_s[e])
-        round_last()
+        round_last(0)
+        round_last(1)
         quantize_last()
         first_product(LAST)
         round_h(LAST - 1)
@@ -290,13 +291,13 @@ def tile_moe_elr_none_kernel(
         round_h(LAST)
         quantize_h(LAST)
 
-        y = [placed([P, S], F32, "y0", last_grouped_at + 2 * PACK * H + 4 * P - 64), held([P, S], F32, "y1")]
+        y = [placed([P, S], F32, "y0", last_load_bytes - 64), held([P, S], F32, "y1")]
 
         def frozen_operands(e, b):
             return w_t[e, b].bitcast(FP4X4), ws[:, e * N + b * P : e * N + (b + 1) * P], xg_w[e], xg_s[e]
 
         def adapter_operands(e, b):
-            return wb_t[e, b].bitcast(FP8X4), wbs[4 * (e % PACK) : P, e // PACK, b * P : (b + 1) * P], h_codes[e][:], h_scales[e][:]
+            return wb_t[e, b].bitcast(FP8X4), wbs[4 * (e % PACK) : P, e // PACK, b * P : (b + 1) * P], h_codes[ORDER.index(e)][:], h_scales[ORDER.index(e)][:]
 
         def y_passes(bank, experts, b, passes, opens=False, closes=False):
             for n, (operands, e) in enumerate(passes):
@@ -327,67 +328,71 @@ def tile_moe_elr_none_kernel(
             return [numbered_bank(number, len(experts)) for experts, number in zip(groups, bank_numbers)]
 
         banks = banks_of(BLOCK0_GROUPS, BLOCK0_BANKS)
-        wide0, wide1, single0, single1 = BLOCK0_GROUPS
-        y_passes(banks[0], wide0, 0, frozen(wide0) + adapter(wide0), True, True)
-        empty(nc.scalar.copy, banks[0], wide0, 0)
-        y_passes(banks[1], wide1, 0, adapter(wide1[:1]) + frozen(wide1) + adapter(wide1[1:]), True, True)
-        empty(nc.scalar.copy, banks[1], wide1, 0)
-        y_passes(banks[2], single0, 0, adapter(single0) + frozen(single0), True, True)
-        empty(nc.vector.tensor_copy, banks[2], single0, 0)
-        y_passes(banks[3], single1, 0, adapter(single1) + frozen(single1), True, True)
-        empty(nc.vector.tensor_copy, banks[3], single1, 0)
+        late = [ORDER[n] for n in LATE_H]
+        for bank, experts in zip(banks[:-1], BLOCK0_GROUPS):
+            y_passes(bank, experts, 0, adapter(sorted(experts, key=lambda e: e not in late)), opens=True)
+        for bank, experts, engine_copy in zip(banks[:-1], BLOCK0_GROUPS, (nc.scalar.copy, nc.vector.tensor_copy)):
+            y_passes(bank, experts, 0, frozen(experts), closes=True)
+            empty(engine_copy, bank, experts, 0)
+        y_passes(banks[-1], (LAST,), 0, frozen((LAST,)) + adapter((LAST,)), True, True)
+        empty(nc.scalar.copy, banks[-1], (LAST,), 0)
         banks = banks_of(BLOCK1_GROUPS, BLOCK1_BANKS)
-        for bank, experts in zip(banks[1:], BLOCK1_GROUPS[1:]):
-            y_passes(bank, experts, 1, frozen(experts), opens=True)
         for bank, experts in zip(banks, BLOCK1_GROUPS):
-            if LAST in experts:
-                y_passes(bank, experts, 1, adapter(experts[::-1]) + frozen(experts), True, True)
-            else:
+            y_passes(bank, experts, 1, frozen(experts), opens=True)
+
+        def close_block1():
+            for bank, experts in zip(banks, BLOCK1_GROUPS):
                 y_passes(bank, experts, 1, adapter(experts), closes=True)
-            empty(nc.scalar.copy, bank, experts, 1)
+                empty(nc.scalar.copy, bank, experts, 1)
 
-        res = [held([P, T], F32, "res%d" % b) for b in range(2)]
-        picked = [[held([P, T], F32, "pick%d_%d" % (b, r)) for r in range(2)] for b in range(2)]
-        half_tokens = T // 2
-        halves = (0, half_tokens)
+        half_tokens = T // 4
+        res, plain, product = {}, {}, {}
 
-        def pick(b, r, first, count):
-            tokens = slice(first, first + count)
-            entries = pos_t[r][:, first // 16 : (first + count) // 16]
-            nc.vector.tensor_tensor(picked[b][r][:, tokens], y[b][:].indirect(entries), gate_t[r][:, tokens], MULT)
+        def tokens(halves):
+            return slice(halves[0] * half_tokens, (halves[-1] + 1) * half_tokens)
 
-        def pick_row_block(b):
-            pick(b, 0, 0, T)
-            for first in halves:
-                pick(b, 1, first, half_tokens)
+        def window(b, r, halves):
+            entries = pos_t[r][:, halves[0] * half_tokens // 16 : (halves[-1] + 1) * half_tokens // 16]
+            return y[b][:].indirect(entries)
 
-        def sum_by_transposes(first, sum_bank, back_bank):
-            chunks = half_tokens // P
-            turned = numbered_bank(sum_bank, chunks)
+        for b in range(2):
             for r in range(2):
-                for a in range(chunks):
-                    nc.tensor.matmul(
-                        turned[:, a, :],
-                        picked[0][r][:, first + a * P : first + (a + 1) * P],
-                        ident[:],
-                        is_transpose=True,
-                        start=(r, a) == (0, 0),
-                        stop=(r, a) == (1, chunks - 1),
-                    )
-            summed = held([P, chunks, P], F32, "summed%d" % first)
-            nc.scalar.copy(out=summed[:], in_=turned[:])
-            back = numbered_bank(back_bank, chunks)
-            for a in range(chunks):
-                nc.tensor.transpose(back[:, a, :], summed[:, a, :], ident[:])
-            tokens = slice(first, first + half_tokens)
-            nc.scalar.copy(out=res[0][:, tokens], in_=back[:].rearrange("p a t -> p (a t)"))
-            nc.scalar.dma_start(out=out[0:P, tokens], in_=res[0][:, tokens])
+                product[b, r] = held([P, T], F32, "prod%d_%d" % (b, r))
+                plain[b, r] = held([P, T], F32, "plain%d_%d" % (b, r))
+            res[b] = held([P, T], F32, "res%d" % b)
 
-        pick_row_block(0)
-        for first, (sum_bank, back_bank) in zip(halves, SUM_BANKS):
-            sum_by_transposes(first, sum_bank, back_bank)
-        pick_row_block(1)
-        for first in halves:
-            tokens = slice(first, first + half_tokens)
-            nc.vector.tensor_tensor(res[1][:, tokens], picked[1][0][:, tokens], picked[1][1][:, tokens], ADD)
-            nc.sync.dma_start(out=out[P:N, tokens], in_=res[1][:, tokens])
+        def gather_times_gate(b, r, *halves):
+            nc.vector.tensor_tensor(product[b, r][:, tokens(halves)], window(b, r, halves), gate_t[r][:, tokens(halves)], MULT)
+
+        def gather(b, r, *halves):
+            nc.scalar.activation(plain[b, r][:, tokens(halves)], window(b, r, halves), COPY)
+
+        def times_gate(b, r, *halves):
+            part = tokens(halves)
+            nc.vector.tensor_tensor(product[b, r][:, part], plain[b, r][:, part], gate_t[r][:, part], MULT)
+
+        def add(b, *halves):
+            part = tokens(halves)
+            nc.vector.tensor_tensor(res[b][:, part], product[b, 0][:, part], product[b, 1][:, part], ADD)
+
+        def store(b, *halves):
+            nc.sync.dma_start(out=out[b * P : (b + 1) * P, tokens(halves)], in_=res[b][:, tokens(halves)])
+
+        gather(0, 0, 0, 1)
+        close_block1()
+        gather_times_gate(0, 1, 0, 3)
+        gather_times_gate(0, 0, 2, 3)
+        times_gate(0, 0, 0)
+        times_gate(0, 0, 1)
+        add(0, 0)
+        add(0, 1, 3)
+        store(0, 0, 3)
+        gather(1, 0, 0, 1)
+        gather(1, 0, 2, 3)
+        gather_times_gate(1, 1, 0, 3)
+        times_gate(1, 0, 0, 1)
+        times_gate(1, 0, 2, 3)
+        add(1, 0, 1)
+        store(1, 0, 1)
+        add(1, 2, 3)
+        store(1, 2, 3)

@@ -24,7 +24,6 @@ COPY = mybir.ActivationFunctionType.Copy
 LAST = E - 1
 ALL_EXPERTS = tuple(range(E))
 GATHERS = ((0, 1, 2), (3, 4, 5), (6, 7))
-LAST_PLACES = (32, 44)
 GATE_BEHIND = (2, 4)
 STREAM_PLACES = (0, 56, 84, 84, 84, 84, 84)
 WARM_UPS = 3
@@ -127,9 +126,8 @@ def tile_moe_elr_none_kernel(
         load_scales(xs[:], 0, x_scales[0].rearrange("(q r) t -> r q t", r=4))
         for e in range(1, LAST):
             load_wa(e)
-        last_raw = [placed([P, PACK, H // 2], F32, "lastraw%d" % u, u * last_load_bytes // 2) for u in range(2)]
-        for u in range(2):
-            load(last_raw[u][:], wa_rows[LAST][:, :, u * H // 2 : (u + 1) * H // 2])
+        last_raw = placed([P, PACK, H], F32, "lastraw", 0)
+        load(last_raw[:], wa_rows[LAST])
         load_wb(ALL_EXPERTS, 0)
         load_scales(ws[:].rearrange("p (e n) -> p e n", e=E), 0, w_scales.rearrange("e s (q r) n -> r q (e s) n", r=4))
         for experts in BLOCK0_LOADS:
@@ -192,11 +190,11 @@ def tile_moe_elr_none_kernel(
 
         grouped[LAST] = placed([P, PACK, P, PACK], BF16, "grp%d" % LAST, last_grouped_at)
 
-        def round_last(u):
-            first, cut, end = u * P // 2, LAST_PLACES[u], P // 2
-            rounded, source = grouped[LAST], last_raw[u]
-            round_wa(nc.vector.tensor_copy, rounded[:, :, first : first + cut, :], source[:, :, 0 : PACK * cut])
-            round_wa(nc.scalar.copy, rounded[:, :, first + cut : first + end, :], source[:, :, PACK * cut : H // 2])
+        def round_last():
+            cut = STREAM_PLACES[-1]
+            rounded, source = grouped[LAST], last_raw
+            round_wa(nc.vector.tensor_copy, rounded[:, :, 0:cut, :], source[:, :, 0 : PACK * cut])
+            round_wa(nc.scalar.copy, rounded[:, :, cut:P, :], source[:, :, PACK * cut : H])
 
         last_codes = [placed([P, P], U32, "lc%d" % t, last_load_bytes - 4 * P * (PACK - t)) for t in range(PACK)]
         last_scales = [held([P, P], U8, "ls%d" % t)[:] for t in range(PACK)]
@@ -281,8 +279,7 @@ def tile_moe_elr_none_kernel(
                 keep_gate(GATE_BEHIND.index(e))
             quantize_expert(e)
             first_product(e)
-        round_last(0)
-        round_last(1)
+        round_last()
         quantize_last()
         first_product(LAST)
         round_h(LAST - 1)

@@ -113,11 +113,12 @@ def tile_moe_elr_none_kernel(
 
         ident = held([P, P], F32, "ident")
         make_identity(nc, ident[:])
-        for g in range(E // PACK):
-            for q in range(4):
-                nc.gpsimd.dma_start(
-                    out=wbs[:].bitcast(I32)[32 * q : 32 * q + 16, g, :],
-                    in_=wb_scales[PACK * g : PACK * (g + 1), 0, 4 * q : 4 * q + 4, :].bitcast(I32),
+
+        def load_wb_scales(q):
+            for g in range(E // PACK):
+                load(
+                    wbs[:].bitcast(I32)[32 * q : 32 * q + 16, g, :],
+                    wb_scales[PACK * g : PACK * (g + 1), 0, 4 * q : 4 * q + 4, :].bitcast(I32),
                 )
 
         load(xw[:].bitcast(I32), x_words[0].rearrange("p t d -> p (t d)").bitcast(I32))
@@ -126,6 +127,8 @@ def tile_moe_elr_none_kernel(
         load_scales(xs[:], 0, x_scales[0].rearrange("(q r) t -> r q t", r=4))
         for e in range(1, LAST):
             load_wa(e)
+            if e <= 4:
+                load_wb_scales(e - 1)
         last_raw = placed([P, PACK, H], F32, "lastraw", 0)
         load(last_raw[:], wa_rows[LAST])
         load_wb(ALL_EXPERTS, 0)

@@ -24,22 +24,23 @@ COPY = mybir.ActivationFunctionType.Copy
 LAST = E - 1
 ALL_EXPERTS = tuple(range(E))
 GATHERS = ((0, 1, 2), (3, 4, 5), (6, 7))
+VECTOR_PLACES = (0, 56, 84, 84, 84, 84, 84, 84)
 GATE_BEHIND = (2, 4)
-STREAM_PLACES = (0, 56, 84, 84, 84, 84, 84)
-WARM_UPS = 3
-WB_PLANE = 4
-
-BLOCK0_LOADS = ((0, 1, 2, 3), (4, 5, 6, 7))
-BLOCK1_LOADS = ((5, 6, 7), (2, 3, 4), (0, 1))
-BLOCK0_GROUPS = ((0, 1, 2, 3), (4, 5, 6), (7,))
-BLOCK1_GROUPS = BLOCK1_LOADS
+HELD_H = 3
 LATE_H = (5, 6)
-ORDER = (1, 2, 3, 4, 5, 0, 6, 7)
 WARM_UP_COLUMNS = (512, 256)
 
+BLOCK0_LOADS = ((0, 1, 2, 3), (4, 5), (6, 7))
+BLOCK1_LOADS = ((5, 6, 7), (3, 4), (1, 2), (0,))
+BLOCK0_GROUPS = ((0, 1, 2, 3), (4, 5), (6,), (LAST,))
+BLOCK1_GROUPS = BLOCK1_LOADS
+
 H_BANKS = (5, 6)
-BLOCK0_BANKS = (0, 1, 2)
-BLOCK1_BANKS = (1, 0, 4)
+LAST_H_BANK = 4
+BLOCK0_BANKS = (0, 1, 2, 3)
+BLOCK1_BANKS = (2, 0, 1, 3)
+
+QUARTER = T // 4
 
 
 def tile_moe_elr_none_kernel(
@@ -50,23 +51,24 @@ def tile_moe_elr_none_kernel(
         keep = ctx.enter_context(tc.tile_pool(name="keep", bufs=1))
         psum = ctx.enter_context(tc.psum_pool(name="psum", bufs=1))
 
-        def held(shape, dtype, name, tag=None):
-            return keep.tile(shape, dtype, name=name, tag=tag or name, align_bytes=64)
+        def held(shape, dtype, name):
+            return keep.tile(shape, dtype, name=name, align_bytes=64)
 
         def numbered_bank(number, parts):
             return psum.tile([P, parts, P], F32, name="bank%d" % number)
 
         tail = ctx.enter_context(tc.tile_pool(name="tail", bufs=1))
-        last_load_bytes = 4 * PACK * H
-        last_grouped_at = last_load_bytes + 4 * S
+        wa_bytes = 4 * PACK * H
+        last_grouped_at = wa_bytes + 4 * S
+        h_bytes = 2 * PACK * C
 
         stream = ctx.enter_context(tc.tile_pool(name="stream", bufs=1))
 
-        def on_raw(shape, dtype, name, e, offset):
-            return stream.tile(shape, dtype, name=name, align_bytes=64, offset=4 * PACK * H * e + offset)
+        def on_load(shape, dtype, name, e, part):
+            return stream.tile(shape, dtype, name=name, align_bytes=64, offset=wa_bytes * e + h_bytes * part)
 
         def placed(shape, dtype, name, offset):
-            return tail.tile(shape, dtype, name=name, tag=name, align_bytes=64, offset=offset)
+            return tail.tile(shape, dtype, name=name, align_bytes=64, offset=offset)
 
         def load(tile_view, dram_view):
             nc.sync.dma_start(out=tile_view, in_=dram_view)
@@ -82,27 +84,29 @@ def tile_moe_elr_none_kernel(
         for scale_tile in (xs, wbs, ws):
             nc.vector.memset(scale_tile[:].bitcast(I32), 0)
 
-        def load_scales(scale_tile, first, rows):
+        def load_scales(scale_tile, rows):
             for r in range(4):
-                load(scale_tile.bitcast(I32)[first + r : P : 32], rows[r].bitcast(I32))
+                load(scale_tile.bitcast(I32)[r:P:32], rows[r].bitcast(I32))
 
         wa_rows = wa.rearrange("e (p j) i -> e p j i", j=PACK)
         raw = {}
 
         def load_wa(e):
-            raw[e] = stream.tile([P, PACK, H], F32, name="raw%d" % e, align_bytes=64, offset=4 * PACK * H * e)
-            load(raw[e][:], wa_rows[ORDER[e]])
+            if e == LAST:
+                raw[e] = placed([P, PACK, H], F32, "raw%d" % e, 0)
+            else:
+                raw[e] = on_load([P, PACK, H], F32, "raw%d" % e, e, 0)
+            load(raw[e][:], wa_rows[e])
 
         w_view = w_words.rearrange("e s p c -> p (e s) c")
         wb_view = wb_words.rearrange("e s p n d -> p (e s) (n d)")
         w_t, wb_t = {}, {}
 
-        def load_w(experts, b):
-            piece = held([P, len(experts), 2 * P], U8, "w%d_%d" % (experts[0], b))
-            rows = slice(experts[0], experts[-1] + 1)
-            load(piece[:].bitcast(I32), w_view[:, rows, 2 * b * P : 2 * (b + 1) * P].bitcast(I32))
-            for n, e in enumerate(experts):
-                w_t[e, b] = piece[:, n, :]
+        def load_w(b):
+            piece = held([P, E, 2 * P], U8, "w%d" % b)
+            load(piece[:].bitcast(I32), w_view[:, :, 2 * b * P : 2 * (b + 1) * P].bitcast(I32))
+            for e in ALL_EXPERTS:
+                w_t[e, b] = piece[:, e, :]
 
         def load_wb(experts, b):
             piece = held([P, len(experts), 4 * P], U8, "wb%d_%d" % (experts[0], b))
@@ -113,31 +117,27 @@ def tile_moe_elr_none_kernel(
 
         ident = held([P, P], F32, "ident")
         make_identity(nc, ident[:])
-
-        def load_wb_scales(q):
-            for g in range(E // PACK):
-                load(
-                    wbs[:].bitcast(I32)[32 * q : 32 * q + 16, g, :],
-                    wb_scales[PACK * g : PACK * (g + 1), 0, 4 * q : 4 * q + 4, :].bitcast(I32),
+        for g in range(E // PACK):
+            for q in range(4):
+                nc.gpsimd.dma_start(
+                    out=wbs[:].bitcast(I32)[32 * q : 32 * q + 16, g, :],
+                    in_=wb_scales[PACK * g : PACK * (g + 1), 0, 4 * q : 4 * q + 4, :].bitcast(I32),
                 )
 
         load(xw[:].bitcast(I32), x_words[0].rearrange("p t d -> p (t d)").bitcast(I32))
         load(offs_t[:], offs)
         load_wa(0)
-        load_scales(xs[:], 0, x_scales[0].rearrange("(q r) t -> r q t", r=4))
-        for e in range(1, LAST):
+        load_scales(xs[:], x_scales[0].rearrange("(q r) t -> r q t", r=4))
+        for e in range(1, E):
             load_wa(e)
-            if e <= 4:
-                load_wb_scales(e - 1)
-        last_raw = placed([P, PACK, H], F32, "lastraw", 0)
-        load(last_raw[:], wa_rows[LAST])
-        load_wb(ALL_EXPERTS, 0)
-        load_scales(ws[:].rearrange("p (e n) -> p e n", e=E), 0, w_scales.rearrange("e s (q r) n -> r q (e s) n", r=4))
-        for experts in BLOCK0_LOADS:
-            load_w(experts, 0)
-        load_w(ALL_EXPERTS, 1)
+        load_wb(BLOCK0_LOADS[0], 0)
+        load_scales(ws[:].rearrange("p (e n) -> p e n", e=E), w_scales.rearrange("e s (q r) n -> r q (e s) n", r=4))
+        load_w(0)
+        for experts in BLOCK0_LOADS[1:]:
+            load_wb(experts, 0)
         load(pos_t[1][:], pos2)
         load(pos_t[0][:], pos1)
+        load_w(1)
         for experts in BLOCK1_LOADS:
             load_wb(experts, 1)
 
@@ -148,41 +148,41 @@ def tile_moe_elr_none_kernel(
                 nc.tensor.transpose(spread[r][:, a, :], gate_cols[:, r, a : a + 1].to_broadcast([P, P]), ident[:])
 
         def keep_gate(r):
-            gate_t[r] = on_raw([P, T], F32, "gate%d" % r, GATE_BEHIND[r], 2 * PACK * C)
+            gate_t[r] = on_load([P, T], F32, "gate%d" % r, GATE_BEHIND[r], 1)
             nc.scalar.copy(
                 out=gate_t[r][:].rearrange("q (p a) -> q p a", p=P), in_=spread[r][:].rearrange("q a p -> q p a")
             )
 
-        xg_w, xg_s, last_gathered = {}, {}, {}
+        xg_w, xg_s = {}, {}
 
         def gather_tokens(table, dtype, name, gathered):
             for experts in GATHERS:
                 entries = offs_t[:, experts[0] * C // 16 : (experts[-1] + 1) * C // 16]
                 piece = held([P, len(experts) * C], dtype, "%s%d" % (name, experts[0]))
-                last_gathered[name] = piece
                 nc.vector.tensor_copy(piece[:], table[:].indirect(entries))
                 for n, e in enumerate(experts):
                     gathered[e] = piece[:, n * C : (n + 1) * C]
-
-        def round_wa(engine_copy, dst, src):
-            engine_copy(
-                out=dst.rearrange("p t (m a) j -> p m j a t", a=2),
-                in_=src.rearrange("p j (m a t) -> p m j a t", a=2, t=PACK),
-            )
 
         wa_codes = [held([P, H], U32, "wac%d" % e) for e in range(LAST)]
         wa_scales = [held([P, H], U8, "was%d" % e) for e in range(LAST)]
         grouped = {}
 
+        def round_tiles(e, tiles):
+            columns = raw[e][:].rearrange("p j (m t) -> p j m t", t=PACK)
+            cut = VECTOR_PLACES[e]
+            shares = [(nc.vector.tensor_copy, slice(0, cut))] if cut else []
+            for engine_copy, places in shares + [(nc.scalar.copy, slice(cut, P))]:
+                engine_copy(
+                    out=grouped[e][:, tiles, places, :].rearrange("p t (m a) j -> p m j a t", a=2),
+                    in_=columns[:, :, places, tiles].rearrange("p j (m a) t -> p m j a t", a=2),
+                )
+
         def round_expert(e):
             if e:
-                grouped[e] = on_raw([P, PACK, P, PACK], BF16, "grp%d" % e, e - 1, 8 * PACK * C)
+                grouped[e] = on_load([P, PACK, P, PACK], BF16, "grp%d" % e, e - 1, 4)
             else:
                 grouped[e] = held([P, PACK, P, PACK], BF16, "grp0")
-            cut = STREAM_PLACES[e]
-            if cut:
-                round_wa(nc.vector.tensor_copy, grouped[e][:, :, 0:cut, :], raw[e][:, :, 0 : PACK * cut])
-            round_wa(nc.scalar.copy, grouped[e][:, :, cut:P, :], raw[e][:, :, PACK * cut : H])
+            round_tiles(e, slice(0, PACK))
 
         def quantize_expert(e):
             nc.vector.quantize_mx(
@@ -192,59 +192,55 @@ def tile_moe_elr_none_kernel(
             )
 
         grouped[LAST] = placed([P, PACK, P, PACK], BF16, "grp%d" % LAST, last_grouped_at)
+        last_codes = [held([P, P], U32, "lc%d" % t) for t in range(PACK - 1)]
+        last_codes.append(placed([P, P], U32, "lc%d" % (PACK - 1), wa_bytes - 4 * P))
+        last_scales = [held([P, P], U8, "ls%d" % t) for t in range(PACK)]
 
-        def round_last():
-            cut = STREAM_PLACES[-1]
-            rounded, source = grouped[LAST], last_raw
-            round_wa(nc.vector.tensor_copy, rounded[:, :, 0:cut, :], source[:, :, 0 : PACK * cut])
-            round_wa(nc.scalar.copy, rounded[:, :, cut:P, :], source[:, :, PACK * cut : H])
-
-        last_codes = [placed([P, P], U32, "lc%d" % t, last_load_bytes - 4 * P * (PACK - t)) for t in range(PACK)]
-        last_scales = [held([P, P], U8, "ls%d" % t)[:] for t in range(PACK)]
-
-        def quantize_last():
+        def round_and_quantize_last():
+            for first in (0, 2):
+                round_tiles(LAST, slice(first, first + 2))
             for t in range(PACK):
                 nc.vector.quantize_mx(
                     out=last_codes[t][:].bitcast(FP8X4),
-                    scales=last_scales[t],
+                    scales=last_scales[t][:],
                     in_=grouped[LAST][:, t].rearrange("p m j -> p (m j)"),
                 )
 
         def stationary_wa(e, t):
             if e == LAST:
-                return last_codes[t][:], last_scales[t]
+                return last_codes[t][:], last_scales[t][:]
             return wa_codes[e][:, t * P : (t + 1) * P], wa_scales[e][:, t * P : (t + 1) * P]
 
         h_bank, h_bf, h_codes, h_scales = {}, {}, {}, {}
 
         def first_product(e):
-            h_bank[e] = numbered_bank(H_BANKS[e % 2] if e < LAST else 4, PACK)
+            h_bank[e] = numbered_bank(H_BANKS[e % 2] if e < LAST else LAST_H_BANK, PACK)
             for t in range(PACK):
                 codes, scales = stationary_wa(e, t)
                 nc.tensor.matmul_mx(
                     out=h_bank[e][:, t, :],
                     lhsT=codes.bitcast(FP8X4),
                     lhsT_scale=scales,
-                    rhs=xg_w[ORDER[e]].bitcast(FP8X4),
-                    rhs_scale=xg_s[ORDER[e]],
+                    rhs=xg_w[e].bitcast(FP8X4),
+                    rhs_scale=xg_s[e],
                     start=True,
                     stop=True,
                 )
 
-        def round_h(e):
-            if e == LAST - 1:
-                h_bf[e] = placed([P, C, PACK], BF16, "hbf%d" % e, last_load_bytes // 2)
-            elif e == LAST:
-                h_bf[e] = held([P, C, PACK], BF16, "hbf%d" % e)
-            else:
-                h_bf[e] = on_raw([P, C, PACK], BF16, "hbf%d" % e, e + 1, 0)
-            nc.scalar.copy(out=h_bf[e][:], in_=h_bank[e][:].rearrange("p t s -> p s t"))
+        def round_h(e, engine_copy, rounded):
+            h_bf[e] = rounded
+            engine_copy(out=rounded[:], in_=h_bank[e][:].rearrange("p t s -> p s t"))
+
+        def round_h_behind(e, later):
+            round_h(e, nc.scalar.copy, on_load([P, C, PACK], BF16, "hbf%d" % e, later, 0))
 
         def quantize_h(e):
             if e in LATE_H:
                 h_codes[e] = placed([P, C], U32, "hc%d" % e, last_grouped_at + 4 * C * LATE_H.index(e))
+            elif e in (HELD_H, LAST):
+                h_codes[e] = held([P, C], U32, "hc%d" % e)
             else:
-                h_codes[e] = on_raw([P, C], U32, "hc%d" % e, e + 2, 6 * PACK * C) if e < 5 else held([P, C], U32, "hc%d" % e)
+                h_codes[e] = on_load([P, C], U32, "hc%d" % e, e + 2, 3)
             h_scales[e] = held([P, C], U8, "hs%d" % e)
             nc.vector.quantize_mx(
                 out=h_codes[e][:].bitcast(FP8X4),
@@ -272,35 +268,41 @@ def tile_moe_elr_none_kernel(
         first_product(0)
         for e in range(1, LAST):
             round_expert(e)
-            if e >= 2 and e - 2 not in LATE_H:
+            if e >= 2 and e - 2 != HELD_H:
                 quantize_h(e - 2)
             if e == LAST - 1:
                 for columns in WARM_UP_COLUMNS:
                     warm_up(e - 2, columns)
-            round_h(e - 1)
+                round_h_behind(HELD_H, e)
+                first_product(HELD_H + 2)
+            elif e - 1 != HELD_H:
+                round_h_behind(e - 1, e)
             if e in GATE_BEHIND:
                 keep_gate(GATE_BEHIND.index(e))
             quantize_expert(e)
-            first_product(e)
-        round_last()
-        quantize_last()
+            if e != HELD_H + 2:
+                first_product(e)
+        quantize_h(HELD_H)
+        round_and_quantize_last()
         first_product(LAST)
-        round_h(LAST - 1)
+        round_h(LATE_H[0], nc.scalar.copy, placed([P, C, PACK], BF16, "hbf5", 0))
+        round_h(LATE_H[1], nc.vector.tensor_copy, placed([P, C, PACK], BF16, "hbf6", last_grouped_at + 2 * h_bytes))
         for e in LATE_H:
             quantize_h(e)
-        round_h(LAST)
+        round_h(LAST, nc.scalar.copy, held([P, C, PACK], BF16, "hbf7"))
         quantize_h(LAST)
 
-        y = [placed([P, S], F32, "y0", last_load_bytes - 64), held([P, S], F32, "y1")]
+        y = [placed([P, S], F32, "y0", wa_bytes - 64), held([P, S], F32, "y1")]
 
-        def frozen_operands(e, b):
+        def frozen(e, b):
             return w_t[e, b].bitcast(FP4X4), ws[:, e * N + b * P : e * N + (b + 1) * P], xg_w[e], xg_s[e]
 
-        def adapter_operands(e, b):
-            return wb_t[e, b].bitcast(FP8X4), wbs[4 * (e % PACK) : P, e // PACK, b * P : (b + 1) * P], h_codes[ORDER.index(e)][:], h_scales[ORDER.index(e)][:]
+        def adapter(e, b):
+            scales = wbs[4 * (e % PACK) : P, e // PACK, b * P : (b + 1) * P]
+            return wb_t[e, b].bitcast(FP8X4), scales, h_codes[e][:], h_scales[e][:]
 
-        def y_passes(bank, experts, b, passes, opens=False, closes=False):
-            for n, (operands, e) in enumerate(passes):
+        def y_passes(bank, experts, b, operands, opens):
+            for e in experts:
                 words, scales, moving, moving_scales = operands(e, b)
                 nc.tensor.matmul_mx(
                     out=bank[:, e - experts[0], :],
@@ -308,15 +310,9 @@ def tile_moe_elr_none_kernel(
                     lhsT_scale=scales,
                     rhs=moving.bitcast(FP8X4),
                     rhs_scale=moving_scales,
-                    start=opens and n == 0,
-                    stop=closes and n == len(passes) - 1,
+                    start=opens and e == experts[0],
+                    stop=not opens and e == experts[-1],
                 )
-
-        def frozen(experts):
-            return [(frozen_operands, e) for e in experts]
-
-        def adapter(experts):
-            return [(adapter_operands, e) for e in experts]
 
         def empty(engine_copy, bank, experts, b):
             engine_copy(
@@ -325,74 +321,70 @@ def tile_moe_elr_none_kernel(
             )
 
         def banks_of(groups, bank_numbers):
-            return [numbered_bank(number, len(experts)) for experts, number in zip(groups, bank_numbers)]
+            return [(numbered_bank(number, len(experts)), experts) for experts, number in zip(groups, bank_numbers)]
 
-        banks = banks_of(BLOCK0_GROUPS, BLOCK0_BANKS)
-        late = [ORDER[n] for n in LATE_H]
-        for bank, experts in zip(banks[:-1], BLOCK0_GROUPS):
-            y_passes(bank, experts, 0, adapter(sorted(experts, key=lambda e: e not in late)), opens=True)
-        for bank, experts, engine_copy in zip(banks[:-1], BLOCK0_GROUPS, (nc.scalar.copy, nc.vector.tensor_copy)):
-            y_passes(bank, experts, 0, frozen(experts), closes=True)
+        (first_bank, first_group), *others = banks_of(BLOCK0_GROUPS, BLOCK0_BANKS)
+        y_passes(first_bank, first_group, 0, adapter, opens=True)
+        y_passes(first_bank, first_group, 0, frozen, opens=False)
+        for bank, experts in others:
+            y_passes(bank, experts, 0, frozen, opens=True)
+        empty(nc.scalar.copy, first_bank, first_group, 0)
+        for (bank, experts), engine_copy in zip(others, (nc.vector.tensor_copy, nc.scalar.copy, nc.vector.tensor_copy)):
+            y_passes(bank, experts, 0, adapter, opens=False)
             empty(engine_copy, bank, experts, 0)
-        y_passes(banks[-1], (LAST,), 0, frozen((LAST,)) + adapter((LAST,)), True, True)
-        empty(nc.scalar.copy, banks[-1], (LAST,), 0)
-        banks = banks_of(BLOCK1_GROUPS, BLOCK1_BANKS)
-        for bank, experts in zip(banks, BLOCK1_GROUPS):
-            y_passes(bank, experts, 1, frozen(experts), opens=True)
+        block1_banks = banks_of(BLOCK1_GROUPS, BLOCK1_BANKS)
+        for bank, experts in block1_banks:
+            y_passes(bank, experts, 1, frozen, opens=True)
 
-        def close_block1():
-            for bank, experts in zip(banks, BLOCK1_GROUPS):
-                y_passes(bank, experts, 1, adapter(experts), closes=True)
-                empty(nc.scalar.copy, bank, experts, 1)
-
-        half_tokens = T // 4
-        res, plain, product = {}, {}, {}
-
-        def tokens(halves):
-            return slice(halves[0] * half_tokens, (halves[-1] + 1) * half_tokens)
-
-        def window(b, r, halves):
-            entries = pos_t[r][:, halves[0] * half_tokens // 16 : (halves[-1] + 1) * half_tokens // 16]
-            return y[b][:].indirect(entries)
-
+        product, plain, res = {}, {}, {}
         for b in range(2):
             for r in range(2):
                 product[b, r] = held([P, T], F32, "prod%d_%d" % (b, r))
-                plain[b, r] = held([P, T], F32, "plain%d_%d" % (b, r))
+            plain[b] = held([P, T], F32, "plain%d" % b)
             res[b] = held([P, T], F32, "res%d" % b)
 
-        def gather_times_gate(b, r, *halves):
-            nc.vector.tensor_tensor(product[b, r][:, tokens(halves)], window(b, r, halves), gate_t[r][:, tokens(halves)], MULT)
+        def tokens(first, last):
+            return slice(first * QUARTER, (last + 1) * QUARTER)
 
-        def gather(b, r, *halves):
-            nc.scalar.activation(plain[b, r][:, tokens(halves)], window(b, r, halves), COPY)
+        def picked(b, r, first, last):
+            return y[b][:].indirect(pos_t[r][:, first * QUARTER // 16 : (last + 1) * QUARTER // 16])
 
-        def times_gate(b, r, *halves):
-            part = tokens(halves)
-            nc.vector.tensor_tensor(product[b, r][:, part], plain[b, r][:, part], gate_t[r][:, part], MULT)
+        def gather_times_gate(b, r, first, last):
+            part = tokens(first, last)
+            nc.vector.tensor_tensor(product[b, r][:, part], picked(b, r, first, last), gate_t[r][:, part], MULT)
 
-        def add(b, *halves):
-            part = tokens(halves)
+        def gather_by_pos1(b, first, last):
+            nc.scalar.activation(plain[b][:, tokens(first, last)], picked(b, 0, first, last), COPY)
+
+        def times_gate(b, first, last):
+            part = tokens(first, last)
+            nc.vector.tensor_tensor(product[b, 0][:, part], plain[b][:, part], gate_t[0][:, part], MULT)
+
+        def add(b, first, last):
+            part = tokens(first, last)
             nc.vector.tensor_tensor(res[b][:, part], product[b, 0][:, part], product[b, 1][:, part], ADD)
 
-        def store(b, *halves):
-            nc.sync.dma_start(out=out[b * P : (b + 1) * P, tokens(halves)], in_=res[b][:, tokens(halves)])
+        def store(b, first, last):
+            part = tokens(first, last)
+            nc.sync.dma_start(out=out[b * P : (b + 1) * P, part], in_=res[b][:, part])
 
-        gather(0, 0, 0, 1)
-        close_block1()
+        gather_by_pos1(0, 0, 2)
+        for bank, experts in block1_banks:
+            y_passes(bank, experts, 1, adapter, opens=False)
+            empty(nc.scalar.copy, bank, experts, 1)
         gather_times_gate(0, 1, 0, 3)
-        gather_times_gate(0, 0, 2, 3)
+        gather_times_gate(0, 0, 3, 3)
         times_gate(0, 0, 0)
-        times_gate(0, 0, 1)
-        add(0, 0)
+        times_gate(0, 1, 2)
+        add(0, 0, 0)
         add(0, 1, 3)
         store(0, 0, 3)
-        gather(1, 0, 0, 1)
-        gather(1, 0, 2, 3)
+        halves = ((0, 1), (2, 3))
+        for first, last in halves:
+            gather_by_pos1(1, first, last)
         gather_times_gate(1, 1, 0, 3)
-        times_gate(1, 0, 0, 1)
-        times_gate(1, 0, 2, 3)
-        add(1, 0, 1)
-        store(1, 0, 1)
-        add(1, 2, 3)
-        store(1, 2, 3)
+        for first, last in halves:
+            times_gate(1, first, last)
+        for first, last in halves:
+            add(1, first, last)
+            store(1, first, last)

@@ -27,7 +27,7 @@ GATHERS = ((0, 1, 2), (3, 4, 5), (6, 7))
 VECTOR_PLACES = (0, 56, 84, 84, 84, 84, 84, 84)
 GATE_BEHIND = (2, 4)
 HELD_H = 3
-LATE_H = (5, 6)
+LATE_H = (6,)
 WARM_UP_COLUMNS = (512, 256)
 
 BLOCK0_LOADS = ((0, 1, 2, 3), (4, 5), (6, 7))
@@ -36,9 +36,10 @@ BLOCK0_GROUPS = ((0, 1, 2, 3), (4, 5), (6,), (LAST,))
 BLOCK1_GROUPS = BLOCK1_LOADS
 
 H_BANKS = (5, 6)
-LAST_H_BANK = 4
+LAST_H_BANKS = (4, 7)
+WARM_BANK = 7
 BLOCK0_BANKS = (0, 1, 2, 3)
-BLOCK1_BANKS = (2, 0, 1, 3)
+BLOCK1_BANKS = (3, 0, 1, 2)
 
 QUARTER = T // 4
 
@@ -214,7 +215,7 @@ def tile_moe_elr_none_kernel(
         h_bank, h_bf, h_codes, h_scales = {}, {}, {}, {}
 
         def first_product(e):
-            h_bank[e] = numbered_bank(H_BANKS[e % 2] if e < LAST else LAST_H_BANK, PACK)
+            h_bank[e] = numbered_bank(H_BANKS[e % 2], PACK)
             for t in range(PACK):
                 codes, scales = stationary_wa(e, t)
                 nc.tensor.matmul_mx(
@@ -227,6 +228,29 @@ def tile_moe_elr_none_kernel(
                     stop=True,
                 )
 
+        def last_first_product():
+            banks = [psum.tile([P, PACK, C // 2], F32, name="bank%d" % number) for number in LAST_H_BANKS]
+            for t in range(PACK):
+                codes, scales = stationary_wa(LAST, t)
+                for half, bank in enumerate(banks):
+                    slots = slice(half * C // 2, (half + 1) * C // 2)
+                    nc.tensor.matmul_mx(
+                        out=bank[:, t, :],
+                        lhsT=codes.bitcast(FP8X4),
+                        lhsT_scale=scales,
+                        rhs=xg_w[LAST][:, slots].bitcast(FP8X4),
+                        rhs_scale=xg_s[LAST][:, slots],
+                        start=True,
+                        stop=True,
+                    )
+            return banks
+
+        def round_last_h(banks):
+            h_bf[LAST] = held([P, C, PACK], BF16, "hbf7")
+            for half, engine_copy in enumerate((nc.scalar.copy, nc.vector.tensor_copy)):
+                slots = slice(half * C // 2, (half + 1) * C // 2)
+                engine_copy(out=h_bf[LAST][:, slots, :], in_=banks[half][:].rearrange("p t s -> p s t"))
+
         def round_h(e, engine_copy, rounded):
             h_bf[e] = rounded
             engine_copy(out=rounded[:], in_=h_bank[e][:].rearrange("p t s -> p s t"))
@@ -237,7 +261,7 @@ def tile_moe_elr_none_kernel(
         def quantize_h(e):
             if e in LATE_H:
                 h_codes[e] = placed([P, C], U32, "hc%d" % e, last_grouped_at + 4 * C * LATE_H.index(e))
-            elif e in (HELD_H, LAST):
+            elif e in (LAST - 2, LAST):
                 h_codes[e] = held([P, C], U32, "hc%d" % e)
             else:
                 h_codes[e] = on_load([P, C], U32, "hc%d" % e, e + 2, 3)
@@ -248,7 +272,7 @@ def tile_moe_elr_none_kernel(
                 in_=h_bf[e][:].rearrange("p s t -> p (s t)"),
             )
 
-        warm = psum.tile([P, H], F32, name="warm")
+        warm = psum.tile([P, H], F32, name="bank%d" % WARM_BANK)
 
         def warm_up(e, columns):
             nc.tensor.matmul_mx(
@@ -268,28 +292,22 @@ def tile_moe_elr_none_kernel(
         first_product(0)
         for e in range(1, LAST):
             round_expert(e)
-            if e >= 2 and e - 2 != HELD_H:
+            if e >= 2:
                 quantize_h(e - 2)
             if e == LAST - 1:
                 for columns in WARM_UP_COLUMNS:
                     warm_up(e - 2, columns)
-                round_h_behind(HELD_H, e)
-                first_product(HELD_H + 2)
-            elif e - 1 != HELD_H:
-                round_h_behind(e - 1, e)
+            round_h_behind(e - 1, e)
             if e in GATE_BEHIND:
                 keep_gate(GATE_BEHIND.index(e))
             quantize_expert(e)
-            if e != HELD_H + 2:
-                first_product(e)
-        quantize_h(HELD_H)
+            first_product(e)
+        quantize_h(LAST - 2)
         round_and_quantize_last()
-        first_product(LAST)
-        round_h(LATE_H[0], nc.scalar.copy, placed([P, C, PACK], BF16, "hbf5", 0))
-        round_h(LATE_H[1], nc.vector.tensor_copy, placed([P, C, PACK], BF16, "hbf6", last_grouped_at + 2 * h_bytes))
-        for e in LATE_H:
-            quantize_h(e)
-        round_h(LAST, nc.scalar.copy, held([P, C, PACK], BF16, "hbf7"))
+        last_banks = last_first_product()
+        round_h(LATE_H[0], nc.scalar.copy, placed([P, C, PACK], BF16, "hbf6", 0))
+        round_last_h(last_banks)
+        quantize_h(LATE_H[0])
         quantize_h(LAST)
 
         y = [placed([P, S], F32, "y0", wa_bytes - 64), held([P, S], F32, "y1")]
@@ -329,7 +347,7 @@ def tile_moe_elr_none_kernel(
         for bank, experts in others:
             y_passes(bank, experts, 0, frozen, opens=True)
         empty(nc.scalar.copy, first_bank, first_group, 0)
-        for (bank, experts), engine_copy in zip(others, (nc.vector.tensor_copy, nc.scalar.copy, nc.vector.tensor_copy)):
+        for (bank, experts), engine_copy in zip(others, (nc.vector.tensor_copy, nc.vector.tensor_copy, nc.scalar.copy)):
             y_passes(bank, experts, 0, adapter, opens=False)
             empty(engine_copy, bank, experts, 0)
         block1_banks = banks_of(BLOCK1_GROUPS, BLOCK1_BANKS)

@@ -24,14 +24,14 @@ COPY = mybir.ActivationFunctionType.Copy
 LAST = E - 1
 ALL_EXPERTS = tuple(range(E))
 GATHERS = ((0, 1, 2), (3, 4, 5), (6, 7))
-VECTOR_PLACES = (0, 56, 84, 84, 84, 84, 84, 84)
+VECTOR_PLACES = (0, 56, 84, 84, 84, 84, 84)
+LAST_VECTOR_PLACES = (84, 68)
 GATE_BEHIND = (2, 4)
-HELD_H = 3
-LATE_H = (6,)
+LATE_H = (5, 6)
 WARM_UP_COLUMNS = (512, 256)
 
-BLOCK0_LOADS = ((0, 1, 2, 3), (4, 5), (6, 7))
-BLOCK1_LOADS = ((5, 6, 7), (3, 4), (1, 2), (0,))
+BLOCK0_LOADS = ((0, 1, 2, 3), (4, 5, 6), (7,))
+BLOCK1_LOADS = ((5, 6, 7), (2, 3, 4), (1,), (0,))
 BLOCK0_GROUPS = ((0, 1, 2, 3), (4, 5), (6,), (LAST,))
 BLOCK1_GROUPS = BLOCK1_LOADS
 
@@ -168,9 +168,8 @@ def tile_moe_elr_none_kernel(
         wa_scales = [held([P, H], U8, "was%d" % e) for e in range(LAST)]
         grouped = {}
 
-        def round_tiles(e, tiles):
+        def round_tiles(e, tiles, cut):
             columns = raw[e][:].rearrange("p j (m t) -> p j m t", t=PACK)
-            cut = VECTOR_PLACES[e]
             shares = [(nc.vector.tensor_copy, slice(0, cut))] if cut else []
             for engine_copy, places in shares + [(nc.scalar.copy, slice(cut, P))]:
                 engine_copy(
@@ -183,7 +182,7 @@ def tile_moe_elr_none_kernel(
                 grouped[e] = on_load([P, PACK, P, PACK], BF16, "grp%d" % e, e - 1, 4)
             else:
                 grouped[e] = held([P, PACK, P, PACK], BF16, "grp0")
-            round_tiles(e, slice(0, PACK))
+            round_tiles(e, slice(0, PACK), VECTOR_PLACES[e])
 
         def quantize_expert(e):
             nc.vector.quantize_mx(
@@ -198,8 +197,8 @@ def tile_moe_elr_none_kernel(
         last_scales = [held([P, P], U8, "ls%d" % t) for t in range(PACK)]
 
         def round_and_quantize_last():
-            for first in (0, 2):
-                round_tiles(LAST, slice(first, first + 2))
+            for first, cut in zip((0, 2), LAST_VECTOR_PLACES):
+                round_tiles(LAST, slice(first, first + 2), cut)
             for t in range(PACK):
                 nc.vector.quantize_mx(
                     out=last_codes[t][:].bitcast(FP8X4),
@@ -247,7 +246,7 @@ def tile_moe_elr_none_kernel(
 
         def round_last_h(banks):
             h_bf[LAST] = held([P, C, PACK], BF16, "hbf7")
-            for half, engine_copy in enumerate((nc.scalar.copy, nc.vector.tensor_copy)):
+            for half, engine_copy in enumerate((nc.vector.tensor_copy, nc.scalar.copy)):
                 slots = slice(half * C // 2, (half + 1) * C // 2)
                 engine_copy(out=h_bf[LAST][:, slots, :], in_=banks[half][:].rearrange("p t s -> p s t"))
 
@@ -261,7 +260,7 @@ def tile_moe_elr_none_kernel(
         def quantize_h(e):
             if e in LATE_H:
                 h_codes[e] = placed([P, C], U32, "hc%d" % e, last_grouped_at + 4 * C * LATE_H.index(e))
-            elif e in (LAST - 2, LAST):
+            elif e == LAST:
                 h_codes[e] = held([P, C], U32, "hc%d" % e)
             else:
                 h_codes[e] = on_load([P, C], U32, "hc%d" % e, e + 2, 3)
@@ -302,12 +301,12 @@ def tile_moe_elr_none_kernel(
                 keep_gate(GATE_BEHIND.index(e))
             quantize_expert(e)
             first_product(e)
-        quantize_h(LAST - 2)
         round_and_quantize_last()
         last_banks = last_first_product()
-        round_h(LATE_H[0], nc.scalar.copy, placed([P, C, PACK], BF16, "hbf6", 0))
+        round_h(LAST - 1, nc.scalar.copy, placed([P, C, PACK], BF16, "hbf6", 0))
         round_last_h(last_banks)
-        quantize_h(LATE_H[0])
+        for e in LATE_H:
+            quantize_h(e)
         quantize_h(LAST)
 
         y = [placed([P, S], F32, "y0", wa_bytes - 64), held([P, S], F32, "y1")]

from contextlib import ExitStack

import concourse.mybir as mybir
from concourse.masks import make_identity

K, T, E, C, H, N = 512, 512, 8, 128, 512, 256
S = E * C
P = 128
PACK = 4
FLOPS = 2 * S * (K * H + K * N + H * N)

F32 = mybir.dt.float32
BF16 = mybir.dt.bfloat16
I32 = mybir.dt.int32
U32 = mybir.dt.uint32
U16 = mybir.dt.uint16
U8 = mybir.dt.uint8
FP8X4 = mybir.dt.float8_e4m3fn_x4
FP4X4 = mybir.dt.float4_e2m1fn_x4
MULT = mybir.AluOpType.mult
ADD = mybir.AluOpType.add
COPY = mybir.ActivationFunctionType.Copy

LAST = E - 1
ALL_EXPERTS = tuple(range(E))
GATHERS = ((0, 1, 2), (3, 4, 5), (6, 7))
VECTOR_PLACES = (0, 56, 84, 84, 84, 84, 84)
LAST_VECTOR_PLACES = (84, 68)
GATE_BEHIND = (2, 4)
LATE_H = (5, 6)
WARM_UP_COLUMNS = (512, 256)

BLOCK0_LOADS = ((0, 1, 2, 3), (4, 5, 6), (7,))
BLOCK1_LOADS = ((5, 6, 7), (2, 3, 4), (1,), (0,))
BLOCK0_GROUPS = ((0, 1, 2, 3), (4, 5), (6,), (LAST,))
BLOCK1_GROUPS = BLOCK1_LOADS

H_BANKS = (5, 6)
LAST_H_BANKS = (4, 7)
WARM_BANK = 7
BLOCK0_BANKS = (0, 1, 2, 3)
BLOCK1_BANKS = (3, 0, 1, 2)

QUARTER = T // 4


def tile_moe_elr_none_kernel(
    tc, x_words, x_scales, w_words, w_scales, wa, wb_words, wb_scales, gate, offs, pos1, pos2, out
):
    nc = tc.nc
    with ExitStack() as ctx:
        keep = ctx.enter_context(tc.tile_pool(name="keep", bufs=1))
        psum = ctx.enter_context(tc.psum_pool(name="psum", bufs=1))

        def held(shape, dtype, name):
            return keep.tile(shape, dtype, name=name, align_bytes=64)

        def numbered_bank(number, parts):
            return psum.tile([P, parts, P], F32, name="bank%d" % number)

        tail = ctx.enter_context(tc.tile_pool(name="tail", bufs=1))
        wa_bytes = 4 * PACK * H
        last_grouped_at = wa_bytes + 4 * S
        h_bytes = 2 * PACK * C

        stream = ctx.enter_context(tc.tile_pool(name="stream", bufs=1))

        def on_load(shape, dtype, name, e, part):
            return stream.tile(shape, dtype, name=name, align_bytes=64, offset=wa_bytes * e + h_bytes * part)

        def placed(shape, dtype, name, offset):
            return tail.tile(shape, dtype, name=name, align_bytes=64, offset=offset)

        def load(tile_view, dram_view):
            nc.sync.dma_start(out=tile_view, in_=dram_view)

        gate_cols = held([P, 2, T // P], F32, "gate_cols")
        offs_t = held([P, S // 16], U16, "offs_t")
        pos_t = [held([P, T // 16], U16, "pos_t%d" % r) for r in range(2)]
        xw = held([P, T], U32, "xw")
        xs = held([P, T], U8, "xs")
        ws = held([P, E * N], U8, "ws")
        wbs = held([P, E // PACK, N], U8, "wbs")
        nc.gpsimd.dma_start(gate_cols[:], gate[:, 0, :].rearrange("r (p a) -> p r a", p=P))
        for scale_tile in (xs, wbs, ws):
            nc.vector.memset(scale_tile[:].bitcast(I32), 0)

        def load_scales(scale_tile, rows):
            for r in range(4):
                load(scale_tile.bitcast(I32)[r:P:32], rows[r].bitcast(I32))

        wa_rows = wa.rearrange("e (p j) i -> e p j i", j=PACK)
        raw = {}

        def load_wa(e):
            if e == LAST:
                raw[e] = placed([P, PACK, H], F32, "raw%d" % e, 0)
            else:
                raw[e] = on_load([P, PACK, H], F32, "raw%d" % e, e, 0)
            load(raw[e][:], wa_rows[e])

        w_view = w_words.rearrange("e s p c -> p (e s) c")
        wb_view = wb_words.rearrange("e s p n d -> p (e s) (n d)")
        w_t, wb_t = {}, {}

        def load_w(b):
            piece = held([P, E, 2 * P], U8, "w%d" % b)
            load(piece[:].bitcast(I32), w_view[:, :, 2 * b * P : 2 * (b + 1) * P].bitcast(I32))
            for e in ALL_EXPERTS:
                w_t[e, b] = piece[:, e, :]

        def load_wb(experts, b):
            piece = held([P, len(experts), 4 * P], U8, "wb%d_%d" % (experts[0], b))
            rows = slice(experts[0], experts[-1] + 1)
            load(piece[:].bitcast(I32), wb_view[:, rows, 4 * b * P : 4 * (b + 1) * P].bitcast(I32))
            for n, e in enumerate(experts):
                wb_t[e, b] = piece[:, n, :]

        ident = held([P, P], F32, "ident")
        make_identity(nc, ident[:])
        for g in range(E // PACK):
            for q in range(4):
                nc.gpsimd.dma_start(
                    out=wbs[:].bitcast(I32)[32 * q : 32 * q + 16, g, :],
                    in_=wb_scales[PACK * g : PACK * (g + 1), 0, 4 * q : 4 * q + 4, :].bitcast(I32),
                )

        load(xw[:].bitcast(I32), x_words[0].rearrange("p t d -> p (t d)").bitcast(I32))
        load(offs_t[:], offs)
        load_wa(0)
        load_scales(xs[:], x_scales[0].rearrange("(q r) t -> r q t", r=4))
        for e in range(1, E):
            load_wa(e)
        load_wb(BLOCK0_LOADS[0], 0)
        load_scales(ws[:].rearrange("p (e n) -> p e n", e=E), w_scales.rearrange("e s (q r) n -> r q (e s) n", r=4))
        load_w(0)
        for experts in BLOCK0_LOADS[1:]:
            load_wb(experts, 0)
        load(pos_t[1][:], pos2)
        load(pos_t[0][:], pos1)
        load_w(1)
        for experts in BLOCK1_LOADS:
            load_wb(experts, 1)

        gate_t, spread = {}, {}
        for r in range(2):
            spread[r] = numbered_bank(r, T // P)
            for a in range(T // P):
                nc.tensor.transpose(spread[r][:, a, :], gate_cols[:, r, a : a + 1].to_broadcast([P, P]), ident[:])

        def keep_gate(r):
            gate_t[r] = on_load([P, T], F32, "gate%d" % r, GATE_BEHIND[r], 1)
            nc.scalar.copy(
                out=gate_t[r][:].rearrange("q (p a) -> q p a", p=P), in_=spread[r][:].rearrange("q a p -> q p a")
            )

        xg_w, xg_s = {}, {}

        def gather_tokens(table, dtype, name, gathered):
            for experts in GATHERS:
                entries = offs_t[:, experts[0] * C // 16 : (experts[-1] + 1) * C // 16]
                piece = held([P, len(experts) * C], dtype, "%s%d" % (name, experts[0]))
                nc.vector.tensor_copy(piece[:], table[:].indirect(entries))
                for n, e in enumerate(experts):
                    gathered[e] = piece[:, n * C : (n + 1) * C]

        wa_codes = [held([P, H], U32, "wac%d" % e) for e in range(LAST)]
        wa_scales = [held([P, H], U8, "was%d" % e) for e in range(LAST)]
        grouped = {}

        def round_tiles(e, tiles, cut):
            columns = raw[e][:].rearrange("p j (m t) -> p j m t", t=PACK)
            shares = [(nc.vector.tensor_copy, slice(0, cut))] if cut else []
            for engine_copy, places in shares + [(nc.scalar.copy, slice(cut, P))]:
                engine_copy(
                    out=grouped[e][:, tiles, places, :].rearrange("p t (m a) j -> p m j a t", a=2),
                    in_=columns[:, :, places, tiles].rearrange("p j (m a) t -> p m j a t", a=2),
                )

        def round_expert(e):
            if e:
                grouped[e] = on_load([P, PACK, P, PACK], BF16, "grp%d" % e, e - 1, 4)
            else:
                grouped[e] = held([P, PACK, P, PACK], BF16, "grp0")
            round_tiles(e, slice(0, PACK), VECTOR_PLACES[e])

        def quantize_expert(e):
            nc.vector.quantize_mx(
                out=wa_codes[e][:].bitcast(FP8X4),
                scales=wa_scales[e][:],
                in_=grouped[e][:].rearrange("p t m j -> p (t m j)"),
            )

        grouped[LAST] = placed([P, PACK, P, PACK], BF16, "grp%d" % LAST, last_grouped_at)
        last_codes = [held([P, P], U32, "lc%d" % t) for t in range(PACK - 1)]
        last_codes.append(placed([P, P], U32, "lc%d" % (PACK - 1), wa_bytes - 4 * P))
        last_scales = [held([P, P], U8, "ls%d" % t) for t in range(PACK)]

        def round_and_quantize_last():
            for first, cut in zip((0, 2), LAST_VECTOR_PLACES):
                round_tiles(LAST, slice(first, first + 2), cut)
            for t in range(PACK):
                nc.vector.quantize_mx(
                    out=last_codes[t][:].bitcast(FP8X4),
                    scales=last_scales[t][:],
                    in_=grouped[LAST][:, t].rearrange("p m j -> p (m j)"),
                )

        def stationary_wa(e, t):
            if e == LAST:
                return last_codes[t][:], last_scales[t][:]
            return wa_codes[e][:, t * P : (t + 1) * P], wa_scales[e][:, t * P : (t + 1) * P]

        h_bank, h_bf, h_codes, h_scales = {}, {}, {}, {}

        def first_product(e):
            h_bank[e] = numbered_bank(H_BANKS[e % 2], PACK)
            for t in range(PACK):
                codes, scales = stationary_wa(e, t)
                nc.tensor.matmul_mx(
                    out=h_bank[e][:, t, :],
                    lhsT=codes.bitcast(FP8X4),
                    lhsT_scale=scales,
                    rhs=xg_w[e].bitcast(FP8X4),
                    rhs_scale=xg_s[e],
                    start=True,
                    stop=True,
                )

        def last_first_product():
            banks = [psum.tile([P, PACK, C // 2], F32, name="bank%d" % number) for number in LAST_H_BANKS]
            for t in range(PACK):
                codes, scales = stationary_wa(LAST, t)
                for half, bank in enumerate(banks):
                    slots = slice(half * C // 2, (half + 1) * C // 2)
                    nc.tensor.matmul_mx(
                        out=bank[:, t, :],
                        lhsT=codes.bitcast(FP8X4),
                        lhsT_scale=scales,
                        rhs=xg_w[LAST][:, slots].bitcast(FP8X4),
                        rhs_scale=xg_s[LAST][:, slots],
                        start=True,
                        stop=True,
                    )
            return banks

        def round_last_h(banks):
            h_bf[LAST] = held([P, C, PACK], BF16, "hbf7")
            for half, engine_copy in enumerate((nc.vector.tensor_copy, nc.scalar.copy)):
                slots = slice(half * C // 2, (half + 1) * C // 2)
                engine_copy(out=h_bf[LAST][:, slots, :], in_=banks[half][:].rearrange("p t s -> p s t"))

        def round_h(e, engine_copy, rounded):
            h_bf[e] = rounded
            engine_copy(out=rounded[:], in_=h_bank[e][:].rearrange("p t s -> p s t"))

        def round_h_behind(e, later):
            round_h(e, nc.scalar.copy, on_load([P, C, PACK], BF16, "hbf%d" % e, later, 0))

        def quantize_h(e):
            if e in LATE_H:
                h_codes[e] = placed([P, C], U32, "hc%d" % e, last_grouped_at + 4 * C * LATE_H.index(e))
            elif e == LAST:
                h_codes[e] = held([P, C], U32, "hc%d" % e)
            else:
                h_codes[e] = on_load([P, C], U32, "hc%d" % e, e + 2, 3)
            h_scales[e] = held([P, C], U8, "hs%d" % e)
            nc.vector.quantize_mx(
                out=h_codes[e][:].bitcast(FP8X4),
                scales=h_scales[e][:],
                in_=h_bf[e][:].rearrange("p s t -> p (s t)"),
            )

        warm = psum.tile([P, H], F32, name="bank%d" % WARM_BANK)

        def warm_up(e, columns):
            nc.tensor.matmul_mx(
                out=warm[:, 0:columns],
                lhsT=h_codes[e][:].bitcast(FP8X4),
                lhsT_scale=h_scales[e][:],
                rhs=wa_codes[e][:, 0:columns].bitcast(FP8X4),
                rhs_scale=wa_scales[e][:, 0:columns],
                start=True,
                stop=True,
            )

        gather_tokens(xw, U32, "xgw", xg_w)
        gather_tokens(xs, U8, "xgs", xg_s)
        round_expert(0)
        quantize_expert(0)
        first_product(0)
        for e in range(1, LAST):
            round_expert(e)
            if e >= 2:
                quantize_h(e - 2)
            if e == LAST - 1:
                for columns in WARM_UP_COLUMNS:
                    warm_up(e - 2, columns)
            round_h_behind(e - 1, e)
            if e in GATE_BEHIND:
                keep_gate(GATE_BEHIND.index(e))
            quantize_expert(e)
            first_product(e)
        round_and_quantize_last()
        last_banks = last_first_product()
        round_h(LAST - 1, nc.scalar.copy, placed([P, C, PACK], BF16, "hbf6", 0))
        round_last_h(last_banks)
        for e in LATE_H:
            quantize_h(e)
        quantize_h(LAST)

        y = [placed([P, S], F32, "y0", wa_bytes - 64), held([P, S], F32, "y1")]

        def frozen(e, b):
            return w_t[e, b].bitcast(FP4X4), ws[:, e * N + b * P : e * N + (b + 1) * P], xg_w[e], xg_s[e]

        def adapter(e, b):
            scales = wbs[4 * (e % PACK) : P, e // PACK, b * P : (b + 1) * P]
            return wb_t[e, b].bitcast(FP8X4), scales, h_codes[e][:], h_scales[e][:]

        def y_passes(bank, experts, b, operands, opens):
            for e in experts:
                words, scales, moving, moving_scales = operands(e, b)
                nc.tensor.matmul_mx(
                    out=bank[:, e - experts[0], :],
                    lhsT=words,
                    lhsT_scale=scales,
                    rhs=moving.bitcast(FP8X4),
                    rhs_scale=moving_scales,
                    start=opens and e == experts[0],
                    stop=not opens and e == experts[-1],
                )

        def empty(engine_copy, bank, experts, b):
            engine_copy(
                out=y[b][:, experts[0] * C : (experts[-1] + 1) * C],
                in_=bank[:].rearrange("p n s -> p (n s)"),
            )

        def banks_of(groups, bank_numbers):
            return [(numbered_bank(number, len(experts)), experts) for experts, number in zip(groups, bank_numbers)]

        (first_bank, first_group), *others = banks_of(BLOCK0_GROUPS, BLOCK0_BANKS)
        y_passes(first_bank, first_group, 0, adapter, opens=True)
        y_passes(first_bank, first_group, 0, frozen, opens=False)
        for bank, experts in others:
            y_passes(bank, experts, 0, frozen, opens=True)
        empty(nc.scalar.copy, first_bank, first_group, 0)
        for (bank, experts), engine_copy in zip(others, (nc.vector.tensor_copy, nc.vector.tensor_copy, nc.scalar.copy)):
            y_passes(bank, experts, 0, adapter, opens=False)
            empty(engine_copy, bank, experts, 0)
        block1_banks = banks_of(BLOCK1_GROUPS, BLOCK1_BANKS)
        for bank, experts in block1_banks:
            y_passes(bank, experts, 1, frozen, opens=True)

        product, plain, res = {}, {}, {}
        for b in range(2):
            for r in range(2):
                product[b, r] = held([P, T], F32, "prod%d_%d" % (b, r))
            plain[b] = held([P, T], F32, "plain%d" % b)
            res[b] = held([P, T], F32, "res%d" % b)

        def tokens(first, last):
            return slice(first * QUARTER, (last + 1) * QUARTER)

        def picked(b, r, first, last):
            return y[b][:].indirect(pos_t[r][:, first * QUARTER // 16 : (last + 1) * QUARTER // 16])

        def gather_times_gate(b, r, first, last):
            part = tokens(first, last)
            nc.vector.tensor_tensor(product[b, r][:, part], picked(b, r, first, last), gate_t[r][:, part], MULT)

        def gather_by_pos1(b, first, last):
            nc.scalar.activation(plain[b][:, tokens(first, last)], picked(b, 0, first, last), COPY)

        def times_gate(b, first, last):
            part = tokens(first, last)
            nc.vector.tensor_tensor(product[b, 0][:, part], plain[b][:, part], gate_t[0][:, part], MULT)

        def add(b, first, last):
            part = tokens(first, last)
            nc.vector.tensor_tensor(res[b][:, part], product[b, 0][:, part], product[b, 1][:, part], ADD)

        def store(b, first, last):
            part = tokens(first, last)
            nc.sync.dma_start(out=out[b * P : (b + 1) * P, part], in_=res[b][:, part])

        gather_by_pos1(0, 0, 2)
        for bank, experts in block1_banks:
            y_passes(bank, experts, 1, adapter, opens=False)
            empty(nc.scalar.copy, bank, experts, 1)
        gather_times_gate(0, 1, 0, 3)
        gather_times_gate(0, 0, 3, 3)
        times_gate(0, 0, 0)
        times_gate(0, 1, 2)
        add(0, 0, 0)
        add(0, 1, 3)
        store(0, 0, 3)
        halves = ((0, 1), (2, 3))
        for first, last in halves:
            gather_by_pos1(1, first, last)
        gather_times_gate(1, 1, 0, 3)
        for first, last in halves:
            times_gate(1, first, last)
        for first, last in halves:
            add(1, first, last)
            store(1, first, last)
